import numpy as np
import ml_dtypes


def mxq(x, axis, fmt="e4m3"):
    dtype, down = {"e4m3": (ml_dtypes.float8_e4m3fn, 7), "e5m2": (ml_dtypes.float8_e5m2, 14)}[fmt]
    v = np.moveaxis(np.asarray(x, np.float32).astype(ml_dtypes.bfloat16).astype(np.float64), axis, -1)
    blocks = v.reshape(v.shape[:-1] + (-1, 32))
    amax = np.abs(blocks).max(-1, keepdims=True)
    byte = np.maximum(np.where(amax > 0, np.frexp(amax)[1] - 1 + 127, 0) - down, 1)
    scale = np.exp2(byte - 127.0)
    codes = (blocks / scale).astype(np.float32).astype(dtype).astype(np.float64)
    return np.moveaxis((codes * scale).reshape(v.shape), -1, axis)


WIDE = False


def mx_kscale(k):
    if not WIDE:
        return np.ones(k)
    levels = np.array([10, -10, 5, -5, 0])
    if k % 512:
        return np.exp2(np.random.permutation(np.resize(levels, k // 32))).repeat(32)
    a = np.empty((k // 512, 16))
    for p in range(k // 512):
        a[p, :8] = np.random.permutation(np.resize(levels, 8))
        for g in range(8):
            far = levels[np.abs(levels - a[p, g]) >= 10]
            a[p, g + 8] = far[np.random.randint(len(far))]
    return np.exp2(a.ravel()).repeat(32)


def f64(x):
    return np.asarray(x).astype(np.float64)


def striped(idx):
    return np.tile(idx.reshape(-1, 16).T, (8, 1)).astype(np.uint16)


def unstriped(offs):
    return offs[:16].T.reshape(-1).astype(np.int64)


E2M1 = np.array([0.0, 0.5, 1.0, 1.5, 2.0, 3.0, 4.0, 6.0, -0.0, -0.5, -1.0, -1.5, -2.0, -3.0, -4.0, -6.0])


def pack_weight(w, fmt):
    k, n = w.shape
    w = f64(np.asarray(w, np.float32).astype(ml_dtypes.bfloat16)).reshape(k // 32, 32, n)
    amax = np.abs(w).max(1)
    if fmt == "e4m3":
        byte = np.frexp(amax)[1] - 1 + 127 - 7
    else:
        mant, ex = np.frexp(amax / 6.0)
        byte = np.where(mant > 0.5, ex, ex - 1) + 127
    byte = np.clip(np.where(amax > 0, byte, 1), 1, 254)
    scaled = (w * np.exp2(127.0 - byte)[:, None, :]).reshape(k, n).astype(np.float32)
    by_word = np.ascontiguousarray(scaled.reshape(k // 512, 128, 4, n).transpose(0, 1, 3, 2))
    if fmt == "e4m3":
        words = by_word.astype(ml_dtypes.float8_e4m3fn).view(np.uint8)
    else:
        c = by_word.astype(ml_dtypes.float4_e2m1fn).view(np.uint8) & 0xF
        words = (c[..., 0::2] | (c[..., 1::2] << 4)).reshape(k // 512, 128, 2 * n)
    return np.ascontiguousarray(words), np.ascontiguousarray(byte.astype(np.uint8).reshape(k // 512, 16, n))


def unpack_weight(words, scales, fmt):
    g, _, n = scales.shape
    words = np.ascontiguousarray(words).reshape(g, 128, n, -1)
    if fmt == "e4m3":
        vals = words.view(ml_dtypes.float8_e4m3fn).astype(np.float64)
    else:
        nib = np.empty((g, 128, n, 4), np.uint8)
        nib[..., 0::2] = words & 0xF
        nib[..., 1::2] = words >> 4
        vals = E2M1[nib]
    vals = vals * np.repeat(np.exp2(scales.astype(np.float64) - 127.0), 8, axis=1)[..., None]
    return vals.transpose(0, 1, 3, 2).reshape(g * 512, n)


def gelu(v):
    return 0.5 * v * (1.0 + np.tanh(np.sqrt(2.0 / np.pi) * (v + 0.044715 * v**3)))


K, T, S, H, T2, S2, N = 1024, 4096, 1024, 512, 2048, 512, 512

def setup_inputs():
    n = np.random.standard_normal
    s = mx_kscale(K)[:, None]
    u = mx_kscale(H)[:, None]
    w = mx_kscale(S2)[:, None]
    tab_words, tab_scales = pack_weight(n((K, T)) * s, "e4m3")
    tab2_words, tab2_scales = pack_weight(0.7 * n((H, T2)) / np.sqrt(H) / u, "e4m3")
    wq_words, wq_scales = pack_weight(n((K, H)) / np.sqrt(K) * u.T / s, "e2m1")
    ex_words, ex_scales = pack_weight(np.exp(0.8 * n((S2, N))) / S2 / w, "e4m3")
    return {
        "tab_words": tab_words, "tab_scales": tab_scales,
        "tab2_words": tab2_words, "tab2_scales": tab2_scales,
        "wq_words": wq_words, "wq_scales": wq_scales,
        "ex_words": ex_words, "ex_scales": ex_scales,
        "bq": (0.7 * n(H) * u[:, 0]).astype(np.float32),
        "seg": (np.exp(0.5 * n(S2)) * w[:, 0]).astype(np.float32),
        "ev": (np.exp(1.2 * n((S2, N))) / S2 / w).astype(np.float32),
        "offs": striped(np.random.permutation(T)[:S]),
        "offs2": striped(np.random.permutation(T2)[:S2]),
    }

def reference(tab_words, tab_scales, tab2_words, tab2_scales, wq_words, wq_scales,
              ex_words, ex_scales, bq, seg, ev, offs, offs2):
    v = unpack_weight(tab_words, tab_scales, "e4m3")[:, unstriped(offs)]
    v2 = unpack_weight(tab2_words, tab2_scales, "e4m3")[:, unstriped(offs2)]
    wq = unpack_weight(wq_words, wq_scales, "e2m1")
    ex = unpack_weight(ex_words, ex_scales, "e4m3")
    h = (wq.T @ v) + f64(bq)[:, None]
    h = mxq(h, 0, "e4m3")
    e = v2.T @ h
    act = np.exp(e) * f64(seg)[:, None]
    act = mxq(act, 0, "e4m3")
    num = mxq(f64(ev), 0, "e4m3").T @ act
    den = ex.T @ act
    return num / den

@@ -1,0 +1,268 @@
+from contextlib import ExitStack
+
+import concourse.mybir as mybir
+
+K, T, S, H, T2, S2, N = 1024, 4096, 1024, 512, 2048, 512, 512
+FLOPS = 2 * (K * H * S + H * S2 * S + 2 * S2 * N * S)
+
+F32 = mybir.dt.float32
+BF16 = mybir.dt.bfloat16
+I32 = mybir.dt.int32
+U32 = mybir.dt.uint32
+U16 = mybir.dt.uint16
+U8 = mybir.dt.uint8
+FP8X4 = mybir.dt.float8_e4m3fn_x4
+FP4X4 = mybir.dt.float4_e2m1fn_x4
+ACT = mybir.ActivationFunctionType
+ALU = mybir.AluOpType
+
+P = 128
+PACK = 4
+QUADS = 4
+JA = 128
+JB = 256
+JC = 512
+
+
+def tile_list_memory_decoder_evidence_kernel(
+    tc, tab_words, tab_scales, tab2_words, tab2_scales, wq_words, wq_scales,
+    ex_words, ex_scales, bq, seg, ev, offs, offs2, out,
+):
+    nc = tc.nc
+    with ExitStack() as ctx:
+        keep = ctx.enter_context(tc.tile_pool(name="keep", bufs=1))
+        ring = ctx.enter_context(tc.tile_pool(name="ring", bufs=4))
+        psum = ctx.enter_context(tc.psum_pool(name="psum", bufs=1))
+
+        def sb(name, shape, dtype, tag=None):
+            return keep.tile(shape, dtype, name=name, tag=tag or name, align_bytes=64)
+
+        def bank(b, shape):
+            return psum.tile(shape, F32, name="bank%d" % b)
+
+        idx = keep.tile([P, S // 16], U16, name="idx")
+        idx2 = keep.tile([P, S2 // 16], U16, name="idx2")
+        tab_sc = sb("tab_sc", [P, T], U8)
+        tab2_sc = sb("tab2_sc", [P, T2], U8)
+        wq_sc_raw = sb("wq_sc_raw", [P, 2, H], U8, tag="tab_w1")
+        v_sc = sb("v_sc", [P, 2 * S], U8)
+        nc.vector.memset(tab_sc[:].bitcast(I32), 0)
+        nc.gpsimd.memset(tab2_sc[:].bitcast(I32), 0)
+        nc.vector.memset(wq_sc_raw[:].bitcast(I32), 0)
+        nc.vector.memset(v_sc[:].bitcast(I32), 0)
+
+        tab2_w = sb("tab2_w", [P, T2], I32)
+        wq_raw = sb("wq_raw", [P, 2, H // 2], I32, tag="tab_w0")
+        seg_sb = sb("seg_sb", [P, PACK], F32)
+        bq_sb = sb("bq_sb", [P, PACK], F32)
+
+        nc.sync.dma_start(idx[:], offs)
+        nc.sync.dma_start(wq_raw[:], wq_words.rearrange("a p c -> p a c").bitcast(I32))
+        nc.sync.dma_start(idx2[:], offs2)
+        nc.sync.dma_start(tab2_w[:], tab2_words[0].rearrange("p t i -> p (t i)").bitcast(I32))
+        nc.scalar.dma_start(seg_sb[:], seg.rearrange("(p t) -> p t", t=PACK))
+        nc.scalar.dma_start(bq_sb[:], bq.rearrange("(p t) -> p t", t=PACK))
+        nc.scalar.dma_start(
+            tab_sc[0:P:4, :].bitcast(I32), tab_scales.rearrange("a q t -> q a t").bitcast(I32)
+        )
+        for q in range(QUADS):
+            nc.gpsimd.dma_start(
+                tab2_sc[32 * q : 32 * q + 4, :].bitcast(I32),
+                tab2_scales[0, 4 * q : 4 * q + 4, :].bitcast(I32),
+            )
+        for q in range(QUADS):
+            nc.scalar.dma_start(
+                wq_sc_raw[32 * q : 32 * q + 4, :, :].bitcast(I32),
+                wq_scales[:, 4 * q : 4 * q + 4, :].rearrange("a r c -> r a c").bitcast(I32),
+            )
+
+
+        wq_w = sb("wq_w", [P, 2 * H // 2], I32)
+        nc.vector.tensor_copy(
+            wq_w[:].bitcast(U16).rearrange("p (a t m) -> p a t m", a=2, t=PACK),
+            wq_raw[:].bitcast(U16).rearrange("p a (m t) -> p a t m", t=PACK),
+        )
+        tab_w0 = sb("tab_w0", [P, T], I32)
+        nc.sync.dma_start(tab_w0[:], tab_words[0].rearrange("p t i -> p (t i)").bitcast(I32))
+        wq_sc = sb("wq_sc", [P, 2 * H], U8)
+        nc.vector.tensor_copy(
+            wq_sc[:].rearrange("p (a t m) -> p a t m", a=2, t=PACK),
+            wq_sc_raw[:].rearrange("p a (m t) -> p a t m", t=PACK),
+        )
+        tab_w1 = sb("tab_w1", [P, T], I32)
+        nc.sync.dma_start(tab_w1[:], tab_words[1].rearrange("p t i -> p (t i)").bitcast(I32))
+        v_sc_g = sb("v_sc_g", [P, S], U8)
+        nc.vector.tensor_copy(v_sc_g[:], tab_sc[:].indirect(idx[:]))
+        for q in range(QUADS):
+            nc.scalar.dma_start(
+                v_sc[32 * q : 32 * q + 4, :].bitcast(I32), v_sc_g[32 * q : 32 * q + 32 : 4, :].bitcast(I32)
+            )
+        ln_seg = sb("ln_seg", [P, PACK], F32, tag="v_sc_g")
+        nc.scalar.activation(ln_seg[:], seg_sb[:], ACT.Ln)
+        warm = sb("warm", [P, 1], F32)
+        nc.scalar.activation(warm[:], ln_seg[:, 0:1], ACT.Exp)
+        v2_g = sb("v2_g", [P, S2], I32, tag="tab_sc")
+        nc.vector.tensor_copy(v2_g[:].bitcast(U32), tab2_w[:].bitcast(U32).indirect(idx2[:]))
+        v2_w = sb("v2_w", [P, S2], I32)
+        nc.vector.tensor_copy(
+            v2_w[:].rearrange("p (t m) -> p t m", t=PACK), v2_g[:].rearrange("p (m t) -> p t m", t=PACK)
+        )
+        v2_sc_g = sb("v2_sc_g", [P, S2], U8, tag="tab_sc")
+        nc.vector.tensor_copy(v2_sc_g[:], tab2_sc[:].indirect(idx2[:]))
+        ex_sc = sb("ex_sc", [P, N], U8, tag="tab2_sc")
+        nc.gpsimd.memset(ex_sc[:].bitcast(I32), 0)
+        for q in range(QUADS):
+            nc.scalar.dma_start(
+                ex_sc[32 * q : 32 * q + 4, :].bitcast(I32),
+                ex_scales[0, 4 * q : 4 * q + 4, :].bitcast(I32),
+            )
+        v2_sc = sb("v2_sc", [P, S2], U8)
+        nc.vector.tensor_copy(
+            v2_sc[:].rearrange("p (t m) -> p t m", t=PACK), v2_sc_g[:].rearrange("p (m t) -> p t m", t=PACK)
+        )
+        ev_sb = sb("ev_sb", [P, PACK, N], F32, tag="tab_sc")
+        nc.sync.dma_start(ev_sb[:], ev.rearrange("(p t) n -> p t n", t=PACK))
+        v_w0 = sb("v_w0", [P, S], I32)
+        nc.vector.tensor_copy(v_w0[:].bitcast(U32), tab_w0[:].bitcast(U32).indirect(idx[:]))
+        ex_w = sb("ex_w", [P, N], I32, tag="tab_w0")
+        nc.sync.dma_start(ex_w[:], ex_words[0].rearrange("p c i -> p (c i)").bitcast(I32))
+
+        def h_pass(acc, a, t, rhs, rhs_scale):
+            col = a * H + t * P
+            nc.tensor.matmul_mx(
+                out=acc[:, t, :],
+                lhsT=wq_w[:].bitcast(U8)[:, 2 * col : 2 * (col + P)].bitcast(FP4X4),
+                lhsT_scale=wq_sc[:, col : col + P],
+                rhs=rhs.bitcast(FP8X4),
+                rhs_scale=rhs_scale,
+                start=(a == 0 and t == 0),
+                stop=(a == 1 and t == PACK - 1),
+            )
+
+        h_acc = [bank(c, [P, PACK, JA]) for c in range(S // JA)]
+        for c in range(S // JA):
+            cols = slice(c * JA, (c + 1) * JA)
+            for t in range(PACK):
+                h_pass(h_acc[c], 0, t, v_w0[:, cols], v_sc[:, cols])
+
+        v_w1 = [sb("v_w1_%d" % hf, [P, JC], I32) for hf in range(S // JC)]
+        h_bf = [sb("h_bf%d" % q, [P, JB * PACK], BF16) for q in range(S // JB)]
+        h_w = [sb("h_w%d" % q, [P, JB], I32) for q in range(S // JB)]
+        h_sc = [sb("h_sc%d" % q, [P, JB], U8) for q in range(S // JB)]
+        planes = [sb("planes%d" % q, [P, PACK, JB], BF16) for q in range(S // JB)]
+        act_bf = [sb("act_bf%d" % q, [P, JB * PACK], BF16) for q in range(S // JB)]
+        act_w = sb("act_w", [P, S], I32)
+        act_sc = sb("act_sc", [P, S], U8)
+
+        def gather_last_pass(hf):
+            nc.vector.tensor_copy(
+                v_w1[hf][:].bitcast(U32),
+                tab_w1[:].bitcast(U32).indirect(idx[:, hf * JC // 16 : (hf + 1) * JC // 16]),
+            )
+
+        def finish_h(c):
+            hf, c0 = divmod(c * JA, JC)
+            for t in range(PACK):
+                h_pass(h_acc[c], 1, t, v_w1[hf][:, c0 : c0 + JA], v_sc[:, S + c * JA : S + (c + 1) * JA])
+            q, j0 = divmod(c * JA, JB)
+            nc.vector.tensor_tensor(
+                h_bf[q][:, PACK * j0 : PACK * (j0 + JA)].rearrange("p (j t) -> p j t", t=PACK),
+                h_acc[c][:].rearrange("p t j -> p j t"),
+                bq_sb[:].unsqueeze(1).to_broadcast([P, JA, PACK]),
+                ALU.add,
+            )
+
+        def scores(q):
+            nc.vector.quantize_mx(out=h_w[q][:].bitcast(FP8X4), scales=h_sc[q][:], in_=h_bf[q][:])
+            for u in range(2):
+                e_acc = bank(2 * q + u, [P, 2, JB])
+                for s in range(2):
+                    t = 2 * u + s
+                    nc.tensor.matmul_mx(
+                        out=e_acc[:, s, :],
+                        lhsT=v2_w[:, t * P : (t + 1) * P].bitcast(FP8X4),
+                        lhsT_scale=v2_sc[:, t * P : (t + 1) * P],
+                        rhs=h_w[q][:].bitcast(FP8X4),
+                        rhs_scale=h_sc[q][:],
+                        start=True,
+                        stop=True,
+                    )
+                for s in range(2):
+                    t = 2 * u + s
+                    nc.scalar.activation(
+                        planes[q][:, t, :], e_acc[:, s, :], ACT.Exp, bias=ln_seg[:, t : t + 1]
+                    )
+
+        def interleave_act(q):
+            nc.vector.tensor_copy(
+                act_bf[q][:].rearrange("p (j t) -> p j t", t=PACK), planes[q][:].rearrange("p t j -> p j t")
+            )
+
+        def quantize_act(q):
+            cols = slice(q * JB, (q + 1) * JB)
+            nc.vector.quantize_mx(out=act_w[:, cols].bitcast(FP8X4), scales=act_sc[:, cols], in_=act_bf[q][:])
+
+        ev_bf = sb("ev_bf", [P, N * PACK], BF16)
+        ev_w = sb("ev_w", [P, N], I32)
+        ev_sc = sb("ev_sc", [P, N], U8)
+
+        def mix(acc, words, scales, nt, hf):
+            nc.tensor.matmul_mx(
+                out=acc[:],
+                lhsT=words[:, nt * P : (nt + 1) * P].bitcast(FP8X4),
+                lhsT_scale=scales[:, nt * P : (nt + 1) * P],
+                rhs=act_w[:, hf * JC : (hf + 1) * JC].bitcast(FP8X4),
+                rhs_scale=act_sc[:, hf * JC : (hf + 1) * JC],
+                start=True,
+                stop=True,
+            )
+
+        def divide(hf):
+            dens = []
+            for nt in range(N // P):
+                den = bank(4 * hf + nt, [P, JC])
+                mix(den, ex_w, ex_sc, nt, hf)
+                dens.append(den)
+            for nt in range(N // P):
+                root = ring.tile([P, JC], F32, name="root")
+                nc.scalar.activation(root[:], dens[nt][:], ACT.Abs_reciprocal_sqrt)
+                num = bank(4 * hf + nt, [P, JC])
+                mix(num, ev_w, ev_sc, nt, hf)
+                part = ring.tile([P, JC], F32, name="part")
+                res = ring.tile([P, JC], F32, name="res")
+                if nt % 2 == 0:
+                    nc.vector.tensor_tensor(part[:], num[:], root[:], ALU.mult)
+                    nc.vector.tensor_tensor(res[:], part[:], root[:], ALU.mult)
+                else:
+                    nc.scalar.activation(part[:], root[:], ACT.Square)
+                    nc.vector.tensor_tensor(res[:], num[:], part[:], ALU.mult)
+                nc.sync.dma_start(out[nt * P : (nt + 1) * P, hf * JC : (hf + 1) * JC], res[:])
+
+        gather_last_pass(0)
+        finish_h(0)
+        finish_h(1)
+        finish_h(2)
+        scores(0)
+        finish_h(3)
+        gather_last_pass(1)
+        scores(1)
+        nc.scalar.copy(
+            ev_bf[:].rearrange("p (n t) -> p n t", t=PACK), ev_sb[:].rearrange("p t n -> p n t")
+        )
+        finish_h(4)
+        finish_h(5)
+        finish_h(6)
+        scores(2)
+        finish_h(7)
+        interleave_act(0)
+        scores(3)
+        interleave_act(1)
+        quantize_act(0)
+        quantize_act(1)
+        interleave_act(2)
+        nc.vector.quantize_mx(out=ev_w[:].bitcast(FP8X4), scales=ev_sc[:], in_=ev_bf[:])
+        quantize_act(2)
+        interleave_act(3)
+        quantize_act(3)
+        divide(0)
+        divide(1)

@@ -22,6 +22,7 @@ QUADS = 4
 JA = 128
 JB = 256
 JC = 512
+SCALAR_QS = 2
 
 
 def tile_list_memory_decoder_evidence_kernel(
@@ -44,22 +45,22 @@ def tile_list_memory_decoder_evidence_kernel(
         idx2 = keep.tile([P, S2 // 16], U16, name="idx2")
         tab_sc = sb("tab_sc", [P, T], U8)
         tab2_sc = sb("tab2_sc", [P, T2], U8)
-        wq_sc_raw = sb("wq_sc_raw", [P, 2, H], U8, tag="tab_w1")
+        wq_sc_raw = sb("wq_sc_raw", [P, 2, H], U8, tag="tab2_w")
         v_sc = sb("v_sc", [P, 2 * S], U8)
         nc.vector.memset(tab_sc[:].bitcast(I32), 0)
         nc.gpsimd.memset(tab2_sc[:].bitcast(I32), 0)
         nc.vector.memset(wq_sc_raw[:].bitcast(I32), 0)
         nc.vector.memset(v_sc[:].bitcast(I32), 0)
 
-        tab2_w = sb("tab2_w", [P, T2], I32)
-        wq_raw = sb("wq_raw", [P, 2, H // 2], I32, tag="tab_w0")
+        wq_raw = sb("wq_raw", [P, 2, H // 2], I32, tag="tab_w1")
+        tab_w0 = sb("tab_w0", [P, T], I32)
         seg_sb = sb("seg_sb", [P, PACK], F32)
         bq_sb = sb("bq_sb", [P, PACK], F32)
 
         nc.sync.dma_start(idx[:], offs)
-        nc.sync.dma_start(wq_raw[:], wq_words.rearrange("a p c -> p a c").bitcast(I32))
         nc.sync.dma_start(idx2[:], offs2)
-        nc.sync.dma_start(tab2_w[:], tab2_words[0].rearrange("p t i -> p (t i)").bitcast(I32))
+        nc.sync.dma_start(tab_w0[:], tab_words[0].rearrange("p t i -> p (t i)").bitcast(I32))
+        nc.scalar.dma_start(wq_raw[:], wq_words.rearrange("a p c -> p a c").bitcast(I32))
         nc.scalar.dma_start(seg_sb[:], seg.rearrange("(p t) -> p t", t=PACK))
         nc.scalar.dma_start(bq_sb[:], bq.rearrange("(p t) -> p t", t=PACK))
         nc.scalar.dma_start(
@@ -76,18 +77,10 @@ def tile_list_memory_decoder_evidence_kernel(
                 wq_scales[:, 4 * q : 4 * q + 4, :].rearrange("a r c -> r a c").bitcast(I32),
             )
 
-
         wq_w = sb("wq_w", [P, 2 * H // 2], I32)
         nc.vector.tensor_copy(
-            wq_w[:].bitcast(U16).rearrange("p (a t m) -> p a t m", a=2, t=PACK),
-            wq_raw[:].bitcast(U16).rearrange("p a (m t) -> p a t m", t=PACK),
-        )
-        tab_w0 = sb("tab_w0", [P, T], I32)
-        nc.sync.dma_start(tab_w0[:], tab_words[0].rearrange("p t i -> p (t i)").bitcast(I32))
-        wq_sc = sb("wq_sc", [P, 2 * H], U8)
-        nc.vector.tensor_copy(
-            wq_sc[:].rearrange("p (a t m) -> p a t m", a=2, t=PACK),
-            wq_sc_raw[:].rearrange("p a (m t) -> p a t m", t=PACK),
+            wq_w[:].bitcast(U16).rearrange("p (a t m) -> p a m t", a=2, t=PACK),
+            wq_raw[:].bitcast(U16).rearrange("p a (m t) -> p a m t", t=PACK),
         )
         tab_w1 = sb("tab_w1", [P, T], I32)
         nc.sync.dma_start(tab_w1[:], tab_words[1].rearrange("p t i -> p (t i)").bitcast(I32))
@@ -97,17 +90,20 @@ def tile_list_memory_decoder_evidence_kernel(
             nc.scalar.dma_start(
                 v_sc[32 * q : 32 * q + 4, :].bitcast(I32), v_sc_g[32 * q : 32 * q + 32 : 4, :].bitcast(I32)
             )
-        ln_seg = sb("ln_seg", [P, PACK], F32, tag="v_sc_g")
+        ln_seg = sb("ln_seg", [P, PACK], F32, tag="tab_sc")
         nc.scalar.activation(ln_seg[:], seg_sb[:], ACT.Ln)
         warm = sb("warm", [P, 1], F32)
         nc.scalar.activation(warm[:], ln_seg[:, 0:1], ACT.Exp)
-        v2_g = sb("v2_g", [P, S2], I32, tag="tab_sc")
-        nc.vector.tensor_copy(v2_g[:].bitcast(U32), tab2_w[:].bitcast(U32).indirect(idx2[:]))
-        v2_w = sb("v2_w", [P, S2], I32)
+        wq_sc = sb("wq_sc", [P, 2 * H], U8)
         nc.vector.tensor_copy(
-            v2_w[:].rearrange("p (t m) -> p t m", t=PACK), v2_g[:].rearrange("p (m t) -> p t m", t=PACK)
+            wq_sc[:].rearrange("p (a t m) -> p a m t", a=2, t=PACK),
+            wq_sc_raw[:].rearrange("p a (m t) -> p a m t", t=PACK),
         )
-        v2_sc_g = sb("v2_sc_g", [P, S2], U8, tag="tab_sc")
+        tab2_w = sb("tab2_w", [P, T2], I32)
+        nc.sync.dma_start(tab2_w[:], tab2_words[0].rearrange("p t i -> p (t i)").bitcast(I32))
+        v_w0 = sb("v_w0", [P, S], I32)
+        nc.vector.tensor_copy(v_w0[:].bitcast(U32), tab_w0[:].bitcast(U32).indirect(idx[:]))
+        v2_sc_g = sb("v2_sc_g", [P, S2], U8, tag="tab_w0")
         nc.vector.tensor_copy(v2_sc_g[:], tab2_sc[:].indirect(idx2[:]))
         ex_sc = sb("ex_sc", [P, N], U8, tag="tab2_sc")
         nc.gpsimd.memset(ex_sc[:].bitcast(I32), 0)
@@ -118,32 +114,37 @@ def tile_list_memory_decoder_evidence_kernel(
             )
         v2_sc = sb("v2_sc", [P, S2], U8)
         nc.vector.tensor_copy(
-            v2_sc[:].rearrange("p (t m) -> p t m", t=PACK), v2_sc_g[:].rearrange("p (m t) -> p t m", t=PACK)
+            v2_sc[:].rearrange("p (t m) -> p m t", t=PACK), v2_sc_g[:].rearrange("p (m t) -> p m t", t=PACK)
         )
-        ev_sb = sb("ev_sb", [P, PACK, N], F32, tag="tab_sc")
+        ev_sb = sb("ev_sb", [P, PACK, N], F32, tag="v_sc_g")
         nc.sync.dma_start(ev_sb[:], ev.rearrange("(p t) n -> p t n", t=PACK))
-        v_w0 = sb("v_w0", [P, S], I32)
-        nc.vector.tensor_copy(v_w0[:].bitcast(U32), tab_w0[:].bitcast(U32).indirect(idx[:]))
         ex_w = sb("ex_w", [P, N], I32, tag="tab_w0")
         nc.sync.dma_start(ex_w[:], ex_words[0].rearrange("p c i -> p (c i)").bitcast(I32))
 
-        def h_pass(acc, a, t, rhs, rhs_scale):
-            col = a * H + t * P
-            nc.tensor.matmul_mx(
-                out=acc[:, t, :],
-                lhsT=wq_w[:].bitcast(U8)[:, 2 * col : 2 * (col + P)].bitcast(FP4X4),
-                lhsT_scale=wq_sc[:, col : col + P],
-                rhs=rhs.bitcast(FP8X4),
-                rhs_scale=rhs_scale,
-                start=(a == 0 and t == 0),
-                stop=(a == 1 and t == PACK - 1),
-            )
+        h_acc = [bank(b, [P, 2, JB] if b < 2 * SCALAR_QS else [P, PACK, JA]) for b in range(S // JA)]
 
-        h_acc = [bank(c, [P, PACK, JA]) for c in range(S // JA)]
-        for c in range(S // JA):
-            cols = slice(c * JA, (c + 1) * JA)
-            for t in range(PACK):
-                h_pass(h_acc[c], 0, t, v_w0[:, cols], v_sc[:, cols])
+        def h_bank(b, a, words, col0):
+            for k in range(PACK):
+                if b < 2 * SCALAR_QS:
+                    s, g = divmod(k, 2)
+                    t, j0 = 2 * (b % 2) + s, (b // 2) * JB + g * JA
+                    dst = h_acc[b][:, s, g * JA : (g + 1) * JA]
+                else:
+                    t, j0 = k, b * JA
+                    dst = h_acc[b][:, k, :]
+                col = a * H + t * P
+                nc.tensor.matmul_mx(
+                    out=dst,
+                    lhsT=wq_w[:].bitcast(U8)[:, 2 * col : 2 * (col + P)].bitcast(FP4X4),
+                    lhsT_scale=wq_sc[:, col : col + P],
+                    rhs=words[:, j0 - col0 : j0 - col0 + JA].bitcast(FP8X4),
+                    rhs_scale=v_sc[:, a * S + j0 : a * S + j0 + JA],
+                    start=(a == 0 and k == 0),
+                    stop=(a == 1 and k == PACK - 1),
+                )
+
+        for b in range(S // JA):
+            h_bank(b, 0, v_w0, 0)
 
         v_w1 = [sb("v_w1_%d" % hf, [P, JC], I32) for hf in range(S // JC)]
         h_bf = [sb("h_bf%d" % q, [P, JB * PACK], BF16) for q in range(S // JB)]
@@ -160,17 +161,33 @@ def tile_list_memory_decoder_evidence_kernel(
                 tab_w1[:].bitcast(U32).indirect(idx[:, hf * JC // 16 : (hf + 1) * JC // 16]),
             )
 
-        def finish_h(c):
-            hf, c0 = divmod(c * JA, JC)
-            for t in range(PACK):
-                h_pass(h_acc[c], 1, t, v_w1[hf][:, c0 : c0 + JA], v_sc[:, S + c * JA : S + (c + 1) * JA])
-            q, j0 = divmod(c * JA, JB)
-            nc.vector.tensor_tensor(
-                h_bf[q][:, PACK * j0 : PACK * (j0 + JA)].rearrange("p (j t) -> p j t", t=PACK),
-                h_acc[c][:].rearrange("p t j -> p j t"),
-                bq_sb[:].unsqueeze(1).to_broadcast([P, JA, PACK]),
-                ALU.add,
+        def interleave(engine_copy, dst, src):
+            engine_copy(
+                dst.rearrange("p (c i t) -> p c t i", i=4, t=PACK), src.rearrange("p t (c i) -> p c t i", i=4)
             )
+
+        h_planes = [sb("h_planes%d" % q, [P, PACK, JB], BF16) for q in range(SCALAR_QS)]
+
+        def finish_h(b):
+            hf = b * JA // JC
+            h_bank(b, 1, v_w1[hf], hf * JC)
+            q, u = divmod(b, 2)
+            if q < SCALAR_QS:
+                for s in range(2):
+                    t = 2 * u + s
+                    nc.scalar.activation(
+                        h_planes[q][:, t, :], h_acc[b][:, s, :], ACT.Identity, bias=bq_sb[:, t : t + 1]
+                    )
+            else:
+                nc.vector.tensor_tensor(
+                    h_bf[q][:, PACK * u * JA : PACK * (u + 1) * JA].rearrange("p (j t) -> p j t", t=PACK),
+                    h_acc[b][:].rearrange("p t j -> p j t"),
+                    bq_sb[:].unsqueeze(1).to_broadcast([P, JA, PACK]),
+                    ALU.add,
+                )
+
+        def interleave_h(q):
+            interleave(nc.vector.tensor_copy, h_bf[q][:], h_planes[q][:])
 
         def scores(q):
             nc.vector.quantize_mx(out=h_w[q][:].bitcast(FP8X4), scales=h_sc[q][:], in_=h_bf[q][:])
@@ -194,9 +211,7 @@ def tile_list_memory_decoder_evidence_kernel(
                     )
 
         def interleave_act(q):
-            nc.vector.tensor_copy(
-                act_bf[q][:].rearrange("p (j t) -> p j t", t=PACK), planes[q][:].rearrange("p t j -> p j t")
-            )
+            interleave(nc.vector.tensor_copy, act_bf[q][:], planes[q][:])
 
         def quantize_act(q):
             cols = slice(q * JB, (q + 1) * JB)
@@ -226,7 +241,7 @@ def tile_list_memory_decoder_evidence_kernel(
             for nt in range(N // P):
                 root = ring.tile([P, JC], F32, name="root")
                 nc.scalar.activation(root[:], dens[nt][:], ACT.Abs_reciprocal_sqrt)
-                num = bank(4 * hf + nt, [P, JC])
+                num = bank(nt, [P, JC])
                 mix(num, ev_w, ev_sc, nt, hf)
                 part = ring.tile([P, JC], F32, name="part")
                 res = ring.tile([P, JC], F32, name="res")
@@ -239,23 +254,32 @@ def tile_list_memory_decoder_evidence_kernel(
                 nc.sync.dma_start(out[nt * P : (nt + 1) * P, hf * JC : (hf + 1) * JC], res[:])
 
         gather_last_pass(0)
-        finish_h(0)
-        finish_h(1)
-        finish_h(2)
-        scores(0)
-        finish_h(3)
+        for b in range(4):
+            finish_h(b)
         gather_last_pass(1)
-        scores(1)
-        nc.scalar.copy(
-            ev_bf[:].rearrange("p (n t) -> p n t", t=PACK), ev_sb[:].rearrange("p t n -> p n t")
+        v2_g = sb("v2_g", [P, S2], I32)
+        nc.vector.tensor_copy(v2_g[:].bitcast(U32), tab2_w[:].bitcast(U32).indirect(idx2[:]))
+        interleave_h(0)
+        v2_w = sb("v2_w", [P, S2], I32)
+        nc.vector.tensor_copy(
+            v2_w[:].rearrange("p (t m) -> p m t", t=PACK), v2_g[:].rearrange("p (m t) -> p m t", t=PACK)
         )
+        scores(0)
+        interleave_h(1)
         finish_h(4)
+        scores(1)
         finish_h(5)
         finish_h(6)
         scores(2)
         finish_h(7)
         interleave_act(0)
         scores(3)
+        for u in range(2):
+            interleave(
+                nc.scalar.copy,
+                ev_bf[:, u * PACK * JB : (u + 1) * PACK * JB],
+                ev_sb[:, :, u * JB : (u + 1) * JB],
+            )
         interleave_act(1)
         quantize_act(0)
         quantize_act(1)

@@ -22,7 +22,7 @@ QUADS = 4
 JA = 128
 JB = 256
 JC = 512
-SCALAR_QS = 2
+SCALAR_Q = 1
 
 
 def tile_list_memory_decoder_evidence_kernel(
@@ -45,24 +45,26 @@ def tile_list_memory_decoder_evidence_kernel(
         idx2 = keep.tile([P, S2 // 16], U16, name="idx2")
         tab_sc = sb("tab_sc", [P, T], U8)
         tab2_sc = sb("tab2_sc", [P, T2], U8)
-        wq_sc_raw = sb("wq_sc_raw", [P, 2, H], U8, tag="tab2_w")
+        wq_sc_raw = sb("wq_sc_raw", [P, 2, H], U8)
+        ex_sc = sb("ex_sc", [P, N], U8)
         v_sc = sb("v_sc", [P, 2 * S], U8)
         nc.vector.memset(tab_sc[:].bitcast(I32), 0)
         nc.gpsimd.memset(tab2_sc[:].bitcast(I32), 0)
         nc.vector.memset(wq_sc_raw[:].bitcast(I32), 0)
+        nc.vector.memset(ex_sc[:].bitcast(I32), 0)
         nc.vector.memset(v_sc[:].bitcast(I32), 0)
 
-        wq_raw = sb("wq_raw", [P, 2, H // 2], I32, tag="tab_w1")
-        tab_w0 = sb("tab_w0", [P, T], I32)
+        wq_raw = sb("wq_raw", [P, 2, H // 2], I32, tag="tab_w0")
+        tab2_w = sb("tab2_w", [P, T2], I32, tag="tab_w1")
         seg_sb = sb("seg_sb", [P, PACK], F32)
         bq_sb = sb("bq_sb", [P, PACK], F32)
 
+        nc.sync.dma_start(wq_raw[:], wq_words.rearrange("a p c -> p a c").bitcast(I32))
         nc.sync.dma_start(idx[:], offs)
-        nc.sync.dma_start(idx2[:], offs2)
-        nc.sync.dma_start(tab_w0[:], tab_words[0].rearrange("p t i -> p (t i)").bitcast(I32))
-        nc.scalar.dma_start(wq_raw[:], wq_words.rearrange("a p c -> p a c").bitcast(I32))
         nc.scalar.dma_start(seg_sb[:], seg.rearrange("(p t) -> p t", t=PACK))
         nc.scalar.dma_start(bq_sb[:], bq.rearrange("(p t) -> p t", t=PACK))
+        nc.sync.dma_start(tab2_w[:], tab2_words[0].rearrange("p t i -> p (t i)").bitcast(I32))
+        nc.sync.dma_start(idx2[:], offs2)
         nc.scalar.dma_start(
             tab_sc[0:P:4, :].bitcast(I32), tab_scales.rearrange("a q t -> q a t").bitcast(I32)
         )
@@ -76,56 +78,68 @@ def tile_list_memory_decoder_evidence_kernel(
                 wq_sc_raw[32 * q : 32 * q + 4, :, :].bitcast(I32),
                 wq_scales[:, 4 * q : 4 * q + 4, :].rearrange("a r c -> r a c").bitcast(I32),
             )
+        for q in range(QUADS):
+            nc.gpsimd.dma_start(
+                ex_sc[32 * q : 32 * q + 4, :].bitcast(I32),
+                ex_scales[0, 4 * q : 4 * q + 4, :].bitcast(I32),
+            )
 
         wq_w = sb("wq_w", [P, 2 * H // 2], I32)
         nc.vector.tensor_copy(
             wq_w[:].bitcast(U16).rearrange("p (a t m) -> p a m t", a=2, t=PACK),
             wq_raw[:].bitcast(U16).rearrange("p a (m t) -> p a m t", t=PACK),
         )
-        tab_w1 = sb("tab_w1", [P, T], I32)
-        nc.sync.dma_start(tab_w1[:], tab_words[1].rearrange("p t i -> p (t i)").bitcast(I32))
+        tab_w0 = sb("tab_w0", [P, T], I32)
+        nc.sync.dma_start(tab_w0[:], tab_words[0].rearrange("p t i -> p (t i)").bitcast(I32))
         v_sc_g = sb("v_sc_g", [P, S], U8)
         nc.vector.tensor_copy(v_sc_g[:], tab_sc[:].indirect(idx[:]))
         for q in range(QUADS):
-            nc.scalar.dma_start(
+            (nc.sync if q % 2 == 0 else nc.scalar).dma_start(
                 v_sc[32 * q : 32 * q + 4, :].bitcast(I32), v_sc_g[32 * q : 32 * q + 32 : 4, :].bitcast(I32)
             )
-        ln_seg = sb("ln_seg", [P, PACK], F32, tag="tab_sc")
+        ln_seg = sb("ln_seg", [P, PACK], F32, tag="v_sc_g")
         nc.scalar.activation(ln_seg[:], seg_sb[:], ACT.Ln)
         warm = sb("warm", [P, 1], F32)
         nc.scalar.activation(warm[:], ln_seg[:, 0:1], ACT.Exp)
-        wq_sc = sb("wq_sc", [P, 2 * H], U8)
+        v2_g = sb("v2_g", [P, S2], I32, tag="tab_sc")
+        nc.vector.tensor_copy(v2_g[:].bitcast(U32), tab2_w[:].bitcast(U32).indirect(idx2[:]))
+        tab_w1 = sb("tab_w1", [P, T], I32)
+        nc.sync.dma_start(tab_w1[:], tab_words[1].rearrange("p t i -> p (t i)").bitcast(I32))
+        v2_w = sb("v2_w", [P, S2], I32)
+        nc.vector.tensor_copy(
+            v2_w[:].rearrange("p (t m) -> p m t", t=PACK), v2_g[:].rearrange("p (m t) -> p m t", t=PACK)
+        )
+        wq_sc = sb("wq_sc", [P, 2 * H], U8, tag="tab_sc")
         nc.vector.tensor_copy(
             wq_sc[:].rearrange("p (a t m) -> p a m t", a=2, t=PACK),
             wq_sc_raw[:].rearrange("p a (m t) -> p a m t", t=PACK),
         )
-        tab2_w = sb("tab2_w", [P, T2], I32)
-        nc.sync.dma_start(tab2_w[:], tab2_words[0].rearrange("p t i -> p (t i)").bitcast(I32))
-        v_w0 = sb("v_w0", [P, S], I32)
-        nc.vector.tensor_copy(v_w0[:].bitcast(U32), tab_w0[:].bitcast(U32).indirect(idx[:]))
+        ev_sb = sb("ev_sb", [P, PACK, N], F32, tag="wq_sc_raw")
+        nc.sync.dma_start(ev_sb[:], ev.rearrange("(p t) n -> p t n", t=PACK))
+
+        def gather_pass(name, window, hf):
+            words = sb(name, [P, JC], I32)
+            nc.vector.tensor_copy(
+                words[:].bitcast(U32),
+                window[:].bitcast(U32).indirect(idx[:, hf * JC // 16 : (hf + 1) * JC // 16]),
+            )
+            return words
+
+        v_w0 = [gather_pass("v_w0_%d" % hf, tab_w0, hf) for hf in range(S // JC)]
         v2_sc_g = sb("v2_sc_g", [P, S2], U8, tag="tab_w0")
         nc.vector.tensor_copy(v2_sc_g[:], tab2_sc[:].indirect(idx2[:]))
-        ex_sc = sb("ex_sc", [P, N], U8, tag="tab2_sc")
-        nc.gpsimd.memset(ex_sc[:].bitcast(I32), 0)
-        for q in range(QUADS):
-            nc.scalar.dma_start(
-                ex_sc[32 * q : 32 * q + 4, :].bitcast(I32),
-                ex_scales[0, 4 * q : 4 * q + 4, :].bitcast(I32),
-            )
         v2_sc = sb("v2_sc", [P, S2], U8)
         nc.vector.tensor_copy(
             v2_sc[:].rearrange("p (t m) -> p m t", t=PACK), v2_sc_g[:].rearrange("p (m t) -> p m t", t=PACK)
         )
-        ev_sb = sb("ev_sb", [P, PACK, N], F32, tag="v_sc_g")
-        nc.sync.dma_start(ev_sb[:], ev.rearrange("(p t) n -> p t n", t=PACK))
         ex_w = sb("ex_w", [P, N], I32, tag="tab_w0")
         nc.sync.dma_start(ex_w[:], ex_words[0].rearrange("p c i -> p (c i)").bitcast(I32))
 
-        h_acc = [bank(b, [P, 2, JB] if b < 2 * SCALAR_QS else [P, PACK, JA]) for b in range(S // JA)]
+        h_acc = [bank(b, [P, 2, JB] if b // 2 == SCALAR_Q else [P, PACK, JA]) for b in range(S // JA)]
 
         def h_bank(b, a, words, col0):
             for k in range(PACK):
-                if b < 2 * SCALAR_QS:
+                if b // 2 == SCALAR_Q:
                     s, g = divmod(k, 2)
                     t, j0 = 2 * (b % 2) + s, (b // 2) * JB + g * JA
                     dst = h_acc[b][:, s, g * JA : (g + 1) * JA]
@@ -144,7 +158,8 @@ def tile_list_memory_decoder_evidence_kernel(
                 )
 
         for b in range(S // JA):
-            h_bank(b, 0, v_w0, 0)
+            hf = b * JA // JC
+            h_bank(b, 0, v_w0[hf], hf * JC)
 
         v_w1 = [sb("v_w1_%d" % hf, [P, JC], I32) for hf in range(S // JC)]
         h_bf = [sb("h_bf%d" % q, [P, JB * PACK], BF16) for q in range(S // JB)]
@@ -166,17 +181,17 @@ def tile_list_memory_decoder_evidence_kernel(
                 dst.rearrange("p (c i t) -> p c t i", i=4, t=PACK), src.rearrange("p t (c i) -> p c t i", i=4)
             )
 
-        h_planes = [sb("h_planes%d" % q, [P, PACK, JB], BF16) for q in range(SCALAR_QS)]
+        h_planes = sb("h_planes", [P, PACK, JB], BF16)
 
         def finish_h(b):
             hf = b * JA // JC
             h_bank(b, 1, v_w1[hf], hf * JC)
             q, u = divmod(b, 2)
-            if q < SCALAR_QS:
+            if q == SCALAR_Q:
                 for s in range(2):
                     t = 2 * u + s
                     nc.scalar.activation(
-                        h_planes[q][:, t, :], h_acc[b][:, s, :], ACT.Identity, bias=bq_sb[:, t : t + 1]
+                        h_planes[:, t, :], h_acc[b][:, s, :], ACT.Identity, bias=bq_sb[:, t : t + 1]
                     )
             else:
                 nc.vector.tensor_tensor(
@@ -187,7 +202,7 @@ def tile_list_memory_decoder_evidence_kernel(
                 )
 
         def interleave_h(q):
-            interleave(nc.vector.tensor_copy, h_bf[q][:], h_planes[q][:])
+            interleave(nc.vector.tensor_copy, h_bf[q][:], h_planes[:])
 
         def scores(q):
             nc.vector.quantize_mx(out=h_w[q][:].bitcast(FP8X4), scales=h_sc[q][:], in_=h_bf[q][:])
@@ -257,13 +272,6 @@ def tile_list_memory_decoder_evidence_kernel(
         for b in range(4):
             finish_h(b)
         gather_last_pass(1)
-        v2_g = sb("v2_g", [P, S2], I32)
-        nc.vector.tensor_copy(v2_g[:].bitcast(U32), tab2_w[:].bitcast(U32).indirect(idx2[:]))
-        interleave_h(0)
-        v2_w = sb("v2_w", [P, S2], I32)
-        nc.vector.tensor_copy(
-            v2_w[:].rearrange("p (t m) -> p m t", t=PACK), v2_g[:].rearrange("p (m t) -> p m t", t=PACK)
-        )
         scores(0)
         interleave_h(1)
         finish_h(4)

@@ -19,10 +19,20 @@ ALU = mybir.AluOpType
 P = 128
 PACK = 4
 QUADS = 4
-JA = 128
-JB = 256
-JC = 512
-SCALAR_Q = 1
+QUAD = P // QUADS
+ROWS = 4
+PASSES = K // (P * PACK)
+LIST_ROWS = 16
+RUN = 4
+
+STRIP = 128
+GROUP = 256
+HALF = 512
+STRIPS, GROUPS, HALVES = S // STRIP, S // GROUP, S // HALF
+N_TILES = N // P
+
+SCALAR_GROUP = 0
+VECTOR_EVERY = 4
 
 
 def tile_list_memory_decoder_evidence_kernel(
@@ -32,30 +42,53 @@ def tile_list_memory_decoder_evidence_kernel(
     nc = tc.nc
     with ExitStack() as ctx:
         keep = ctx.enter_context(tc.tile_pool(name="keep", bufs=1))
-        ring = ctx.enter_context(tc.tile_pool(name="ring", bufs=4))
+        shared = ctx.enter_context(tc.tile_pool(name="shared", bufs=1))
+        ring = ctx.enter_context(tc.tile_pool(name="ring", bufs=HALVES * N_TILES))
         psum = ctx.enter_context(tc.psum_pool(name="psum", bufs=1))
 
         def sb(name, shape, dtype, tag=None):
             return keep.tile(shape, dtype, name=name, tag=tag or name, align_bytes=64)
 
+        def sb_at(name, shape, dtype, offset):
+            return shared.tile(shape, dtype, name=name, offset=offset, align_bytes=64)
+
         def bank(b, shape):
             return psum.tile(shape, F32, name="bank%d" % b)
 
-        idx = keep.tile([P, S // 16], U16, name="idx")
-        idx2 = keep.tile([P, S2 // 16], U16, name="idx2")
-        tab_sc = sb("tab_sc", [P, T], U8)
+        def scale_rows(tile, quad):
+            return tile[QUAD * quad : QUAD * quad + ROWS]
+
+        def rows_of(quad):
+            return slice(ROWS * quad, ROWS * (quad + 1))
+
+        def reorder(dst, src):
+            nc.vector.tensor_copy(
+                dst.rearrange("p (t m) -> p m t", t=PACK), src.rearrange("p (m t) -> p m t", t=PACK)
+            )
+
+        def reorder_passes(dst, src):
+            nc.vector.tensor_copy(
+                dst.rearrange("p (a t m) -> p a m t", a=PASSES, t=PACK),
+                src.rearrange("p a (m t) -> p a m t", t=PACK),
+            )
+
+        tab_w1_end = 4 * T
+
+        idx = keep.tile([P, S // LIST_ROWS], U16, name="idx")
+        idx2 = keep.tile([P, S2 // LIST_ROWS], U16, name="idx2")
+        tab_sc = sb_at("tab_sc", [P, T], U8, tab_w1_end - T // 2)
         tab2_sc = sb("tab2_sc", [P, T2], U8)
-        wq_sc_raw = sb("wq_sc_raw", [P, 2, H], U8)
+        wq_sc_raw = sb("wq_sc_raw", [P, PASSES, H], U8)
         ex_sc = sb("ex_sc", [P, N], U8)
-        v_sc = sb("v_sc", [P, 2 * S], U8)
+        v_sc = sb("v_sc", [P, PASSES * S], U8)
         nc.vector.memset(tab_sc[:].bitcast(I32), 0)
         nc.gpsimd.memset(tab2_sc[:].bitcast(I32), 0)
         nc.vector.memset(wq_sc_raw[:].bitcast(I32), 0)
         nc.vector.memset(ex_sc[:].bitcast(I32), 0)
         nc.vector.memset(v_sc[:].bitcast(I32), 0)
 
-        wq_raw = sb("wq_raw", [P, 2, H // 2], I32, tag="tab_w0")
-        tab2_w = sb("tab2_w", [P, T2], I32, tag="tab_w1")
+        wq_raw = sb("wq_raw", [P, PASSES, H // 2], I32, tag="tab_w0")
+        tab2_w = sb("tab2_w", [P, T2], I32)
         seg_sb = sb("seg_sb", [P, PACK], F32)
         bq_sb = sb("bq_sb", [P, PACK], F32)
 
@@ -65,129 +98,118 @@ def tile_list_memory_decoder_evidence_kernel(
         nc.scalar.dma_start(bq_sb[:], bq.rearrange("(p t) -> p t", t=PACK))
         nc.sync.dma_start(tab2_w[:], tab2_words[0].rearrange("p t i -> p (t i)").bitcast(I32))
         nc.sync.dma_start(idx2[:], offs2)
+        tab_sc_step = P // (PASSES * QUADS * ROWS)
         nc.scalar.dma_start(
-            tab_sc[0:P:4, :].bitcast(I32), tab_scales.rearrange("a q t -> q a t").bitcast(I32)
+            tab_sc[0:P:tab_sc_step, :].bitcast(I32), tab_scales.rearrange("a q t -> q a t").bitcast(I32)
         )
-        for q in range(QUADS):
+        for quad in range(QUADS):
             nc.gpsimd.dma_start(
-                tab2_sc[32 * q : 32 * q + 4, :].bitcast(I32),
-                tab2_scales[0, 4 * q : 4 * q + 4, :].bitcast(I32),
+                scale_rows(tab2_sc, quad).bitcast(I32), tab2_scales[0, rows_of(quad), :].bitcast(I32)
             )
-        for q in range(QUADS):
+        for quad in range(QUADS):
             nc.scalar.dma_start(
-                wq_sc_raw[32 * q : 32 * q + 4, :, :].bitcast(I32),
-                wq_scales[:, 4 * q : 4 * q + 4, :].rearrange("a r c -> r a c").bitcast(I32),
+                scale_rows(wq_sc_raw, quad).bitcast(I32),
+                wq_scales[:, rows_of(quad), :].rearrange("a r c -> r a c").bitcast(I32),
             )
-        for q in range(QUADS):
+        for quad in range(QUADS):
             nc.gpsimd.dma_start(
-                ex_sc[32 * q : 32 * q + 4, :].bitcast(I32),
-                ex_scales[0, 4 * q : 4 * q + 4, :].bitcast(I32),
+                scale_rows(ex_sc, quad).bitcast(I32), ex_scales[0, rows_of(quad), :].bitcast(I32)
             )
 
-        wq_w = sb("wq_w", [P, 2 * H // 2], I32)
-        nc.vector.tensor_copy(
-            wq_w[:].bitcast(U16).rearrange("p (a t m) -> p a m t", a=2, t=PACK),
-            wq_raw[:].bitcast(U16).rearrange("p a (m t) -> p a m t", t=PACK),
-        )
+        wq_w = sb("wq_w", [P, PASSES * H // 2], I32)
+        reorder_passes(wq_w[:].bitcast(U16), wq_raw[:].bitcast(U16))
         tab_w0 = sb("tab_w0", [P, T], I32)
         nc.sync.dma_start(tab_w0[:], tab_words[0].rearrange("p t i -> p (t i)").bitcast(I32))
+
         v_sc_g = sb("v_sc_g", [P, S], U8)
         nc.vector.tensor_copy(v_sc_g[:], tab_sc[:].indirect(idx[:]))
-        for q in range(QUADS):
-            (nc.sync if q % 2 == 0 else nc.scalar).dma_start(
-                v_sc[32 * q : 32 * q + 4, :].bitcast(I32), v_sc_g[32 * q : 32 * q + 32 : 4, :].bitcast(I32)
+        for quad in range(QUADS):
+            (nc.sync if quad % 2 == 0 else nc.scalar).dma_start(
+                scale_rows(v_sc, quad).bitcast(I32),
+                v_sc_g[QUAD * quad : QUAD * (quad + 1) : tab_sc_step, :].bitcast(I32),
             )
+        tab_w1 = sb_at("tab_w1", [P, T], I32, 0)
+        nc.sync.dma_start(tab_w1[:], tab_words[1].rearrange("p t i -> p (t i)").bitcast(I32))
+
         ln_seg = sb("ln_seg", [P, PACK], F32, tag="v_sc_g")
         nc.scalar.activation(ln_seg[:], seg_sb[:], ACT.Ln)
         warm = sb("warm", [P, 1], F32)
         nc.scalar.activation(warm[:], ln_seg[:, 0:1], ACT.Exp)
-        v2_g = sb("v2_g", [P, S2], I32, tag="tab_sc")
+
+        v2_g = sb_at("v2_g", [P, S2], I32, tab_w1_end)
         nc.vector.tensor_copy(v2_g[:].bitcast(U32), tab2_w[:].bitcast(U32).indirect(idx2[:]))
-        tab_w1 = sb("tab_w1", [P, T], I32)
-        nc.sync.dma_start(tab_w1[:], tab_words[1].rearrange("p t i -> p (t i)").bitcast(I32))
         v2_w = sb("v2_w", [P, S2], I32)
-        nc.vector.tensor_copy(
-            v2_w[:].rearrange("p (t m) -> p m t", t=PACK), v2_g[:].rearrange("p (m t) -> p m t", t=PACK)
-        )
-        wq_sc = sb("wq_sc", [P, 2 * H], U8, tag="tab_sc")
-        nc.vector.tensor_copy(
-            wq_sc[:].rearrange("p (a t m) -> p a m t", a=2, t=PACK),
-            wq_sc_raw[:].rearrange("p a (m t) -> p a m t", t=PACK),
-        )
+        reorder(v2_w[:], v2_g[:])
+        wq_sc = sb_at("wq_sc", [P, PASSES * H], U8, tab_w1_end)
+        reorder_passes(wq_sc[:], wq_sc_raw[:])
         ev_sb = sb("ev_sb", [P, PACK, N], F32, tag="wq_sc_raw")
         nc.sync.dma_start(ev_sb[:], ev.rearrange("(p t) n -> p t n", t=PACK))
 
-        def gather_pass(name, window, hf):
-            words = sb(name, [P, JC], I32)
+        def gather_half(words, window, half):
+            cols = HALF // LIST_ROWS
             nc.vector.tensor_copy(
-                words[:].bitcast(U32),
-                window[:].bitcast(U32).indirect(idx[:, hf * JC // 16 : (hf + 1) * JC // 16]),
+                words[:].bitcast(U32), window[:].bitcast(U32).indirect(idx[:, half * cols : (half + 1) * cols])
             )
-            return words
 
-        v_w0 = [gather_pass("v_w0_%d" % hf, tab_w0, hf) for hf in range(S // JC)]
+        v_w0 = []
+        for half in range(HALVES):
+            v_w0.append(sb("v_w0_%d" % half, [P, HALF], I32))
+            gather_half(v_w0[half], tab_w0, half)
         v2_sc_g = sb("v2_sc_g", [P, S2], U8, tag="tab_w0")
         nc.vector.tensor_copy(v2_sc_g[:], tab2_sc[:].indirect(idx2[:]))
         v2_sc = sb("v2_sc", [P, S2], U8)
-        nc.vector.tensor_copy(
-            v2_sc[:].rearrange("p (t m) -> p m t", t=PACK), v2_sc_g[:].rearrange("p (m t) -> p m t", t=PACK)
-        )
+        reorder(v2_sc[:], v2_sc_g[:])
         ex_w = sb("ex_w", [P, N], I32, tag="tab_w0")
         nc.sync.dma_start(ex_w[:], ex_words[0].rearrange("p c i -> p (c i)").bitcast(I32))
 
-        h_acc = [bank(b, [P, 2, JB] if b // 2 == SCALAR_Q else [P, PACK, JA]) for b in range(S // JA)]
+        h_acc = [bank(b, [P, 2, GROUP] if b // 2 == SCALAR_GROUP else [P, PACK, STRIP]) for b in range(STRIPS)]
 
-        def h_bank(b, a, words, col0):
-            for k in range(PACK):
-                if b // 2 == SCALAR_Q:
-                    s, g = divmod(k, 2)
-                    t, j0 = 2 * (b % 2) + s, (b // 2) * JB + g * JA
-                    dst = h_acc[b][:, s, g * JA : (g + 1) * JA]
+        def h_bank(b, a, words):
+            half_start = b * STRIP // HALF * HALF
+            for step in range(PACK):
+                if b // 2 == SCALAR_GROUP:
+                    s, strip = divmod(step, 2)
+                    t, j0 = 2 * (b % 2) + s, (b // 2) * GROUP + strip * STRIP
+                    dst = h_acc[b][:, s, strip * STRIP : (strip + 1) * STRIP]
                 else:
-                    t, j0 = k, b * JA
-                    dst = h_acc[b][:, k, :]
+                    t, j0 = step, b * STRIP
+                    dst = h_acc[b][:, step, :]
                 col = a * H + t * P
                 nc.tensor.matmul_mx(
                     out=dst,
                     lhsT=wq_w[:].bitcast(U8)[:, 2 * col : 2 * (col + P)].bitcast(FP4X4),
                     lhsT_scale=wq_sc[:, col : col + P],
-                    rhs=words[:, j0 - col0 : j0 - col0 + JA].bitcast(FP8X4),
-                    rhs_scale=v_sc[:, a * S + j0 : a * S + j0 + JA],
-                    start=(a == 0 and k == 0),
-                    stop=(a == 1 and k == PACK - 1),
+                    rhs=words[:, j0 - half_start : j0 - half_start + STRIP].bitcast(FP8X4),
+                    rhs_scale=v_sc[:, a * S + j0 : a * S + j0 + STRIP],
+                    start=(a == 0 and step == 0),
+                    stop=(a == PASSES - 1 and step == PACK - 1),
                 )
 
-        for b in range(S // JA):
-            hf = b * JA // JC
-            h_bank(b, 0, v_w0[hf], hf * JC)
+        for b in range(STRIPS):
+            h_bank(b, 0, v_w0[b * STRIP // HALF])
 
-        v_w1 = [sb("v_w1_%d" % hf, [P, JC], I32) for hf in range(S // JC)]
-        h_bf = [sb("h_bf%d" % q, [P, JB * PACK], BF16) for q in range(S // JB)]
-        h_w = [sb("h_w%d" % q, [P, JB], I32) for q in range(S // JB)]
-        h_sc = [sb("h_sc%d" % q, [P, JB], U8) for q in range(S // JB)]
-        planes = [sb("planes%d" % q, [P, PACK, JB], BF16) for q in range(S // JB)]
-        act_bf = [sb("act_bf%d" % q, [P, JB * PACK], BF16) for q in range(S // JB)]
+        v_w1 = [sb("v_w1_%d" % half, [P, HALF], I32) for half in range(HALVES)]
+        h_bf = [sb("h_bf%d" % g, [P, GROUP * PACK], BF16) for g in range(GROUPS)]
+        h_w = [sb("h_w%d" % g, [P, GROUP], I32) for g in range(GROUPS)]
+        h_sc = [sb("h_sc%d" % g, [P, GROUP], U8) for g in range(GROUPS)]
+        act_planes = [sb("act_planes%d" % g, [P, PACK, GROUP], BF16) for g in range(GROUPS)]
+        act_bf = [sb("act_bf%d" % g, [P, GROUP * PACK], BF16) for g in range(GROUPS)]
         act_w = sb("act_w", [P, S], I32)
         act_sc = sb("act_sc", [P, S], U8)
-
-        def gather_last_pass(hf):
-            nc.vector.tensor_copy(
-                v_w1[hf][:].bitcast(U32),
-                tab_w1[:].bitcast(U32).indirect(idx[:, hf * JC // 16 : (hf + 1) * JC // 16]),
-            )
+        h_planes = sb("h_planes", [P, PACK, GROUP], BF16)
+        ev_bf = sb("ev_bf", [P, N * PACK], BF16)
+        ev_w = sb("ev_w", [P, N], I32)
+        ev_sc = sb("ev_sc", [P, N], U8)
 
         def interleave(engine_copy, dst, src):
             engine_copy(
-                dst.rearrange("p (c i t) -> p c t i", i=4, t=PACK), src.rearrange("p t (c i) -> p c t i", i=4)
+                dst.rearrange("p (c i t) -> p c t i", i=RUN, t=PACK), src.rearrange("p t (c i) -> p c t i", i=RUN)
             )
 
-        h_planes = sb("h_planes", [P, PACK, JB], BF16)
-
         def finish_h(b):
-            hf = b * JA // JC
-            h_bank(b, 1, v_w1[hf], hf * JC)
-            q, u = divmod(b, 2)
-            if q == SCALAR_Q:
+            h_bank(b, PASSES - 1, v_w1[b * STRIP // HALF])
+            g, u = divmod(b, 2)
+            if g == SCALAR_GROUP:
                 for s in range(2):
                     t = 2 * u + s
                     nc.scalar.activation(
@@ -195,86 +217,79 @@ def tile_list_memory_decoder_evidence_kernel(
                     )
             else:
                 nc.vector.tensor_tensor(
-                    h_bf[q][:, PACK * u * JA : PACK * (u + 1) * JA].rearrange("p (j t) -> p j t", t=PACK),
+                    h_bf[g][:, PACK * u * STRIP : PACK * (u + 1) * STRIP].rearrange("p (j t) -> p j t", t=PACK),
                     h_acc[b][:].rearrange("p t j -> p j t"),
-                    bq_sb[:].unsqueeze(1).to_broadcast([P, JA, PACK]),
+                    bq_sb[:].unsqueeze(1).to_broadcast([P, STRIP, PACK]),
                     ALU.add,
                 )
 
-        def interleave_h(q):
-            interleave(nc.vector.tensor_copy, h_bf[q][:], h_planes[:])
-
-        def scores(q):
-            nc.vector.quantize_mx(out=h_w[q][:].bitcast(FP8X4), scales=h_sc[q][:], in_=h_bf[q][:])
+        def scores(g):
+            nc.vector.quantize_mx(out=h_w[g][:].bitcast(FP8X4), scales=h_sc[g][:], in_=h_bf[g][:])
             for u in range(2):
-                e_acc = bank(2 * q + u, [P, 2, JB])
+                e_acc = bank(2 * g + u, [P, 2, GROUP])
                 for s in range(2):
                     t = 2 * u + s
                     nc.tensor.matmul_mx(
                         out=e_acc[:, s, :],
                         lhsT=v2_w[:, t * P : (t + 1) * P].bitcast(FP8X4),
                         lhsT_scale=v2_sc[:, t * P : (t + 1) * P],
-                        rhs=h_w[q][:].bitcast(FP8X4),
-                        rhs_scale=h_sc[q][:],
+                        rhs=h_w[g][:].bitcast(FP8X4),
+                        rhs_scale=h_sc[g][:],
                         start=True,
                         stop=True,
                     )
                 for s in range(2):
                     t = 2 * u + s
                     nc.scalar.activation(
-                        planes[q][:, t, :], e_acc[:, s, :], ACT.Exp, bias=ln_seg[:, t : t + 1]
+                        act_planes[g][:, t, :], e_acc[:, s, :], ACT.Exp, bias=ln_seg[:, t : t + 1]
                     )
 
-        def interleave_act(q):
-            interleave(nc.vector.tensor_copy, act_bf[q][:], planes[q][:])
+        def interleave_act(g):
+            interleave(nc.vector.tensor_copy, act_bf[g][:], act_planes[g][:])
 
-        def quantize_act(q):
-            cols = slice(q * JB, (q + 1) * JB)
-            nc.vector.quantize_mx(out=act_w[:, cols].bitcast(FP8X4), scales=act_sc[:, cols], in_=act_bf[q][:])
+        def quantize_act(g):
+            cols = slice(g * GROUP, (g + 1) * GROUP)
+            nc.vector.quantize_mx(out=act_w[:, cols].bitcast(FP8X4), scales=act_sc[:, cols], in_=act_bf[g][:])
 
-        ev_bf = sb("ev_bf", [P, N * PACK], BF16)
-        ev_w = sb("ev_w", [P, N], I32)
-        ev_sc = sb("ev_sc", [P, N], U8)
-
-        def mix(acc, words, scales, nt, hf):
+        def mix(acc, words, scales, nt, half):
             nc.tensor.matmul_mx(
                 out=acc[:],
                 lhsT=words[:, nt * P : (nt + 1) * P].bitcast(FP8X4),
                 lhsT_scale=scales[:, nt * P : (nt + 1) * P],
-                rhs=act_w[:, hf * JC : (hf + 1) * JC].bitcast(FP8X4),
-                rhs_scale=act_sc[:, hf * JC : (hf + 1) * JC],
+                rhs=act_w[:, half * HALF : (half + 1) * HALF].bitcast(FP8X4),
+                rhs_scale=act_sc[:, half * HALF : (half + 1) * HALF],
                 start=True,
                 stop=True,
             )
 
-        def divide(hf):
+        def divide(half):
             dens = []
-            for nt in range(N // P):
-                den = bank(4 * hf + nt, [P, JC])
-                mix(den, ex_w, ex_sc, nt, hf)
+            for nt in range(N_TILES):
+                den = bank(N_TILES * half + nt, [P, HALF])
+                mix(den, ex_w, ex_sc, nt, half)
                 dens.append(den)
-            for nt in range(N // P):
-                root = ring.tile([P, JC], F32, name="root")
+            for nt in range(N_TILES):
+                root = ring.tile([P, HALF], F32, name="root")
                 nc.scalar.activation(root[:], dens[nt][:], ACT.Abs_reciprocal_sqrt)
-                num = bank(nt, [P, JC])
-                mix(num, ev_w, ev_sc, nt, hf)
-                part = ring.tile([P, JC], F32, name="part")
-                res = ring.tile([P, JC], F32, name="res")
-                if nt % 2 == 0:
+                num = bank(nt, [P, HALF])
+                mix(num, ev_w, ev_sc, nt, half)
+                part = ring.tile([P, HALF], F32, name="part")
+                res = ring.tile([P, HALF], F32, name="res")
+                if (N_TILES * half + nt) % VECTOR_EVERY == 0:
                     nc.vector.tensor_tensor(part[:], num[:], root[:], ALU.mult)
                     nc.vector.tensor_tensor(res[:], part[:], root[:], ALU.mult)
                 else:
                     nc.scalar.activation(part[:], root[:], ACT.Square)
                     nc.vector.tensor_tensor(res[:], num[:], part[:], ALU.mult)
-                nc.sync.dma_start(out[nt * P : (nt + 1) * P, hf * JC : (hf + 1) * JC], res[:])
+                nc.sync.dma_start(out[nt * P : (nt + 1) * P, half * HALF : (half + 1) * HALF], res[:])
 
-        gather_last_pass(0)
-        for b in range(4):
+        gather_half(v_w1[0], tab_w1, 0)
+        for b in range(STRIPS // HALVES):
             finish_h(b)
-        gather_last_pass(1)
-        scores(0)
-        interleave_h(1)
+        gather_half(v_w1[1], tab_w1, 1)
+        interleave(nc.vector.tensor_copy, h_bf[SCALAR_GROUP][:], h_planes[:])
         finish_h(4)
+        scores(0)
         scores(1)
         finish_h(5)
         finish_h(6)
@@ -282,11 +297,12 @@ def tile_list_memory_decoder_evidence_kernel(
         finish_h(7)
         interleave_act(0)
         scores(3)
+        piece = N // 2
         for u in range(2):
             interleave(
                 nc.scalar.copy,
-                ev_bf[:, u * PACK * JB : (u + 1) * PACK * JB],
-                ev_sb[:, :, u * JB : (u + 1) * JB],
+                ev_bf[:, u * PACK * piece : (u + 1) * PACK * piece],
+                ev_sb[:, :, u * piece : (u + 1) * piece],
             )
         interleave_act(1)
         quantize_act(0)
@@ -296,5 +312,5 @@ def tile_list_memory_decoder_evidence_kernel(
         quantize_act(2)
         interleave_act(3)
         quantize_act(3)
-        divide(0)
-        divide(1)
+        for half in range(HALVES):
+            divide(half)

@@ -21,6 +21,7 @@ PACK = 4
 QUADS = 4
 QUAD = P // QUADS
 ROWS = 4
+BLOCKS = QUADS * ROWS
 PASSES = K // (P * PACK)
 LIST_ROWS = 16
 RUN = 4
@@ -31,8 +32,8 @@ HALF = 512
 STRIPS, GROUPS, HALVES = S // STRIP, S // GROUP, S // HALF
 N_TILES = N // P
 
-SCALAR_GROUP = 0
-VECTOR_EVERY = 4
+SCALAR_GROUPS = 2
+VECTOR_TILES = (2, 4, 6)
 
 
 def tile_list_memory_decoder_evidence_kernel(
@@ -58,9 +59,6 @@ def tile_list_memory_decoder_evidence_kernel(
         def scale_rows(tile, quad):
             return tile[QUAD * quad : QUAD * quad + ROWS]
 
-        def rows_of(quad):
-            return slice(ROWS * quad, ROWS * (quad + 1))
-
         def reorder(dst, src):
             nc.vector.tensor_copy(
                 dst.rearrange("p (t m) -> p m t", t=PACK), src.rearrange("p (m t) -> p m t", t=PACK)
@@ -72,78 +70,65 @@ def tile_list_memory_decoder_evidence_kernel(
                 src.rearrange("p a (m t) -> p a m t", t=PACK),
             )
 
-        tab_w1_end = 4 * T
-
         idx = keep.tile([P, S // LIST_ROWS], U16, name="idx")
         idx2 = keep.tile([P, S2 // LIST_ROWS], U16, name="idx2")
-        tab_sc = sb_at("tab_sc", [P, T], U8, tab_w1_end - T // 2)
-        tab2_sc = sb("tab2_sc", [P, T2], U8)
-        wq_sc_raw = sb("wq_sc_raw", [P, PASSES, H], U8)
-        ex_sc = sb("ex_sc", [P, N], U8)
-        v_sc = sb("v_sc", [P, PASSES * S], U8)
-        nc.vector.memset(tab_sc[:].bitcast(I32), 0)
-        nc.gpsimd.memset(tab2_sc[:].bitcast(I32), 0)
-        nc.vector.memset(wq_sc_raw[:].bitcast(I32), 0)
-        nc.vector.memset(ex_sc[:].bitcast(I32), 0)
-        nc.vector.memset(v_sc[:].bitcast(I32), 0)
 
-        wq_raw = sb("wq_raw", [P, PASSES, H // 2], I32, tag="tab_w0")
-        tab2_w = sb("tab2_w", [P, T2], I32)
+        two_pass_row0 = P - PASSES * BLOCKS
+        one_pass_row0 = P - BLOCKS
+        tab_sc = sb("tab_sc", [P, T], U8)
+        wq_sc_raw = sb("wq_sc_raw", [P, H], U8)
+        tab2_sc = sb("tab2_sc", [P, T2], U8)
+        first_rows = sb("first_rows", [P, S + H], U8)
+        first_sc = sb("first_sc", [P, PASSES * (S + H)], U8)
+        later_rows = sb("later_rows", [P, S2 + N], U8)
+        later_sc = sb("later_sc", [P, S2 + N], U8)
+        nc.vector.memset(tab_sc[0:two_pass_row0, :].bitcast(I32), 0)
+        nc.vector.memset(wq_sc_raw[0:two_pass_row0, :].bitcast(I32), 0)
+        nc.vector.memset(tab2_sc[0:one_pass_row0, :].bitcast(I32), 0)
+        nc.vector.memset(first_sc[:].bitcast(I32), 0)
+        nc.vector.memset(later_sc[:].bitcast(I32), 0)
+
+        wq_raw = sb("wq_raw", [P, PASSES, H // 2], I32)
+        tab_w0 = sb("tab_w0", [P, T], I32)
         seg_sb = sb("seg_sb", [P, PACK], F32)
         bq_sb = sb("bq_sb", [P, PACK], F32)
 
-        nc.sync.dma_start(wq_raw[:], wq_words.rearrange("a p c -> p a c").bitcast(I32))
+        nc.scalar.dma_start(tab_sc[two_pass_row0:P, :].bitcast(I32), tab_scales.rearrange("a q t -> q a t").bitcast(I32))
         nc.sync.dma_start(idx[:], offs)
-        nc.scalar.dma_start(seg_sb[:], seg.rearrange("(p t) -> p t", t=PACK))
-        nc.scalar.dma_start(bq_sb[:], bq.rearrange("(p t) -> p t", t=PACK))
-        nc.sync.dma_start(tab2_w[:], tab2_words[0].rearrange("p t i -> p (t i)").bitcast(I32))
+        nc.scalar.dma_start(wq_sc_raw[two_pass_row0:P, :].bitcast(I32), wq_scales.rearrange("a q c -> q a c").bitcast(I32))
         nc.sync.dma_start(idx2[:], offs2)
-        tab_sc_step = P // (PASSES * QUADS * ROWS)
-        nc.scalar.dma_start(
-            tab_sc[0:P:tab_sc_step, :].bitcast(I32), tab_scales.rearrange("a q t -> q a t").bitcast(I32)
-        )
-        for quad in range(QUADS):
-            nc.gpsimd.dma_start(
-                scale_rows(tab2_sc, quad).bitcast(I32), tab2_scales[0, rows_of(quad), :].bitcast(I32)
-            )
-        for quad in range(QUADS):
-            nc.scalar.dma_start(
-                scale_rows(wq_sc_raw, quad).bitcast(I32),
-                wq_scales[:, rows_of(quad), :].rearrange("a r c -> r a c").bitcast(I32),
-            )
-        for quad in range(QUADS):
-            nc.gpsimd.dma_start(
-                scale_rows(ex_sc, quad).bitcast(I32), ex_scales[0, rows_of(quad), :].bitcast(I32)
-            )
-
-        wq_w = sb("wq_w", [P, PASSES * H // 2], I32)
-        reorder_passes(wq_w[:].bitcast(U16), wq_raw[:].bitcast(U16))
-        tab_w0 = sb("tab_w0", [P, T], I32)
+        nc.scalar.dma_start(tab2_sc[one_pass_row0:P, :].bitcast(I32), tab2_scales[0].bitcast(I32))
+        nc.scalar.dma_start(wq_raw[:], wq_words.rearrange("a p c -> p a c").bitcast(I32))
         nc.sync.dma_start(tab_w0[:], tab_words[0].rearrange("p t i -> p (t i)").bitcast(I32))
+        ex_w = sb("ex_w", [P, N], I32)
+        nc.sync.dma_start(ex_w[:], ex_words[0].rearrange("p c i -> p (c i)").bitcast(I32))
+        nc.gpsimd.dma_start(seg_sb[:], seg.rearrange("(p t) -> p t", t=PACK))
+        nc.gpsimd.dma_start(bq_sb[:], bq.rearrange("(p t) -> p t", t=PACK))
+        nc.gpsimd.dma_start(later_rows[one_pass_row0:P, S2:].bitcast(I32), ex_scales[0].bitcast(I32))
 
-        v_sc_g = sb("v_sc_g", [P, S], U8)
-        nc.vector.tensor_copy(v_sc_g[:], tab_sc[:].indirect(idx[:]))
-        for quad in range(QUADS):
-            (nc.sync if quad % 2 == 0 else nc.scalar).dma_start(
-                scale_rows(v_sc, quad).bitcast(I32),
-                v_sc_g[QUAD * quad : QUAD * (quad + 1) : tab_sc_step, :].bitcast(I32),
-            )
-        tab_w1 = sb_at("tab_w1", [P, T], I32, 0)
-        nc.sync.dma_start(tab_w1[:], tab_words[1].rearrange("p t i -> p (t i)").bitcast(I32))
-
-        ln_seg = sb("ln_seg", [P, PACK], F32, tag="v_sc_g")
+        ln_seg = sb("ln_seg", [P, PACK], F32)
         nc.scalar.activation(ln_seg[:], seg_sb[:], ACT.Ln)
         warm = sb("warm", [P, 1], F32)
         nc.scalar.activation(warm[:], ln_seg[:, 0:1], ACT.Exp)
 
-        v2_g = sb_at("v2_g", [P, S2], I32, tab_w1_end)
-        nc.vector.tensor_copy(v2_g[:].bitcast(U32), tab2_w[:].bitcast(U32).indirect(idx2[:]))
-        v2_w = sb("v2_w", [P, S2], I32)
-        reorder(v2_w[:], v2_g[:])
-        wq_sc = sb_at("wq_sc", [P, PASSES * H], U8, tab_w1_end)
-        reorder_passes(wq_sc[:], wq_sc_raw[:])
-        ev_sb = sb("ev_sb", [P, PACK, N], F32, tag="wq_sc_raw")
-        nc.sync.dma_start(ev_sb[:], ev.rearrange("(p t) n -> p t n", t=PACK))
+        tab2_at = 4 * T
+        v_sc_g = sb_at("v_sc_g", [P, S], U8, tab2_at - S // 2)
+        nc.vector.tensor_copy(v_sc_g[:], tab_sc[:].indirect(idx[:]))
+        reorder(first_rows[:, S:], wq_sc_raw[:])
+        nc.vector.tensor_copy(first_rows[:, 0:S].bitcast(I32), v_sc_g[:].bitcast(I32))
+        rows_a_quad = PASSES * ROWS
+        for quad in range(QUADS):
+            row0 = two_pass_row0 + rows_a_quad * quad
+            nc.sync.dma_start(
+                scale_rows(first_sc, quad).bitcast(I32), first_rows[row0 : row0 + rows_a_quad, :].bitcast(I32)
+            )
+        tab_w1 = sb_at("tab_w1", [P, T], I32, 0)
+        nc.sync.dma_start(tab_w1[:], tab_words[1].rearrange("p t i -> p (t i)").bitcast(I32))
+        tab2_w = sb_at("tab2_w", [P, T2], I32, tab2_at)
+        nc.sync.dma_start(tab2_w[:], tab2_words[0].rearrange("p t i -> p (t i)").bitcast(I32))
+
+        wq_w = sb("wq_w", [P, PASSES * H // 2], I32)
+        reorder_passes(wq_w[:].bitcast(U16), wq_raw[:].bitcast(U16))
 
         def gather_half(words, window, half):
             cols = HALF // LIST_ROWS
@@ -155,19 +140,25 @@ def tile_list_memory_decoder_evidence_kernel(
         for half in range(HALVES):
             v_w0.append(sb("v_w0_%d" % half, [P, HALF], I32))
             gather_half(v_w0[half], tab_w0, half)
-        v2_sc_g = sb("v2_sc_g", [P, S2], U8, tag="tab_w0")
-        nc.vector.tensor_copy(v2_sc_g[:], tab2_sc[:].indirect(idx2[:]))
-        v2_sc = sb("v2_sc", [P, S2], U8)
-        reorder(v2_sc[:], v2_sc_g[:])
-        ex_w = sb("ex_w", [P, N], I32, tag="tab_w0")
-        nc.sync.dma_start(ex_w[:], ex_words[0].rearrange("p c i -> p (c i)").bitcast(I32))
 
-        h_acc = [bank(b, [P, 2, GROUP] if b // 2 == SCALAR_GROUP else [P, PACK, STRIP]) for b in range(STRIPS)]
+        ev_at = tab2_at + 4 * T2
+        v2_sc_g = sb_at("v2_sc_g", [P, S2], U8, ev_at)
+        nc.vector.tensor_copy(v2_sc_g[:], tab2_sc[:].indirect(idx2[:]))
+        reorder(later_rows[:, 0:S2], v2_sc_g[:])
+        for quad in range(QUADS):
+            row0 = one_pass_row0 + ROWS * quad
+            nc.sync.dma_start(scale_rows(later_sc, quad).bitcast(I32), later_rows[row0 : row0 + ROWS, :].bitcast(I32))
+        v2_sc = later_sc[:, 0:S2]
+        ex_sc = later_sc[:, S2:]
+        ev_sb = sb_at("ev_sb", [P, PACK, N], F32, ev_at)
+        nc.sync.dma_start(ev_sb[:], ev.rearrange("(p t) n -> p t n", t=PACK))
+
+        h_acc = [bank(b, [P, 2, GROUP] if b // 2 < SCALAR_GROUPS else [P, PACK, STRIP]) for b in range(STRIPS)]
 
         def h_bank(b, a, words):
             half_start = b * STRIP // HALF * HALF
             for step in range(PACK):
-                if b // 2 == SCALAR_GROUP:
+                if b // 2 < SCALAR_GROUPS:
                     s, strip = divmod(step, 2)
                     t, j0 = 2 * (b % 2) + s, (b // 2) * GROUP + strip * STRIP
                     dst = h_acc[b][:, s, strip * STRIP : (strip + 1) * STRIP]
@@ -178,9 +169,9 @@ def tile_list_memory_decoder_evidence_kernel(
                 nc.tensor.matmul_mx(
                     out=dst,
                     lhsT=wq_w[:].bitcast(U8)[:, 2 * col : 2 * (col + P)].bitcast(FP4X4),
-                    lhsT_scale=wq_sc[:, col : col + P],
+                    lhsT_scale=first_sc[:, a * (S + H) + S + t * P : a * (S + H) + S + (t + 1) * P],
                     rhs=words[:, j0 - half_start : j0 - half_start + STRIP].bitcast(FP8X4),
-                    rhs_scale=v_sc[:, a * S + j0 : a * S + j0 + STRIP],
+                    rhs_scale=first_sc[:, a * (S + H) + j0 : a * (S + H) + j0 + STRIP],
                     start=(a == 0 and step == 0),
                     stop=(a == PASSES - 1 and step == PACK - 1),
                 )
@@ -189,14 +180,15 @@ def tile_list_memory_decoder_evidence_kernel(
             h_bank(b, 0, v_w0[b * STRIP // HALF])
 
         v_w1 = [sb("v_w1_%d" % half, [P, HALF], I32) for half in range(HALVES)]
-        h_bf = [sb("h_bf%d" % g, [P, GROUP * PACK], BF16) for g in range(GROUPS)]
+        h_bf = [sb_at("h_bf%d" % g, [P, GROUP * PACK], BF16, tab2_at + 2 * g * GROUP * PACK) for g in range(GROUPS)]
         h_w = [sb("h_w%d" % g, [P, GROUP], I32) for g in range(GROUPS)]
         h_sc = [sb("h_sc%d" % g, [P, GROUP], U8) for g in range(GROUPS)]
         act_planes = [sb("act_planes%d" % g, [P, PACK, GROUP], BF16) for g in range(GROUPS)]
         act_bf = [sb("act_bf%d" % g, [P, GROUP * PACK], BF16) for g in range(GROUPS)]
         act_w = sb("act_w", [P, S], I32)
         act_sc = sb("act_sc", [P, S], U8)
-        h_planes = sb("h_planes", [P, PACK, GROUP], BF16)
+        h_planes = [sb("h_planes%d" % g, [P, PACK, GROUP], BF16) for g in range(SCALAR_GROUPS)]
+        v2_w = sb("v2_w", [P, S2], I32)
         ev_bf = sb("ev_bf", [P, N * PACK], BF16)
         ev_w = sb("ev_w", [P, N], I32)
         ev_sc = sb("ev_sc", [P, N], U8)
@@ -209,11 +201,11 @@ def tile_list_memory_decoder_evidence_kernel(
         def finish_h(b):
             h_bank(b, PASSES - 1, v_w1[b * STRIP // HALF])
             g, u = divmod(b, 2)
-            if g == SCALAR_GROUP:
+            if g < SCALAR_GROUPS:
                 for s in range(2):
                     t = 2 * u + s
                     nc.scalar.activation(
-                        h_planes[:, t, :], h_acc[b][:, s, :], ACT.Identity, bias=bq_sb[:, t : t + 1]
+                        h_planes[g][:, t, :], h_acc[b][:, s, :], ACT.Identity, bias=bq_sb[:, t : t + 1]
                     )
             else:
                 nc.vector.tensor_tensor(
@@ -265,17 +257,17 @@ def tile_list_memory_decoder_evidence_kernel(
         def divide(half):
             dens = []
             for nt in range(N_TILES):
-                den = bank(N_TILES * half + nt, [P, HALF])
+                den = bank(nt, [P, HALF])
                 mix(den, ex_w, ex_sc, nt, half)
                 dens.append(den)
             for nt in range(N_TILES):
                 root = ring.tile([P, HALF], F32, name="root")
                 nc.scalar.activation(root[:], dens[nt][:], ACT.Abs_reciprocal_sqrt)
-                num = bank(nt, [P, HALF])
+                num = bank(N_TILES + nt, [P, HALF])
                 mix(num, ev_w, ev_sc, nt, half)
                 part = ring.tile([P, HALF], F32, name="part")
                 res = ring.tile([P, HALF], F32, name="res")
-                if (N_TILES * half + nt) % VECTOR_EVERY == 0:
+                if N_TILES * half + nt in VECTOR_TILES:
                     nc.vector.tensor_tensor(part[:], num[:], root[:], ALU.mult)
                     nc.vector.tensor_tensor(res[:], part[:], root[:], ALU.mult)
                 else:
@@ -283,34 +275,32 @@ def tile_list_memory_decoder_evidence_kernel(
                     nc.vector.tensor_tensor(res[:], num[:], part[:], ALU.mult)
                 nc.sync.dma_start(out[nt * P : (nt + 1) * P, half * HALF : (half + 1) * HALF], res[:])
 
-        gather_half(v_w1[0], tab_w1, 0)
-        for b in range(STRIPS // HALVES):
+        for half in range(HALVES):
+            gather_half(v_w1[half], tab_w1, half)
+        for b in range(2 * SCALAR_GROUPS):
             finish_h(b)
-        gather_half(v_w1[1], tab_w1, 1)
-        interleave(nc.vector.tensor_copy, h_bf[SCALAR_GROUP][:], h_planes[:])
+        nc.vector.tensor_copy(
+            v2_w[:].bitcast(U32).rearrange("p (t m) -> p m t", t=PACK), tab2_w[:].bitcast(U32).indirect(idx2[:])
+        )
+        interleave(nc.vector.tensor_copy, h_bf[0][:], h_planes[0][:])
         finish_h(4)
         scores(0)
-        scores(1)
+        interleave(nc.vector.tensor_copy, h_bf[1][:], h_planes[1][:])
         finish_h(5)
+        scores(1)
         finish_h(6)
         scores(2)
         finish_h(7)
         interleave_act(0)
         scores(3)
-        piece = N // 2
-        for u in range(2):
-            interleave(
-                nc.scalar.copy,
-                ev_bf[:, u * PACK * piece : (u + 1) * PACK * piece],
-                ev_sb[:, :, u * piece : (u + 1) * piece],
-            )
         interleave_act(1)
         quantize_act(0)
+        interleave(nc.vector.tensor_copy, ev_bf[:], ev_sb[:])
         quantize_act(1)
-        interleave_act(2)
         nc.vector.quantize_mx(out=ev_w[:].bitcast(FP8X4), scales=ev_sc[:], in_=ev_bf[:])
-        quantize_act(2)
+        interleave_act(2)
         interleave_act(3)
+        quantize_act(2)
         quantize_act(3)
         for half in range(HALVES):
             divide(half)

@@ -33,7 +33,7 @@ STRIPS, GROUPS, HALVES = S // STRIP, S // GROUP, S // HALF
 N_TILES = N // P
 
 SCALAR_GROUPS = 2
-VECTOR_TILES = (2, 4, 6)
+GPSIMD_TILES = (0, 1, 3, 5)
 
 
 def tile_list_memory_decoder_evidence_kernel(
@@ -84,9 +84,9 @@ def tile_list_memory_decoder_evidence_kernel(
         later_sc = sb("later_sc", [P, S2 + N], U8)
         nc.vector.memset(tab_sc[0:two_pass_row0, :].bitcast(I32), 0)
         nc.vector.memset(wq_sc_raw[0:two_pass_row0, :].bitcast(I32), 0)
-        nc.vector.memset(tab2_sc[0:one_pass_row0, :].bitcast(I32), 0)
+        nc.gpsimd.memset(tab2_sc[0:one_pass_row0, :].bitcast(I32), 0)
         nc.vector.memset(first_sc[:].bitcast(I32), 0)
-        nc.vector.memset(later_sc[:].bitcast(I32), 0)
+        nc.gpsimd.memset(later_sc[:].bitcast(I32), 0)
 
         wq_raw = sb("wq_raw", [P, PASSES, H // 2], I32)
         tab_w0 = sb("tab_w0", [P, T], I32)
@@ -94,22 +94,15 @@ def tile_list_memory_decoder_evidence_kernel(
         bq_sb = sb("bq_sb", [P, PACK], F32)
 
         nc.scalar.dma_start(tab_sc[two_pass_row0:P, :].bitcast(I32), tab_scales.rearrange("a q t -> q a t").bitcast(I32))
-        nc.sync.dma_start(idx[:], offs)
-        nc.scalar.dma_start(wq_sc_raw[two_pass_row0:P, :].bitcast(I32), wq_scales.rearrange("a q c -> q a c").bitcast(I32))
-        nc.sync.dma_start(idx2[:], offs2)
-        nc.scalar.dma_start(tab2_sc[one_pass_row0:P, :].bitcast(I32), tab2_scales[0].bitcast(I32))
         nc.scalar.dma_start(wq_raw[:], wq_words.rearrange("a p c -> p a c").bitcast(I32))
+        nc.sync.dma_start(idx[:], offs)
+        nc.sync.dma_start(wq_sc_raw[two_pass_row0:P, :].bitcast(I32), wq_scales.rearrange("a q c -> q a c").bitcast(I32))
+        nc.sync.dma_start(idx2[:], offs2)
+        nc.sync.dma_start(tab2_sc[one_pass_row0:P, :].bitcast(I32), tab2_scales[0].bitcast(I32))
         nc.sync.dma_start(tab_w0[:], tab_words[0].rearrange("p t i -> p (t i)").bitcast(I32))
-        ex_w = sb("ex_w", [P, N], I32)
-        nc.sync.dma_start(ex_w[:], ex_words[0].rearrange("p c i -> p (c i)").bitcast(I32))
         nc.gpsimd.dma_start(seg_sb[:], seg.rearrange("(p t) -> p t", t=PACK))
         nc.gpsimd.dma_start(bq_sb[:], bq.rearrange("(p t) -> p t", t=PACK))
         nc.gpsimd.dma_start(later_rows[one_pass_row0:P, S2:].bitcast(I32), ex_scales[0].bitcast(I32))
-
-        ln_seg = sb("ln_seg", [P, PACK], F32)
-        nc.scalar.activation(ln_seg[:], seg_sb[:], ACT.Ln)
-        warm = sb("warm", [P, 1], F32)
-        nc.scalar.activation(warm[:], ln_seg[:, 0:1], ACT.Exp)
 
         tab2_at = 4 * T
         v_sc_g = sb_at("v_sc_g", [P, S], U8, tab2_at - S // 2)
@@ -119,13 +112,18 @@ def tile_list_memory_decoder_evidence_kernel(
         rows_a_quad = PASSES * ROWS
         for quad in range(QUADS):
             row0 = two_pass_row0 + rows_a_quad * quad
-            nc.sync.dma_start(
+            (nc.scalar if quad == 0 else nc.sync).dma_start(
                 scale_rows(first_sc, quad).bitcast(I32), first_rows[row0 : row0 + rows_a_quad, :].bitcast(I32)
             )
         tab_w1 = sb_at("tab_w1", [P, T], I32, 0)
         nc.sync.dma_start(tab_w1[:], tab_words[1].rearrange("p t i -> p (t i)").bitcast(I32))
         tab2_w = sb_at("tab2_w", [P, T2], I32, tab2_at)
         nc.sync.dma_start(tab2_w[:], tab2_words[0].rearrange("p t i -> p (t i)").bitcast(I32))
+
+        ln_seg = sb("ln_seg", [P, PACK], F32, tag="first_rows")
+        nc.scalar.activation(ln_seg[:], seg_sb[:], ACT.Ln)
+        warm = sb("warm", [P, 1], F32)
+        nc.scalar.activation(warm[:], ln_seg[:, 0:1], ACT.Exp)
 
         wq_w = sb("wq_w", [P, PASSES * H // 2], I32)
         reorder_passes(wq_w[:].bitcast(U16), wq_raw[:].bitcast(U16))
@@ -142,7 +140,8 @@ def tile_list_memory_decoder_evidence_kernel(
             gather_half(v_w0[half], tab_w0, half)
 
         ev_at = tab2_at + 4 * T2
-        v2_sc_g = sb_at("v2_sc_g", [P, S2], U8, ev_at)
+        ex_at = ev_at + 4 * PACK * N
+        v2_sc_g = sb_at("v2_sc_g", [P, S2], U8, ex_at - S2 // 2)
         nc.vector.tensor_copy(v2_sc_g[:], tab2_sc[:].indirect(idx2[:]))
         reorder(later_rows[:, 0:S2], v2_sc_g[:])
         for quad in range(QUADS):
@@ -152,6 +151,8 @@ def tile_list_memory_decoder_evidence_kernel(
         ex_sc = later_sc[:, S2:]
         ev_sb = sb_at("ev_sb", [P, PACK, N], F32, ev_at)
         nc.sync.dma_start(ev_sb[:], ev.rearrange("(p t) n -> p t n", t=PACK))
+        ex_w = sb_at("ex_w", [P, N], I32, ex_at)
+        nc.sync.dma_start(ex_w[:], ex_words[0].rearrange("p c i -> p (c i)").bitcast(I32))
 
         h_acc = [bank(b, [P, 2, GROUP] if b // 2 < SCALAR_GROUPS else [P, PACK, STRIP]) for b in range(STRIPS)]
 
@@ -184,7 +185,7 @@ def tile_list_memory_decoder_evidence_kernel(
         h_w = [sb("h_w%d" % g, [P, GROUP], I32) for g in range(GROUPS)]
         h_sc = [sb("h_sc%d" % g, [P, GROUP], U8) for g in range(GROUPS)]
         act_planes = [sb("act_planes%d" % g, [P, PACK, GROUP], BF16) for g in range(GROUPS)]
-        act_bf = [sb("act_bf%d" % g, [P, GROUP * PACK], BF16) for g in range(GROUPS)]
+        act_bf = [sb("act_bf%d" % half, [P, HALF * PACK], BF16) for half in range(HALVES)]
         act_w = sb("act_w", [P, S], I32)
         act_sc = sb("act_sc", [P, S], U8)
         h_planes = [sb("h_planes%d" % g, [P, PACK, GROUP], BF16) for g in range(SCALAR_GROUPS)]
@@ -237,11 +238,13 @@ def tile_list_memory_decoder_evidence_kernel(
                     )
 
         def interleave_act(g):
-            interleave(nc.vector.tensor_copy, act_bf[g][:], act_planes[g][:])
+            half, u = divmod(g, 2)
+            dst = act_bf[half][:, u * GROUP * PACK : (u + 1) * GROUP * PACK]
+            interleave(nc.vector.tensor_copy, dst, act_planes[g][:])
 
-        def quantize_act(g):
-            cols = slice(g * GROUP, (g + 1) * GROUP)
-            nc.vector.quantize_mx(out=act_w[:, cols].bitcast(FP8X4), scales=act_sc[:, cols], in_=act_bf[g][:])
+        def quantize_act(half):
+            cols = slice(half * HALF, (half + 1) * HALF)
+            nc.vector.quantize_mx(out=act_w[:, cols].bitcast(FP8X4), scales=act_sc[:, cols], in_=act_bf[half][:])
 
         def mix(acc, words, scales, nt, half):
             nc.tensor.matmul_mx(
@@ -267,12 +270,11 @@ def tile_list_memory_decoder_evidence_kernel(
                 mix(num, ev_w, ev_sc, nt, half)
                 part = ring.tile([P, HALF], F32, name="part")
                 res = ring.tile([P, HALF], F32, name="res")
-                if N_TILES * half + nt in VECTOR_TILES:
-                    nc.vector.tensor_tensor(part[:], num[:], root[:], ALU.mult)
-                    nc.vector.tensor_tensor(res[:], part[:], root[:], ALU.mult)
+                if N_TILES * half + nt in GPSIMD_TILES:
+                    nc.gpsimd.tensor_tensor(part[:], root[:], root[:], ALU.mult)
                 else:
                     nc.scalar.activation(part[:], root[:], ACT.Square)
-                    nc.vector.tensor_tensor(res[:], num[:], part[:], ALU.mult)
+                nc.vector.tensor_tensor(res[:], num[:], part[:], ALU.mult)
                 nc.sync.dma_start(out[nt * P : (nt + 1) * P, half * HALF : (half + 1) * HALF], res[:])
 
         for half in range(HALVES):
@@ -285,7 +287,7 @@ def tile_list_memory_decoder_evidence_kernel(
         interleave(nc.vector.tensor_copy, h_bf[0][:], h_planes[0][:])
         finish_h(4)
         scores(0)
-        interleave(nc.vector.tensor_copy, h_bf[1][:], h_planes[1][:])
+        interleave(nc.scalar.copy, h_bf[1][:], h_planes[1][:])
         finish_h(5)
         scores(1)
         finish_h(6)
@@ -294,13 +296,11 @@ def tile_list_memory_decoder_evidence_kernel(
         interleave_act(0)
         scores(3)
         interleave_act(1)
-        quantize_act(0)
         interleave(nc.vector.tensor_copy, ev_bf[:], ev_sb[:])
-        quantize_act(1)
-        nc.vector.quantize_mx(out=ev_w[:].bitcast(FP8X4), scales=ev_sc[:], in_=ev_bf[:])
+        quantize_act(0)
         interleave_act(2)
         interleave_act(3)
-        quantize_act(2)
-        quantize_act(3)
+        nc.vector.quantize_mx(out=ev_w[:].bitcast(FP8X4), scales=ev_sc[:], in_=ev_bf[:])
+        quantize_act(1)
         for half in range(HALVES):
             divide(half)

@@ -33,7 +33,7 @@ STRIPS, GROUPS, HALVES = S // STRIP, S // GROUP, S // HALF
 N_TILES = N // P
 
 SCALAR_GROUPS = 2
-GPSIMD_TILES = (0, 1, 3, 5)
+GPSIMD_TILES = (0, 2, 4, 6)
 
 
 def tile_list_memory_decoder_evidence_kernel(
@@ -75,17 +75,21 @@ def tile_list_memory_decoder_evidence_kernel(
 
         two_pass_row0 = P - PASSES * BLOCKS
         one_pass_row0 = P - BLOCKS
-        tab_sc = sb("tab_sc", [P, T], U8)
+        gap_at = 4 * T
+        tab2_at = gap_at + T
+        tab_sc = sb_at("tab_sc", [P, T], U8, tab2_at - T // 2)
         wq_sc_raw = sb("wq_sc_raw", [P, H], U8)
         tab2_sc = sb("tab2_sc", [P, T2], U8)
-        first_rows = sb("first_rows", [P, S + H], U8)
-        first_sc = sb("first_sc", [P, PASSES * (S + H)], U8)
+        first_rows = sb("first_rows", [P, HALF + H], U8)
+        first_sc = sb("first_sc", [P, PASSES * (HALF + H)], U8)
+        second_sc = sb("second_sc", [P, PASSES * HALF], U8)
         later_rows = sb("later_rows", [P, S2 + N], U8)
         later_sc = sb("later_sc", [P, S2 + N], U8)
         nc.vector.memset(tab_sc[0:two_pass_row0, :].bitcast(I32), 0)
         nc.vector.memset(wq_sc_raw[0:two_pass_row0, :].bitcast(I32), 0)
         nc.gpsimd.memset(tab2_sc[0:one_pass_row0, :].bitcast(I32), 0)
         nc.vector.memset(first_sc[:].bitcast(I32), 0)
+        nc.gpsimd.memset(second_sc[:].bitcast(I32), 0)
         nc.gpsimd.memset(later_sc[:].bitcast(I32), 0)
 
         wq_raw = sb("wq_raw", [P, PASSES, H // 2], I32)
@@ -95,8 +99,8 @@ def tile_list_memory_decoder_evidence_kernel(
 
         nc.scalar.dma_start(tab_sc[two_pass_row0:P, :].bitcast(I32), tab_scales.rearrange("a q t -> q a t").bitcast(I32))
         nc.scalar.dma_start(wq_raw[:], wq_words.rearrange("a p c -> p a c").bitcast(I32))
-        nc.sync.dma_start(idx[:], offs)
         nc.sync.dma_start(wq_sc_raw[two_pass_row0:P, :].bitcast(I32), wq_scales.rearrange("a q c -> q a c").bitcast(I32))
+        nc.sync.dma_start(idx[:], offs)
         nc.sync.dma_start(idx2[:], offs2)
         nc.sync.dma_start(tab2_sc[one_pass_row0:P, :].bitcast(I32), tab2_scales[0].bitcast(I32))
         nc.sync.dma_start(tab_w0[:], tab_words[0].rearrange("p t i -> p (t i)").bitcast(I32))
@@ -104,11 +108,11 @@ def tile_list_memory_decoder_evidence_kernel(
         nc.gpsimd.dma_start(bq_sb[:], bq.rearrange("(p t) -> p t", t=PACK))
         nc.gpsimd.dma_start(later_rows[one_pass_row0:P, S2:].bitcast(I32), ex_scales[0].bitcast(I32))
 
-        tab2_at = 4 * T
-        v_sc_g = sb_at("v_sc_g", [P, S], U8, tab2_at - S // 2)
-        nc.vector.tensor_copy(v_sc_g[:], tab_sc[:].indirect(idx[:]))
-        reorder(first_rows[:, S:], wq_sc_raw[:])
-        nc.vector.tensor_copy(first_rows[:, 0:S].bitcast(I32), v_sc_g[:].bitcast(I32))
+        half_cols = HALF // LIST_ROWS
+        v_sc_g = sb_at("v_sc_g", [P, HALF], U8, gap_at - HALF // 2)
+        reorder(first_rows[:, HALF:], wq_sc_raw[:])
+        nc.vector.tensor_copy(v_sc_g[:], tab_sc[:].indirect(idx[:, 0:half_cols]))
+        nc.vector.tensor_copy(first_rows[:, 0:HALF].bitcast(I32), v_sc_g[:].bitcast(I32))
         rows_a_quad = PASSES * ROWS
         for quad in range(QUADS):
             row0 = two_pass_row0 + rows_a_quad * quad
@@ -117,6 +121,13 @@ def tile_list_memory_decoder_evidence_kernel(
             )
         tab_w1 = sb_at("tab_w1", [P, T], I32, 0)
         nc.sync.dma_start(tab_w1[:], tab_words[1].rearrange("p t i -> p (t i)").bitcast(I32))
+        second_rows = sb("second_rows", [P, HALF], U8)
+        nc.vector.tensor_copy(second_rows[:], tab_sc[:].indirect(idx[:, half_cols:]))
+        for quad in range(QUADS):
+            row0 = two_pass_row0 + rows_a_quad * quad
+            nc.sync.dma_start(
+                scale_rows(second_sc, quad).bitcast(I32), second_rows[row0 : row0 + rows_a_quad, :].bitcast(I32)
+            )
         tab2_w = sb_at("tab2_w", [P, T2], I32, tab2_at)
         nc.sync.dma_start(tab2_w[:], tab2_words[0].rearrange("p t i -> p (t i)").bitcast(I32))
 
@@ -154,7 +165,7 @@ def tile_list_memory_decoder_evidence_kernel(
         ex_w = sb_at("ex_w", [P, N], I32, ex_at)
         nc.sync.dma_start(ex_w[:], ex_words[0].rearrange("p c i -> p (c i)").bitcast(I32))
 
-        h_acc = [bank(b, [P, 2, GROUP] if b // 2 < SCALAR_GROUPS else [P, PACK, STRIP]) for b in range(STRIPS)]
+        h_acc = [bank(b, [P, 2, GROUP]) for b in range(STRIPS // HALVES)]
 
         def h_bank(b, a, words):
             half_start = b * STRIP // HALF * HALF
@@ -167,18 +178,19 @@ def tile_list_memory_decoder_evidence_kernel(
                     t, j0 = step, b * STRIP
                     dst = h_acc[b][:, step, :]
                 col = a * H + t * P
+                v_sc = second_sc[:, a * HALF :] if half_start else first_sc[:, a * (HALF + H) :]
                 nc.tensor.matmul_mx(
                     out=dst,
                     lhsT=wq_w[:].bitcast(U8)[:, 2 * col : 2 * (col + P)].bitcast(FP4X4),
-                    lhsT_scale=first_sc[:, a * (S + H) + S + t * P : a * (S + H) + S + (t + 1) * P],
+                    lhsT_scale=first_sc[:, a * (HALF + H) + HALF + t * P : a * (HALF + H) + HALF + (t + 1) * P],
                     rhs=words[:, j0 - half_start : j0 - half_start + STRIP].bitcast(FP8X4),
-                    rhs_scale=first_sc[:, a * (S + H) + j0 : a * (S + H) + j0 + STRIP],
+                    rhs_scale=v_sc[:, j0 - half_start : j0 - half_start + STRIP],
                     start=(a == 0 and step == 0),
                     stop=(a == PASSES - 1 and step == PACK - 1),
                 )
 
-        for b in range(STRIPS):
-            h_bank(b, 0, v_w0[b * STRIP // HALF])
+        for b in range(STRIPS // HALVES):
+            h_bank(b, 0, v_w0[0])
 
         v_w1 = [sb("v_w1_%d" % half, [P, HALF], I32) for half in range(HALVES)]
         h_bf = [sb_at("h_bf%d" % g, [P, GROUP * PACK], BF16, tab2_at + 2 * g * GROUP * PACK) for g in range(GROUPS)]
@@ -200,6 +212,9 @@ def tile_list_memory_decoder_evidence_kernel(
             )
 
         def finish_h(b):
+            if b >= STRIPS // HALVES:
+                h_acc.append(bank(b - STRIPS // HALVES, [P, PACK, STRIP]))
+                h_bank(b, 0, v_w0[1])
             h_bank(b, PASSES - 1, v_w1[b * STRIP // HALF])
             g, u = divmod(b, 2)
             if g < SCALAR_GROUPS:
@@ -219,7 +234,7 @@ def tile_list_memory_decoder_evidence_kernel(
         def scores(g):
             nc.vector.quantize_mx(out=h_w[g][:].bitcast(FP8X4), scales=h_sc[g][:], in_=h_bf[g][:])
             for u in range(2):
-                e_acc = bank(2 * g + u, [P, 2, GROUP])
+                e_acc = bank(N_TILES + 2 * (g % 2) + u, [P, 2, GROUP])
                 for s in range(2):
                     t = 2 * u + s
                     nc.tensor.matmul_mx(
@@ -257,25 +272,28 @@ def tile_list_memory_decoder_evidence_kernel(
                 stop=True,
             )
 
-        def divide(half):
-            dens = []
-            for nt in range(N_TILES):
-                den = bank(nt, [P, HALF])
-                mix(den, ex_w, ex_sc, nt, half)
-                dens.append(den)
-            for nt in range(N_TILES):
-                root = ring.tile([P, HALF], F32, name="root")
-                nc.scalar.activation(root[:], dens[nt][:], ACT.Abs_reciprocal_sqrt)
-                num = bank(N_TILES + nt, [P, HALF])
-                mix(num, ev_w, ev_sc, nt, half)
-                part = ring.tile([P, HALF], F32, name="part")
-                res = ring.tile([P, HALF], F32, name="res")
-                if N_TILES * half + nt in GPSIMD_TILES:
-                    nc.gpsimd.tensor_tensor(part[:], root[:], root[:], ALU.mult)
-                else:
-                    nc.scalar.activation(part[:], root[:], ACT.Square)
-                nc.vector.tensor_tensor(res[:], num[:], part[:], ALU.mult)
-                nc.sync.dma_start(out[nt * P : (nt + 1) * P, half * HALF : (half + 1) * HALF], res[:])
+        inverses = []
+
+        def invert(tile):
+            half, nt = divmod(tile, N_TILES)
+            den = bank(nt, [P, HALF])
+            mix(den, ex_w, ex_sc, nt, half)
+            root = ring.tile([P, HALF], F32, name="root")
+            nc.scalar.activation(root[:], den[:], ACT.Abs_reciprocal_sqrt)
+            inverse = ring.tile([P, HALF], F32, name="inverse")
+            if tile in GPSIMD_TILES:
+                nc.gpsimd.tensor_tensor(inverse[:], root[:], root[:], ALU.mult)
+            else:
+                nc.scalar.activation(inverse[:], root[:], ACT.Square)
+            inverses.append(inverse)
+
+        def multiply(tile, step):
+            half, nt = divmod(tile, N_TILES)
+            num = bank(N_TILES + step % N_TILES, [P, HALF])
+            mix(num, ev_w, ev_sc, nt, half)
+            res = ring.tile([P, HALF], F32, name="res")
+            nc.vector.tensor_tensor(res[:], num[:], inverses[tile][:], ALU.mult)
+            nc.sync.dma_start(out[nt * P : (nt + 1) * P, half * HALF : (half + 1) * HALF], res[:])
 
         for half in range(HALVES):
             gather_half(v_w1[half], tab_w1, half)
@@ -302,5 +320,7 @@ def tile_list_memory_decoder_evidence_kernel(
         interleave_act(3)
         nc.vector.quantize_mx(out=ev_w[:].bitcast(FP8X4), scales=ev_sc[:], in_=ev_bf[:])
         quantize_act(1)
-        for half in range(HALVES):
-            divide(half)
+        tiles = HALVES * N_TILES
+        for tile in range(tiles):
+            invert(tile)
+            multiply(tile, tile)

@@ -165,7 +165,8 @@ def tile_list_memory_decoder_evidence_kernel(
         ex_w = sb_at("ex_w", [P, N], I32, ex_at)
         nc.sync.dma_start(ex_w[:], ex_words[0].rearrange("p c i -> p (c i)").bitcast(I32))
 
-        h_acc = [bank(b, [P, 2, GROUP]) for b in range(STRIPS // HALVES)]
+        plane_acc = [bank(b, [P, GROUP]) for b in range(SCALAR_GROUPS * PACK)]
+        h_acc = [None] * (STRIPS // HALVES)
 
         def h_bank(b, a, words):
             half_start = b * STRIP // HALF * HALF
@@ -173,10 +174,12 @@ def tile_list_memory_decoder_evidence_kernel(
                 if b // 2 < SCALAR_GROUPS:
                     s, strip = divmod(step, 2)
                     t, j0 = 2 * (b % 2) + s, (b // 2) * GROUP + strip * STRIP
-                    dst = h_acc[b][:, s, strip * STRIP : (strip + 1) * STRIP]
+                    dst = plane_acc[2 * b + s][:, strip * STRIP : (strip + 1) * STRIP]
+                    first, last = strip == 0, strip == 1
                 else:
                     t, j0 = step, b * STRIP
                     dst = h_acc[b][:, step, :]
+                    first, last = step == 0, step == PACK - 1
                 col = a * H + t * P
                 v_sc = second_sc[:, a * HALF :] if half_start else first_sc[:, a * (HALF + H) :]
                 nc.tensor.matmul_mx(
@@ -185,8 +188,8 @@ def tile_list_memory_decoder_evidence_kernel(
                     lhsT_scale=first_sc[:, a * (HALF + H) + HALF + t * P : a * (HALF + H) + HALF + (t + 1) * P],
                     rhs=words[:, j0 - half_start : j0 - half_start + STRIP].bitcast(FP8X4),
                     rhs_scale=v_sc[:, j0 - half_start : j0 - half_start + STRIP],
-                    start=(a == 0 and step == 0),
-                    stop=(a == PASSES - 1 and step == PACK - 1),
+                    start=(a == 0 and first),
+                    stop=(a == PASSES - 1 and last),
                 )
 
         for b in range(STRIPS // HALVES):
@@ -211,7 +214,16 @@ def tile_list_memory_decoder_evidence_kernel(
                 dst.rearrange("p (c i t) -> p c t i", i=RUN, t=PACK), src.rearrange("p t (c i) -> p c t i", i=RUN)
             )
 
-        def finish_h(b):
+        def add_bias(b, j0, j1):
+            g, u = divmod(b, 2)
+            nc.vector.tensor_tensor(
+                h_bf[g][:, PACK * (u * STRIP + j0) : PACK * (u * STRIP + j1)].rearrange("p (j t) -> p j t", t=PACK),
+                h_acc[b][:, :, j0:j1].rearrange("p t j -> p j t"),
+                bq_sb[:].unsqueeze(1).to_broadcast([P, j1 - j0, PACK]),
+                ALU.add,
+            )
+
+        def finish_h(b, width=STRIP):
             if b >= STRIPS // HALVES:
                 h_acc.append(bank(b - STRIPS // HALVES, [P, PACK, STRIP]))
                 h_bank(b, 0, v_w0[1])
@@ -221,22 +233,18 @@ def tile_list_memory_decoder_evidence_kernel(
                 for s in range(2):
                     t = 2 * u + s
                     nc.scalar.activation(
-                        h_planes[g][:, t, :], h_acc[b][:, s, :], ACT.Identity, bias=bq_sb[:, t : t + 1]
+                        h_planes[g][:, t, :], plane_acc[2 * b + s][:], ACT.Identity, bias=bq_sb[:, t : t + 1]
                     )
             else:
-                nc.vector.tensor_tensor(
-                    h_bf[g][:, PACK * u * STRIP : PACK * (u + 1) * STRIP].rearrange("p (j t) -> p j t", t=PACK),
-                    h_acc[b][:].rearrange("p t j -> p j t"),
-                    bq_sb[:].unsqueeze(1).to_broadcast([P, STRIP, PACK]),
-                    ALU.add,
-                )
+                add_bias(b, 0, width)
 
         def scores(g):
             nc.vector.quantize_mx(out=h_w[g][:].bitcast(FP8X4), scales=h_sc[g][:], in_=h_bf[g][:])
-            for u in range(2):
-                e_acc = bank(N_TILES + 2 * (g % 2) + u, [P, 2, GROUP])
-                for s in range(2):
-                    t = 2 * u + s
+            planes = 1 if g == 0 else 2
+            for u in range(PACK // planes):
+                e_acc = bank((4, 0, 4, 6)[g] + u, [P, planes, GROUP])
+                for s in range(planes):
+                    t = planes * u + s
                     nc.tensor.matmul_mx(
                         out=e_acc[:, s, :],
                         lhsT=v2_w[:, t * P : (t + 1) * P].bitcast(FP8X4),
@@ -246,8 +254,8 @@ def tile_list_memory_decoder_evidence_kernel(
                         start=True,
                         stop=True,
                     )
-                for s in range(2):
-                    t = 2 * u + s
+                for s in range(planes):
+                    t = planes * u + s
                     nc.scalar.activation(
                         act_planes[g][:, t, :], e_acc[:, s, :], ACT.Exp, bias=ln_seg[:, t : t + 1]
                     )
@@ -303,8 +311,9 @@ def tile_list_memory_decoder_evidence_kernel(
             v2_w[:].bitcast(U32).rearrange("p (t m) -> p m t", t=PACK), tab2_w[:].bitcast(U32).indirect(idx2[:])
         )
         interleave(nc.vector.tensor_copy, h_bf[0][:], h_planes[0][:])
-        finish_h(4)
+        finish_h(4, STRIP // 2)
         scores(0)
+        add_bias(4, STRIP // 2, STRIP)
         interleave(nc.scalar.copy, h_bf[1][:], h_planes[1][:])
         finish_h(5)
         scores(1)
@@ -314,11 +323,12 @@ def tile_list_memory_decoder_evidence_kernel(
         interleave_act(0)
         scores(3)
         interleave_act(1)
-        interleave(nc.vector.tensor_copy, ev_bf[:], ev_sb[:])
+        interleave(nc.vector.tensor_copy, ev_bf[:, 0 : PACK * GROUP], ev_sb[:, :, 0:GROUP])
         quantize_act(0)
+        interleave(nc.vector.tensor_copy, ev_bf[:, PACK * GROUP :], ev_sb[:, :, GROUP:])
         interleave_act(2)
-        interleave_act(3)
         nc.vector.quantize_mx(out=ev_w[:].bitcast(FP8X4), scales=ev_sc[:], in_=ev_bf[:])
+        interleave_act(3)
         quantize_act(1)
         tiles = HALVES * N_TILES
         for tile in range(tiles):

@@ -29,10 +29,10 @@ RUN = 4
 STRIP = 128
 GROUP = 256
 HALF = 512
-STRIPS, GROUPS, HALVES = S // STRIP, S // GROUP, S // HALF
+GROUPS, HALVES = S // GROUP, S // HALF
 N_TILES = N // P
 
-SCALAR_GROUPS = 2
+EARLY = T // 4
 GPSIMD_TILES = (0, 2, 4, 6)
 
 
@@ -47,8 +47,8 @@ def tile_list_memory_decoder_evidence_kernel(
         ring = ctx.enter_context(tc.tile_pool(name="ring", bufs=HALVES * N_TILES))
         psum = ctx.enter_context(tc.psum_pool(name="psum", bufs=1))
 
-        def sb(name, shape, dtype, tag=None):
-            return keep.tile(shape, dtype, name=name, tag=tag or name, align_bytes=64)
+        def sb(name, shape, dtype):
+            return keep.tile(shape, dtype, name=name, align_bytes=64)
 
         def sb_at(name, shape, dtype, offset):
             return shared.tile(shape, dtype, name=name, offset=offset, align_bytes=64)
@@ -56,156 +56,137 @@ def tile_list_memory_decoder_evidence_kernel(
         def bank(b, shape):
             return psum.tile(shape, F32, name="bank%d" % b)
 
-        def scale_rows(tile, quad):
-            return tile[QUAD * quad : QUAD * quad + ROWS]
-
         def reorder(dst, src):
             nc.vector.tensor_copy(
                 dst.rearrange("p (t m) -> p m t", t=PACK), src.rearrange("p (m t) -> p m t", t=PACK)
             )
 
-        def reorder_passes(dst, src):
-            nc.vector.tensor_copy(
-                dst.rearrange("p (a t m) -> p a m t", a=PASSES, t=PACK),
-                src.rearrange("p a (m t) -> p a m t", t=PACK),
-            )
+        def move_scale_rows(dst, src, row0):
+            for i in range(ROWS):
+                nc.sync.dma_start(dst[i:P:QUAD].bitcast(I32), src[row0 + i : row0 + BLOCKS : ROWS, :].bitcast(I32))
+
+        def words_of(dram):
+            return dram.rearrange("p t i -> p (t i)").bitcast(I32)
 
         idx = keep.tile([P, S // LIST_ROWS], U16, name="idx")
         idx2 = keep.tile([P, S2 // LIST_ROWS], U16, name="idx2")
 
         two_pass_row0 = P - PASSES * BLOCKS
         one_pass_row0 = P - BLOCKS
-        gap_at = 4 * T
-        tab2_at = gap_at + T
-        tab_sc = sb_at("tab_sc", [P, T], U8, tab2_at - T // 2)
+        tab_sc = sb("tab_sc", [P, T], U8)
         wq_sc_raw = sb("wq_sc_raw", [P, H], U8)
         tab2_sc = sb("tab2_sc", [P, T2], U8)
-        first_rows = sb("first_rows", [P, HALF + H], U8)
-        first_sc = sb("first_sc", [P, PASSES * (HALF + H)], U8)
-        second_sc = sb("second_sc", [P, PASSES * HALF], U8)
+        first_rows = sb("first_rows", [P, S + H], U8)
+        first_sc = [sb("first_sc%d" % a, [P, S + H], U8) for a in range(PASSES)]
         later_rows = sb("later_rows", [P, S2 + N], U8)
         later_sc = sb("later_sc", [P, S2 + N], U8)
         nc.vector.memset(tab_sc[0:two_pass_row0, :].bitcast(I32), 0)
         nc.vector.memset(wq_sc_raw[0:two_pass_row0, :].bitcast(I32), 0)
+        nc.vector.memset(first_sc[0][:].bitcast(I32), 0)
+        nc.gpsimd.memset(first_sc[1][:].bitcast(I32), 0)
         nc.gpsimd.memset(tab2_sc[0:one_pass_row0, :].bitcast(I32), 0)
-        nc.vector.memset(first_sc[:].bitcast(I32), 0)
-        nc.gpsimd.memset(second_sc[:].bitcast(I32), 0)
         nc.gpsimd.memset(later_sc[:].bitcast(I32), 0)
 
-        wq_raw = sb("wq_raw", [P, PASSES, H // 2], I32)
-        tab_w0 = sb("tab_w0", [P, T], I32)
+        head_at = 16 * 1024
+        wq_raw = sb_at("wq_raw", [P, PASSES, H // 2], I32, head_at)
+        tab_w = [sb("tab_w%d" % a, [P, T], I32) for a in range(PASSES)]
         seg_sb = sb("seg_sb", [P, PACK], F32)
         bq_sb = sb("bq_sb", [P, PACK], F32)
 
-        nc.scalar.dma_start(tab_sc[two_pass_row0:P, :].bitcast(I32), tab_scales.rearrange("a q t -> q a t").bitcast(I32))
+        nc.scalar.dma_start(tab_sc[two_pass_row0:P, :].bitcast(I32), tab_scales.rearrange("a q t -> (a q) t").bitcast(I32))
         nc.scalar.dma_start(wq_raw[:], wq_words.rearrange("a p c -> p a c").bitcast(I32))
-        nc.sync.dma_start(wq_sc_raw[two_pass_row0:P, :].bitcast(I32), wq_scales.rearrange("a q c -> q a c").bitcast(I32))
+        nc.scalar.dma_start(bq_sb[:], bq.rearrange("(p t) -> p t", t=PACK))
         nc.sync.dma_start(idx[:], offs)
+        nc.sync.dma_start(wq_sc_raw[two_pass_row0:P, :].bitcast(I32), wq_scales.rearrange("a q c -> (a q) c").bitcast(I32))
         nc.sync.dma_start(idx2[:], offs2)
         nc.sync.dma_start(tab2_sc[one_pass_row0:P, :].bitcast(I32), tab2_scales[0].bitcast(I32))
-        nc.sync.dma_start(tab_w0[:], tab_words[0].rearrange("p t i -> p (t i)").bitcast(I32))
-        nc.gpsimd.dma_start(seg_sb[:], seg.rearrange("(p t) -> p t", t=PACK))
-        nc.gpsimd.dma_start(bq_sb[:], bq.rearrange("(p t) -> p t", t=PACK))
-        nc.gpsimd.dma_start(later_rows[one_pass_row0:P, S2:].bitcast(I32), ex_scales[0].bitcast(I32))
+        nc.sync.dma_start(tab_w[1][:, 0:EARLY], words_of(tab_words[1])[:, 0:EARLY])
+        nc.sync.dma_start(tab_w[0][:], words_of(tab_words[0]))
+        nc.sync.dma_start(seg_sb[:], seg.rearrange("(p t) -> p t", t=PACK))
+        nc.sync.dma_start(later_rows[one_pass_row0:P, S2:].bitcast(I32), ex_scales[0].bitcast(I32))
 
-        half_cols = HALF // LIST_ROWS
-        v_sc_g = sb_at("v_sc_g", [P, HALF], U8, gap_at - HALF // 2)
-        reorder(first_rows[:, HALF:], wq_sc_raw[:])
-        nc.vector.tensor_copy(v_sc_g[:], tab_sc[:].indirect(idx[:, 0:half_cols]))
-        nc.vector.tensor_copy(first_rows[:, 0:HALF].bitcast(I32), v_sc_g[:].bitcast(I32))
-        rows_a_quad = PASSES * ROWS
-        for quad in range(QUADS):
-            row0 = two_pass_row0 + rows_a_quad * quad
-            (nc.scalar if quad == 0 else nc.sync).dma_start(
-                scale_rows(first_sc, quad).bitcast(I32), first_rows[row0 : row0 + rows_a_quad, :].bitcast(I32)
-            )
-        tab_w1 = sb_at("tab_w1", [P, T], I32, 0)
-        nc.sync.dma_start(tab_w1[:], tab_words[1].rearrange("p t i -> p (t i)").bitcast(I32))
-        second_rows = sb("second_rows", [P, HALF], U8)
-        nc.vector.tensor_copy(second_rows[:], tab_sc[:].indirect(idx[:, half_cols:]))
-        for quad in range(QUADS):
-            row0 = two_pass_row0 + rows_a_quad * quad
-            nc.sync.dma_start(
-                scale_rows(second_sc, quad).bitcast(I32), second_rows[row0 : row0 + rows_a_quad, :].bitcast(I32)
-            )
-        tab2_w = sb_at("tab2_w", [P, T2], I32, tab2_at)
-        nc.sync.dma_start(tab2_w[:], tab2_words[0].rearrange("p t i -> p (t i)").bitcast(I32))
+        v_sc_g = sb_at("v_sc_g", [P, S], U8, head_at + H * PASSES * 2)
+        nc.vector.tensor_copy(v_sc_g[:], tab_sc[:].indirect(idx[:]))
+        reorder(first_rows[:, S:], wq_sc_raw[:])
+        nc.vector.tensor_copy(first_rows[:, 0:S].bitcast(I32), v_sc_g[:].bitcast(I32))
+        move_scale_rows(first_sc[0], first_rows, two_pass_row0)
+        nc.sync.dma_start(tab_w[1][:, EARLY:], words_of(tab_words[1])[:, EARLY:])
+        move_scale_rows(first_sc[1], first_rows, two_pass_row0 + BLOCKS)
 
-        ln_seg = sb("ln_seg", [P, PACK], F32, tag="first_rows")
+        v2_sc_g = sb_at("v2_sc_g", [P, S2], U8, head_at + H * PASSES * 2)
+        nc.vector.tensor_copy(v2_sc_g[:], tab2_sc[:].indirect(idx2[:]))
+        reorder(later_rows[:, 0:S2], v2_sc_g[:])
+        v2_sc = later_sc[:, 0:S2]
+        ex_sc = later_sc[:, S2:]
+        tab2_w = sb_at("tab2_w", [P, T2], I32, 0)
+        ev_sb = sb("ev_sb", [P, PACK, N], F32)
+        ex_w = sb("ex_w", [P, N], I32)
+        nc.sync.dma_start(tab2_w[:], words_of(tab2_words[0]))
+        move_scale_rows(later_sc, later_rows, one_pass_row0)
+        nc.sync.dma_start(ev_sb[:], ev.rearrange("(p t) n -> p t n", t=PACK))
+        nc.sync.dma_start(ex_w[:], words_of(ex_words[0]))
+
+        ln_seg = sb("ln_seg", [P, PACK], F32)
         nc.scalar.activation(ln_seg[:], seg_sb[:], ACT.Ln)
         warm = sb("warm", [P, 1], F32)
         nc.scalar.activation(warm[:], ln_seg[:, 0:1], ACT.Exp)
 
-        wq_w = sb("wq_w", [P, PASSES * H // 2], I32)
-        reorder_passes(wq_w[:].bitcast(U16), wq_raw[:].bitcast(U16))
-
-        def gather_half(words, window, half):
-            cols = HALF // LIST_ROWS
+        def gather(words, window, j0, width):
             nc.vector.tensor_copy(
-                words[:].bitcast(U32), window[:].bitcast(U32).indirect(idx[:, half * cols : (half + 1) * cols])
+                words[:].bitcast(U32),
+                window[:].bitcast(U32).indirect(idx[:, j0 // LIST_ROWS : (j0 + width) // LIST_ROWS]),
             )
 
-        v_w0 = []
-        for half in range(HALVES):
-            v_w0.append(sb("v_w0_%d" % half, [P, HALF], I32))
-            gather_half(v_w0[half], tab_w0, half)
+        v_w0 = [sb_at("v_w0_0", [P, GROUP], I32, head_at)] + [sb("v_w0_%d" % g, [P, GROUP], I32) for g in range(1, GROUPS)]
+        wq_w = sb("wq_w", [P, PASSES * H // 2], I32)
+        nc.vector.tensor_copy(
+            wq_w[:].bitcast(U16).rearrange("p (a t m) -> p a m t", a=PASSES, t=PACK),
+            wq_raw[:].bitcast(U16).rearrange("p a (m t) -> p a m t", t=PACK),
+        )
 
-        ev_at = tab2_at + 4 * T2
-        ex_at = ev_at + 4 * PACK * N
-        v2_sc_g = sb_at("v2_sc_g", [P, S2], U8, ex_at - S2 // 2)
-        nc.vector.tensor_copy(v2_sc_g[:], tab2_sc[:].indirect(idx2[:]))
-        reorder(later_rows[:, 0:S2], v2_sc_g[:])
-        for quad in range(QUADS):
-            row0 = one_pass_row0 + ROWS * quad
-            nc.sync.dma_start(scale_rows(later_sc, quad).bitcast(I32), later_rows[row0 : row0 + ROWS, :].bitcast(I32))
-        v2_sc = later_sc[:, 0:S2]
-        ex_sc = later_sc[:, S2:]
-        ev_sb = sb_at("ev_sb", [P, PACK, N], F32, ev_at)
-        nc.sync.dma_start(ev_sb[:], ev.rearrange("(p t) n -> p t n", t=PACK))
-        ex_w = sb_at("ex_w", [P, N], I32, ex_at)
-        nc.sync.dma_start(ex_w[:], ex_words[0].rearrange("p c i -> p (c i)").bitcast(I32))
-
-        plane_acc = [bank(b, [P, GROUP]) for b in range(SCALAR_GROUPS * PACK)]
-        h_acc = [None] * (STRIPS // HALVES)
+        h_acc = [
+            bank(b, [P, 2, GROUP] if b // 2 % 2 == 0 else [P, PACK, STRIP]) for b in range(2 * GROUPS)
+        ]
 
         def h_bank(b, a, words):
-            half_start = b * STRIP // HALF * HALF
-            for step in range(PACK):
-                if b // 2 < SCALAR_GROUPS:
-                    s, strip = divmod(step, 2)
-                    t, j0 = 2 * (b % 2) + s, (b // 2) * GROUP + strip * STRIP
-                    dst = plane_acc[2 * b + s][:, strip * STRIP : (strip + 1) * STRIP]
-                    first, last = strip == 0, strip == 1
-                else:
-                    t, j0 = step, b * STRIP
-                    dst = h_acc[b][:, step, :]
-                    first, last = step == 0, step == PACK - 1
+            g, u = divmod(b, 2)
+            steps = 2 if g % 2 == 0 else PACK
+            for step in range(steps):
+                t, j0, width = (2 * u + step, 0, GROUP) if g % 2 == 0 else (step, u * STRIP, STRIP)
                 col = a * H + t * P
-                v_sc = second_sc[:, a * HALF :] if half_start else first_sc[:, a * (HALF + H) :]
                 nc.tensor.matmul_mx(
-                    out=dst,
+                    out=h_acc[b][:, step, :],
                     lhsT=wq_w[:].bitcast(U8)[:, 2 * col : 2 * (col + P)].bitcast(FP4X4),
-                    lhsT_scale=first_sc[:, a * (HALF + H) + HALF + t * P : a * (HALF + H) + HALF + (t + 1) * P],
-                    rhs=words[:, j0 - half_start : j0 - half_start + STRIP].bitcast(FP8X4),
-                    rhs_scale=v_sc[:, j0 - half_start : j0 - half_start + STRIP],
-                    start=(a == 0 and first),
-                    stop=(a == PASSES - 1 and last),
+                    lhsT_scale=first_sc[a][:, S + t * P : S + (t + 1) * P],
+                    rhs=words[:, j0 : j0 + width].bitcast(FP8X4),
+                    rhs_scale=first_sc[a][:, g * GROUP + j0 : g * GROUP + j0 + width],
+                    start=(a == 0 and step == 0),
+                    stop=(a == PASSES - 1 and step == steps - 1),
                 )
 
-        for b in range(STRIPS // HALVES):
-            h_bank(b, 0, v_w0[0])
+        for g in range(GROUPS):
+            gather(v_w0[g], tab_w[0], g * GROUP, GROUP)
+            for u in range(2):
+                h_bank(2 * g + u, 0, v_w0[g])
 
-        v_w1 = [sb("v_w1_%d" % half, [P, HALF], I32) for half in range(HALVES)]
-        h_bf = [sb_at("h_bf%d" % g, [P, GROUP * PACK], BF16, tab2_at + 2 * g * GROUP * PACK) for g in range(GROUPS)]
-        h_w = [sb("h_w%d" % g, [P, GROUP], I32) for g in range(GROUPS)]
+        kib = 1024
+        v_w1 = [sb("v_w1_%d" % g, [P, GROUP], I32) for g in range(GROUPS)]
+        h_bf = {
+            0: sb("h_bf0", [P, GROUP * PACK], BF16),
+            (1, 0): sb_at("h_bf10", [P, STRIP * PACK], BF16, 0),
+            (1, 1): sb_at("h_bf11", [P, STRIP * PACK], BF16, kib),
+            2: sb_at("h_bf2", [P, GROUP * PACK], BF16, 4 * kib),
+            3: sb_at("h_bf3", [P, GROUP * PACK], BF16, 6 * kib),
+        }
+        h_w = [sb_at("h_w%d" % g, [P, GROUP], I32, (3 - g) * kib) if g < 2 else sb("h_w%d" % g, [P, GROUP], I32) for g in range(GROUPS)]
         h_sc = [sb("h_sc%d" % g, [P, GROUP], U8) for g in range(GROUPS)]
+        h_planes = {g: sb("h_planes%d" % g, [P, PACK, GROUP], BF16) for g in (0, 2)}
         act_planes = [sb("act_planes%d" % g, [P, PACK, GROUP], BF16) for g in range(GROUPS)]
         act_bf = [sb("act_bf%d" % half, [P, HALF * PACK], BF16) for half in range(HALVES)]
         act_w = sb("act_w", [P, S], I32)
         act_sc = sb("act_sc", [P, S], U8)
-        h_planes = [sb("h_planes%d" % g, [P, PACK, GROUP], BF16) for g in range(SCALAR_GROUPS)]
         v2_w = sb("v2_w", [P, S2], I32)
-        ev_bf = sb("ev_bf", [P, N * PACK], BF16)
+        ev_bf = sb_at("ev_bf", [P, N * PACK], BF16, 6 * kib)
         ev_w = sb("ev_w", [P, N], I32)
         ev_sc = sb("ev_sc", [P, N], U8)
 
@@ -214,37 +195,35 @@ def tile_list_memory_decoder_evidence_kernel(
                 dst.rearrange("p (c i t) -> p c t i", i=RUN, t=PACK), src.rearrange("p t (c i) -> p c t i", i=RUN)
             )
 
-        def add_bias(b, j0, j1):
-            g, u = divmod(b, 2)
+        def last_pass(g):
+            gather(v_w1[g], tab_w[1], g * GROUP, GROUP)
+            for u in range(2):
+                h_bank(2 * g + u, PASSES - 1, v_w1[g])
+
+        def bias_planes(g):
+            for t in range(PACK):
+                nc.scalar.activation(
+                    h_planes[g][:, t, :], h_acc[2 * g + t // 2][:, t % 2, :], ACT.Identity, bias=bq_sb[:, t : t + 1]
+                )
+
+        def bias_strip(dst, b):
             nc.vector.tensor_tensor(
-                h_bf[g][:, PACK * (u * STRIP + j0) : PACK * (u * STRIP + j1)].rearrange("p (j t) -> p j t", t=PACK),
-                h_acc[b][:, :, j0:j1].rearrange("p t j -> p j t"),
-                bq_sb[:].unsqueeze(1).to_broadcast([P, j1 - j0, PACK]),
+                dst.rearrange("p (j t) -> p j t", t=PACK),
+                h_acc[b][:].rearrange("p t j -> p j t"),
+                bq_sb[:].unsqueeze(1).to_broadcast([P, STRIP, PACK]),
                 ALU.add,
             )
 
-        def finish_h(b, width=STRIP):
-            if b >= STRIPS // HALVES:
-                h_acc.append(bank(b - STRIPS // HALVES, [P, PACK, STRIP]))
-                h_bank(b, 0, v_w0[1])
-            h_bank(b, PASSES - 1, v_w1[b * STRIP // HALF])
-            g, u = divmod(b, 2)
-            if g < SCALAR_GROUPS:
-                for s in range(2):
-                    t = 2 * u + s
-                    nc.scalar.activation(
-                        h_planes[g][:, t, :], plane_acc[2 * b + s][:], ACT.Identity, bias=bq_sb[:, t : t + 1]
-                    )
-            else:
-                add_bias(b, 0, width)
+        def quantize_h(g, src, j0, width):
+            nc.vector.quantize_mx(
+                out=h_w[g][:, j0 : j0 + width].bitcast(FP8X4), scales=h_sc[g][:, j0 : j0 + width], in_=src
+            )
 
         def scores(g):
-            nc.vector.quantize_mx(out=h_w[g][:].bitcast(FP8X4), scales=h_sc[g][:], in_=h_bf[g][:])
-            planes = 1 if g == 0 else 2
-            for u in range(PACK // planes):
-                e_acc = bank((4, 0, 4, 6)[g] + u, [P, planes, GROUP])
-                for s in range(planes):
-                    t = planes * u + s
+            for u in range(2):
+                e_acc = bank(2 * g + u, [P, 2, GROUP])
+                for s in range(2):
+                    t = 2 * u + s
                     nc.tensor.matmul_mx(
                         out=e_acc[:, s, :],
                         lhsT=v2_w[:, t * P : (t + 1) * P].bitcast(FP8X4),
@@ -254,16 +233,14 @@ def tile_list_memory_decoder_evidence_kernel(
                         start=True,
                         stop=True,
                     )
-                for s in range(planes):
-                    t = planes * u + s
-                    nc.scalar.activation(
-                        act_planes[g][:, t, :], e_acc[:, s, :], ACT.Exp, bias=ln_seg[:, t : t + 1]
-                    )
+                for s in range(2):
+                    t = 2 * u + s
+                    nc.scalar.activation(act_planes[g][:, t, :], e_acc[:, s, :], ACT.Exp, bias=ln_seg[:, t : t + 1])
 
-        def interleave_act(g):
+        def interleave_act(g, j0=0, j1=GROUP):
             half, u = divmod(g, 2)
-            dst = act_bf[half][:, u * GROUP * PACK : (u + 1) * GROUP * PACK]
-            interleave(nc.vector.tensor_copy, dst, act_planes[g][:])
+            dst = act_bf[half][:, (u * GROUP + j0) * PACK : (u * GROUP + j1) * PACK]
+            interleave(nc.vector.tensor_copy, dst, act_planes[g][:, :, j0:j1])
 
         def quantize_act(half):
             cols = slice(half * HALF, (half + 1) * HALF)
@@ -280,11 +257,9 @@ def tile_list_memory_decoder_evidence_kernel(
                 stop=True,
             )
 
-        inverses = []
-
-        def invert(tile):
+        def divide(tile):
             half, nt = divmod(tile, N_TILES)
-            den = bank(nt, [P, HALF])
+            den = bank(N_TILES + (nt + 2) % N_TILES, [P, HALF])
             mix(den, ex_w, ex_sc, nt, half)
             root = ring.tile([P, HALF], F32, name="root")
             nc.scalar.activation(root[:], den[:], ACT.Abs_reciprocal_sqrt)
@@ -293,35 +268,38 @@ def tile_list_memory_decoder_evidence_kernel(
                 nc.gpsimd.tensor_tensor(inverse[:], root[:], root[:], ALU.mult)
             else:
                 nc.scalar.activation(inverse[:], root[:], ACT.Square)
-            inverses.append(inverse)
-
-        def multiply(tile, step):
-            half, nt = divmod(tile, N_TILES)
-            num = bank(N_TILES + step % N_TILES, [P, HALF])
+            num = bank(nt, [P, HALF])
             mix(num, ev_w, ev_sc, nt, half)
             res = ring.tile([P, HALF], F32, name="res")
-            nc.vector.tensor_tensor(res[:], num[:], inverses[tile][:], ALU.mult)
+            nc.vector.tensor_tensor(res[:], num[:], inverse[:], ALU.mult)
             nc.sync.dma_start(out[nt * P : (nt + 1) * P, half * HALF : (half + 1) * HALF], res[:])
 
-        for half in range(HALVES):
-            gather_half(v_w1[half], tab_w1, half)
-        for b in range(2 * SCALAR_GROUPS):
-            finish_h(b)
+        last_pass(0)
+        bias_planes(0)
+        interleave(nc.scalar.copy, h_bf[0][:], h_planes[0][:])
+        last_pass(2)
+        last_pass(1)
+        bias_planes(2)
+        last_pass(3)
         nc.vector.tensor_copy(
             v2_w[:].bitcast(U32).rearrange("p (t m) -> p m t", t=PACK), tab2_w[:].bitcast(U32).indirect(idx2[:])
         )
-        interleave(nc.vector.tensor_copy, h_bf[0][:], h_planes[0][:])
-        finish_h(4, STRIP // 2)
+        quantize_h(0, h_bf[0][:], 0, GROUP)
         scores(0)
-        add_bias(4, STRIP // 2, STRIP)
-        interleave(nc.scalar.copy, h_bf[1][:], h_planes[1][:])
-        finish_h(5)
+        bias_strip(h_bf[1, 0][:], 2)
+        bias_strip(h_bf[1, 1][:], 3)
+        quantize_h(1, h_bf[1, 0][:], 0, STRIP)
+        quantize_h(1, h_bf[1, 1][:], STRIP, STRIP)
         scores(1)
-        finish_h(6)
+        interleave(nc.vector.tensor_copy, h_bf[2][:], h_planes[2][:])
+        bias_strip(h_bf[3][:, 0 : STRIP * PACK], 6)
+        quantize_h(2, h_bf[2][:], 0, GROUP)
         scores(2)
-        finish_h(7)
-        interleave_act(0)
+        bias_strip(h_bf[3][:, STRIP * PACK :], 7)
+        interleave_act(0, 0, STRIP)
+        quantize_h(3, h_bf[3][:], 0, GROUP)
         scores(3)
+        interleave_act(0, STRIP, GROUP)
         interleave_act(1)
         interleave(nc.vector.tensor_copy, ev_bf[:, 0 : PACK * GROUP], ev_sb[:, :, 0:GROUP])
         quantize_act(0)
@@ -330,7 +308,5 @@ def tile_list_memory_decoder_evidence_kernel(
         nc.vector.quantize_mx(out=ev_w[:].bitcast(FP8X4), scales=ev_sc[:], in_=ev_bf[:])
         interleave_act(3)
         quantize_act(1)
-        tiles = HALVES * N_TILES
-        for tile in range(tiles):
-            invert(tile)
-            multiply(tile, tile)
+        for tile in range(HALVES * N_TILES):
+            divide(tile)

@@ -33,6 +33,9 @@ GROUPS, HALVES = S // GROUP, S // HALF
 N_TILES = N // P
 
 EARLY = T // 4
+SCALAR_GROUPS = 2
+H_BANKS = ((0, 1, 6, 7), (2, 3), (4, 5), (6, 7))
+E_BANKS = ((0, 1, 2, 3), (0, 1), (4, 5), (6, 7))
 GPSIMD_TILES = (0, 2, 4, 6)
 
 
@@ -78,7 +81,8 @@ def tile_list_memory_decoder_evidence_kernel(
         tab2_sc = sb("tab2_sc", [P, T2], U8)
         first_rows = sb("first_rows", [P, S + H], U8)
         first_sc = [sb("first_sc%d" % a, [P, S + H], U8) for a in range(PASSES)]
-        later_rows = sb("later_rows", [P, S2 + N], U8)
+        later_wide = sb_at("later_wide", [P, 8 * 1024], U8, 0)
+        later_rows = later_wide[:, 0 : S2 + N]
         later_sc = sb("later_sc", [P, S2 + N], U8)
         nc.vector.memset(tab_sc[0:two_pass_row0, :].bitcast(I32), 0)
         nc.vector.memset(wq_sc_raw[0:two_pass_row0, :].bitcast(I32), 0)
@@ -118,7 +122,7 @@ def tile_list_memory_decoder_evidence_kernel(
         reorder(later_rows[:, 0:S2], v2_sc_g[:])
         v2_sc = later_sc[:, 0:S2]
         ex_sc = later_sc[:, S2:]
-        tab2_w = sb_at("tab2_w", [P, T2], I32, 0)
+        tab2_w = sb("tab2_w", [P, T2], I32)
         ev_sb = sb("ev_sb", [P, PACK, N], F32)
         ex_w = sb("ex_w", [P, N], I32)
         nc.sync.dma_start(tab2_w[:], words_of(tab2_words[0]))
@@ -144,43 +148,40 @@ def tile_list_memory_decoder_evidence_kernel(
             wq_raw[:].bitcast(U16).rearrange("p a (m t) -> p a m t", t=PACK),
         )
 
-        h_acc = [
-            bank(b, [P, 2, GROUP] if b // 2 % 2 == 0 else [P, PACK, STRIP]) for b in range(2 * GROUPS)
-        ]
+        h_acc = {}
 
-        def h_bank(b, a, words):
-            g, u = divmod(b, 2)
-            steps = 2 if g % 2 == 0 else PACK
-            for step in range(steps):
-                t, j0, width = (2 * u + step, 0, GROUP) if g % 2 == 0 else (step, u * STRIP, STRIP)
-                col = a * H + t * P
-                nc.tensor.matmul_mx(
-                    out=h_acc[b][:, step, :],
-                    lhsT=wq_w[:].bitcast(U8)[:, 2 * col : 2 * (col + P)].bitcast(FP4X4),
-                    lhsT_scale=first_sc[a][:, S + t * P : S + (t + 1) * P],
-                    rhs=words[:, j0 : j0 + width].bitcast(FP8X4),
-                    rhs_scale=first_sc[a][:, g * GROUP + j0 : g * GROUP + j0 + width],
-                    start=(a == 0 and step == 0),
-                    stop=(a == PASSES - 1 and step == steps - 1),
-                )
+        def h_pass(g, a, words):
+            banks = H_BANKS[g]
+            steps = PACK // len(banks) if g < SCALAR_GROUPS else PACK
+            for u, b in enumerate(banks):
+                if a == 0:
+                    h_acc[g, u] = bank(b, [P, steps, GROUP if g < SCALAR_GROUPS else STRIP])
+                for step in range(steps):
+                    t, j0, width = (steps * u + step, 0, GROUP) if g < SCALAR_GROUPS else (step, u * STRIP, STRIP)
+                    col = a * H + t * P
+                    nc.tensor.matmul_mx(
+                        out=h_acc[g, u][:, step, :],
+                        lhsT=wq_w[:].bitcast(U8)[:, 2 * col : 2 * (col + P)].bitcast(FP4X4),
+                        lhsT_scale=first_sc[a][:, S + t * P : S + (t + 1) * P],
+                        rhs=words[:, j0 : j0 + width].bitcast(FP8X4),
+                        rhs_scale=first_sc[a][:, g * GROUP + j0 : g * GROUP + j0 + width],
+                        start=(a == 0 and step == 0),
+                        stop=(a == PASSES - 1 and step == steps - 1),
+                    )
 
         for g in range(GROUPS):
             gather(v_w0[g], tab_w[0], g * GROUP, GROUP)
-            for u in range(2):
-                h_bank(2 * g + u, 0, v_w0[g])
+            if g < GROUPS - 1:
+                h_pass(g, 0, v_w0[g])
 
         kib = 1024
-        v_w1 = [sb("v_w1_%d" % g, [P, GROUP], I32) for g in range(GROUPS)]
-        h_bf = {
-            0: sb("h_bf0", [P, GROUP * PACK], BF16),
-            (1, 0): sb_at("h_bf10", [P, STRIP * PACK], BF16, 0),
-            (1, 1): sb_at("h_bf11", [P, STRIP * PACK], BF16, kib),
-            2: sb_at("h_bf2", [P, GROUP * PACK], BF16, 4 * kib),
-            3: sb_at("h_bf3", [P, GROUP * PACK], BF16, 6 * kib),
-        }
-        h_w = [sb_at("h_w%d" % g, [P, GROUP], I32, (3 - g) * kib) if g < 2 else sb("h_w%d" % g, [P, GROUP], I32) for g in range(GROUPS)]
+        v_w1 = [sb("v_w1_%d" % g, [P, GROUP], I32) for g in range(SCALAR_GROUPS)]
+        v_w1_rest = sb("v_w1_rest", [P, S - SCALAR_GROUPS * GROUP], I32)
+        h_bf = [sb("h_bf%d" % g, [P, GROUP * PACK], BF16) for g in range(SCALAR_GROUPS)]
+        h_bf = h_bf + [sb_at("h_bf%d" % g, [P, GROUP * PACK], BF16, 2 * g * kib) for g in range(SCALAR_GROUPS, GROUPS)]
+        h_w = [sb_at("h_w%d" % g, [P, GROUP], I32, g * kib) for g in range(GROUPS)]
         h_sc = [sb("h_sc%d" % g, [P, GROUP], U8) for g in range(GROUPS)]
-        h_planes = {g: sb("h_planes%d" % g, [P, PACK, GROUP], BF16) for g in (0, 2)}
+        h_planes = [sb("h_planes%d" % g, [P, PACK, GROUP], BF16) for g in range(SCALAR_GROUPS)]
         act_planes = [sb("act_planes%d" % g, [P, PACK, GROUP], BF16) for g in range(GROUPS)]
         act_bf = [sb("act_bf%d" % half, [P, HALF * PACK], BF16) for half in range(HALVES)]
         act_w = sb("act_w", [P, S], I32)
@@ -195,35 +196,33 @@ def tile_list_memory_decoder_evidence_kernel(
                 dst.rearrange("p (c i t) -> p c t i", i=RUN, t=PACK), src.rearrange("p t (c i) -> p c t i", i=RUN)
             )
 
-        def last_pass(g):
-            gather(v_w1[g], tab_w[1], g * GROUP, GROUP)
-            for u in range(2):
-                h_bank(2 * g + u, PASSES - 1, v_w1[g])
+        def last_pass(g, words):
+            if g == GROUPS - 1:
+                h_pass(g, 0, v_w0[g])
+            h_pass(g, PASSES - 1, words)
 
         def bias_planes(g):
+            planes = PACK // len(H_BANKS[g])
             for t in range(PACK):
                 nc.scalar.activation(
-                    h_planes[g][:, t, :], h_acc[2 * g + t // 2][:, t % 2, :], ACT.Identity, bias=bq_sb[:, t : t + 1]
+                    h_planes[g][:, t, :], h_acc[g, t // planes][:, t % planes, :], ACT.Identity, bias=bq_sb[:, t : t + 1]
                 )
 
-        def bias_strip(dst, b):
+        def bias_strip(g, u):
             nc.vector.tensor_tensor(
-                dst.rearrange("p (j t) -> p j t", t=PACK),
-                h_acc[b][:].rearrange("p t j -> p j t"),
+                h_bf[g][:, u * STRIP * PACK : (u + 1) * STRIP * PACK].rearrange("p (j t) -> p j t", t=PACK),
+                h_acc[g, u][:].rearrange("p t j -> p j t"),
                 bq_sb[:].unsqueeze(1).to_broadcast([P, STRIP, PACK]),
                 ALU.add,
             )
 
-        def quantize_h(g, src, j0, width):
-            nc.vector.quantize_mx(
-                out=h_w[g][:, j0 : j0 + width].bitcast(FP8X4), scales=h_sc[g][:, j0 : j0 + width], in_=src
-            )
-
         def scores(g):
-            for u in range(2):
-                e_acc = bank(2 * g + u, [P, 2, GROUP])
-                for s in range(2):
-                    t = 2 * u + s
+            nc.vector.quantize_mx(out=h_w[g][:].bitcast(FP8X4), scales=h_sc[g][:], in_=h_bf[g][:])
+            planes = PACK // len(E_BANKS[g])
+            for u, b in enumerate(E_BANKS[g]):
+                e_acc = bank(b, [P, planes, GROUP])
+                for s in range(planes):
+                    t = planes * u + s
                     nc.tensor.matmul_mx(
                         out=e_acc[:, s, :],
                         lhsT=v2_w[:, t * P : (t + 1) * P].bitcast(FP8X4),
@@ -233,8 +232,8 @@ def tile_list_memory_decoder_evidence_kernel(
                         start=True,
                         stop=True,
                     )
-                for s in range(2):
-                    t = 2 * u + s
+                for s in range(planes):
+                    t = planes * u + s
                     nc.scalar.activation(act_planes[g][:, t, :], e_acc[:, s, :], ACT.Exp, bias=ln_seg[:, t : t + 1])
 
         def interleave_act(g, j0=0, j1=GROUP):
@@ -242,9 +241,11 @@ def tile_list_memory_decoder_evidence_kernel(
             dst = act_bf[half][:, (u * GROUP + j0) * PACK : (u * GROUP + j1) * PACK]
             interleave(nc.vector.tensor_copy, dst, act_planes[g][:, :, j0:j1])
 
-        def quantize_act(half):
-            cols = slice(half * HALF, (half + 1) * HALF)
-            nc.vector.quantize_mx(out=act_w[:, cols].bitcast(FP8X4), scales=act_sc[:, cols], in_=act_bf[half][:])
+        def quantize_act(half, j0=0, j1=HALF):
+            cols = slice(half * HALF + j0, half * HALF + j1)
+            nc.vector.quantize_mx(
+                out=act_w[:, cols].bitcast(FP8X4), scales=act_sc[:, cols], in_=act_bf[half][:, j0 * PACK : j1 * PACK]
+            )
 
         def mix(acc, words, scales, nt, half):
             nc.tensor.matmul_mx(
@@ -274,35 +275,32 @@ def tile_list_memory_decoder_evidence_kernel(
             nc.vector.tensor_tensor(res[:], num[:], inverse[:], ALU.mult)
             nc.sync.dma_start(out[nt * P : (nt + 1) * P, half * HALF : (half + 1) * HALF], res[:])
 
-        last_pass(0)
-        bias_planes(0)
-        interleave(nc.scalar.copy, h_bf[0][:], h_planes[0][:])
-        last_pass(2)
-        last_pass(1)
-        bias_planes(2)
-        last_pass(3)
+        for g in range(SCALAR_GROUPS):
+            gather(v_w1[g], tab_w[1], g * GROUP, GROUP)
+            last_pass(g, v_w1[g])
+            bias_planes(g)
+        interleave(nc.scalar.copy, h_bf[1][:], h_planes[1][:])
+        gather(v_w1_rest, tab_w[1], SCALAR_GROUPS * GROUP, S - SCALAR_GROUPS * GROUP)
+        for g in range(SCALAR_GROUPS, GROUPS):
+            last_pass(g, v_w1_rest[:, (g - SCALAR_GROUPS) * GROUP : (g - SCALAR_GROUPS + 1) * GROUP])
+        interleave(nc.vector.tensor_copy, h_bf[0][:], h_planes[0][:])
         nc.vector.tensor_copy(
             v2_w[:].bitcast(U32).rearrange("p (t m) -> p m t", t=PACK), tab2_w[:].bitcast(U32).indirect(idx2[:])
         )
-        quantize_h(0, h_bf[0][:], 0, GROUP)
         scores(0)
-        bias_strip(h_bf[1, 0][:], 2)
-        bias_strip(h_bf[1, 1][:], 3)
-        quantize_h(1, h_bf[1, 0][:], 0, STRIP)
-        quantize_h(1, h_bf[1, 1][:], STRIP, STRIP)
+        bias_strip(2, 0)
         scores(1)
-        interleave(nc.vector.tensor_copy, h_bf[2][:], h_planes[2][:])
-        bias_strip(h_bf[3][:, 0 : STRIP * PACK], 6)
-        quantize_h(2, h_bf[2][:], 0, GROUP)
+        bias_strip(2, 1)
+        bias_strip(3, 0)
         scores(2)
-        bias_strip(h_bf[3][:, STRIP * PACK :], 7)
+        bias_strip(3, 1)
         interleave_act(0, 0, STRIP)
-        quantize_h(3, h_bf[3][:], 0, GROUP)
         scores(3)
         interleave_act(0, STRIP, GROUP)
         interleave_act(1)
+        quantize_act(0, 0, GROUP)
+        quantize_act(0, GROUP, HALF)
         interleave(nc.vector.tensor_copy, ev_bf[:, 0 : PACK * GROUP], ev_sb[:, :, 0:GROUP])
-        quantize_act(0)
         interleave(nc.vector.tensor_copy, ev_bf[:, PACK * GROUP :], ev_sb[:, :, GROUP:])
         interleave_act(2)
         nc.vector.quantize_mx(out=ev_w[:].bitcast(FP8X4), scales=ev_sc[:], in_=ev_bf[:])

@@ -279,11 +279,14 @@ def tile_list_memory_decoder_evidence_kernel(
             gather(v_w1[g], tab_w[1], g * GROUP, GROUP)
             last_pass(g, v_w1[g])
             bias_planes(g)
+        nc.gpsimd.tensor_scalar(
+            h_bf[0][:].rearrange("p (j t) -> p j t", t=PACK), h_planes[0][:].rearrange("p t j -> p j t"),
+            1.0, 0.0, ALU.mult, ALU.add,
+        )
         interleave(nc.scalar.copy, h_bf[1][:], h_planes[1][:])
         gather(v_w1_rest, tab_w[1], SCALAR_GROUPS * GROUP, S - SCALAR_GROUPS * GROUP)
         for g in range(SCALAR_GROUPS, GROUPS):
             last_pass(g, v_w1_rest[:, (g - SCALAR_GROUPS) * GROUP : (g - SCALAR_GROUPS + 1) * GROUP])
-        interleave(nc.vector.tensor_copy, h_bf[0][:], h_planes[0][:])
         nc.vector.tensor_copy(
             v2_w[:].bitcast(U32).rearrange("p (t m) -> p m t", t=PACK), tab2_w[:].bitcast(U32).indirect(idx2[:])
         )

@@ -32,11 +32,14 @@ HALF = 512
 GROUPS, HALVES = S // GROUP, S // HALF
 N_TILES = N // P
 
+KIB = 1024
+
 EARLY = T // 4
 SCALAR_GROUPS = 2
 H_BANKS = ((0, 1, 6, 7), (2, 3), (4, 5), (6, 7))
 E_BANKS = ((0, 1, 2, 3), (0, 1), (4, 5), (6, 7))
-GPSIMD_TILES = (0, 2, 4, 6)
+DEN_BANKS = (6, 7, 4, 5)
+GPSIMD_EVERY = 2
 
 
 def tile_list_memory_decoder_evidence_kernel(
@@ -81,7 +84,7 @@ def tile_list_memory_decoder_evidence_kernel(
         tab2_sc = sb("tab2_sc", [P, T2], U8)
         first_rows = sb("first_rows", [P, S + H], U8)
         first_sc = [sb("first_sc%d" % a, [P, S + H], U8) for a in range(PASSES)]
-        later_wide = sb_at("later_wide", [P, 8 * 1024], U8, 0)
+        later_wide = sb_at("later_wide", [P, 8 * KIB], U8, 0)
         later_rows = later_wide[:, 0 : S2 + N]
         later_sc = sb("later_sc", [P, S2 + N], U8)
         nc.vector.memset(tab_sc[0:two_pass_row0, :].bitcast(I32), 0)
@@ -91,8 +94,9 @@ def tile_list_memory_decoder_evidence_kernel(
         nc.gpsimd.memset(tab2_sc[0:one_pass_row0, :].bitcast(I32), 0)
         nc.gpsimd.memset(later_sc[:].bitcast(I32), 0)
 
-        head_at = 16 * 1024
-        wq_raw = sb_at("wq_raw", [P, PASSES, H // 2], I32, head_at)
+        wq_at = 16 * KIB
+        gathered_sc_at = wq_at + 2 * PASSES * H
+        wq_raw = sb_at("wq_raw", [P, PASSES, H // 2], I32, wq_at)
         tab_w = [sb("tab_w%d" % a, [P, T], I32) for a in range(PASSES)]
         seg_sb = sb("seg_sb", [P, PACK], F32)
         bq_sb = sb("bq_sb", [P, PACK], F32)
@@ -109,7 +113,7 @@ def tile_list_memory_decoder_evidence_kernel(
         nc.sync.dma_start(seg_sb[:], seg.rearrange("(p t) -> p t", t=PACK))
         nc.sync.dma_start(later_rows[one_pass_row0:P, S2:].bitcast(I32), ex_scales[0].bitcast(I32))
 
-        v_sc_g = sb_at("v_sc_g", [P, S], U8, head_at + H * PASSES * 2)
+        v_sc_g = sb_at("v_sc_g", [P, S], U8, gathered_sc_at)
         nc.vector.tensor_copy(v_sc_g[:], tab_sc[:].indirect(idx[:]))
         reorder(first_rows[:, S:], wq_sc_raw[:])
         nc.vector.tensor_copy(first_rows[:, 0:S].bitcast(I32), v_sc_g[:].bitcast(I32))
@@ -117,7 +121,7 @@ def tile_list_memory_decoder_evidence_kernel(
         nc.sync.dma_start(tab_w[1][:, EARLY:], words_of(tab_words[1])[:, EARLY:])
         move_scale_rows(first_sc[1], first_rows, two_pass_row0 + BLOCKS)
 
-        v2_sc_g = sb_at("v2_sc_g", [P, S2], U8, head_at + H * PASSES * 2)
+        v2_sc_g = sb_at("v2_sc_g", [P, S2], U8, gathered_sc_at)
         nc.vector.tensor_copy(v2_sc_g[:], tab2_sc[:].indirect(idx2[:]))
         reorder(later_rows[:, 0:S2], v2_sc_g[:])
         v2_sc = later_sc[:, 0:S2]
@@ -141,7 +145,8 @@ def tile_list_memory_decoder_evidence_kernel(
                 window[:].bitcast(U32).indirect(idx[:, j0 // LIST_ROWS : (j0 + width) // LIST_ROWS]),
             )
 
-        v_w0 = [sb_at("v_w0_0", [P, GROUP], I32, head_at)] + [sb("v_w0_%d" % g, [P, GROUP], I32) for g in range(1, GROUPS)]
+        v_w0 = [sb_at("v_w0_0", [P, GROUP], I32, wq_at)]
+        v_w0 = v_w0 + [sb("v_w0_%d" % g, [P, GROUP], I32) for g in range(1, GROUPS)]
         wq_w = sb("wq_w", [P, PASSES * H // 2], I32)
         nc.vector.tensor_copy(
             wq_w[:].bitcast(U16).rearrange("p (a t m) -> p a m t", a=PASSES, t=PACK),
@@ -174,12 +179,11 @@ def tile_list_memory_decoder_evidence_kernel(
             if g < GROUPS - 1:
                 h_pass(g, 0, v_w0[g])
 
-        kib = 1024
         v_w1 = [sb("v_w1_%d" % g, [P, GROUP], I32) for g in range(SCALAR_GROUPS)]
         v_w1_rest = sb("v_w1_rest", [P, S - SCALAR_GROUPS * GROUP], I32)
         h_bf = [sb("h_bf%d" % g, [P, GROUP * PACK], BF16) for g in range(SCALAR_GROUPS)]
-        h_bf = h_bf + [sb_at("h_bf%d" % g, [P, GROUP * PACK], BF16, 2 * g * kib) for g in range(SCALAR_GROUPS, GROUPS)]
-        h_w = [sb_at("h_w%d" % g, [P, GROUP], I32, g * kib) for g in range(GROUPS)]
+        h_bf = h_bf + [sb_at("h_bf%d" % g, [P, GROUP * PACK], BF16, 2 * g * KIB) for g in range(SCALAR_GROUPS, GROUPS)]
+        h_w = [sb_at("h_w%d" % g, [P, GROUP], I32, g * KIB) for g in range(GROUPS)]
         h_sc = [sb("h_sc%d" % g, [P, GROUP], U8) for g in range(GROUPS)]
         h_planes = [sb("h_planes%d" % g, [P, PACK, GROUP], BF16) for g in range(SCALAR_GROUPS)]
         act_planes = [sb("act_planes%d" % g, [P, PACK, GROUP], BF16) for g in range(GROUPS)]
@@ -187,7 +191,7 @@ def tile_list_memory_decoder_evidence_kernel(
         act_w = sb("act_w", [P, S], I32)
         act_sc = sb("act_sc", [P, S], U8)
         v2_w = sb("v2_w", [P, S2], I32)
-        ev_bf = sb_at("ev_bf", [P, N * PACK], BF16, 6 * kib)
+        ev_bf = sb_at("ev_bf", [P, N * PACK], BF16, 2 * (GROUPS - 1) * KIB)
         ev_w = sb("ev_w", [P, N], I32)
         ev_sc = sb("ev_sc", [P, N], U8)
 
@@ -260,12 +264,12 @@ def tile_list_memory_decoder_evidence_kernel(
 
         def divide(tile):
             half, nt = divmod(tile, N_TILES)
-            den = bank(N_TILES + (nt + 2) % N_TILES, [P, HALF])
+            den = bank(DEN_BANKS[nt], [P, HALF])
             mix(den, ex_w, ex_sc, nt, half)
             root = ring.tile([P, HALF], F32, name="root")
             nc.scalar.activation(root[:], den[:], ACT.Abs_reciprocal_sqrt)
             inverse = ring.tile([P, HALF], F32, name="inverse")
-            if tile in GPSIMD_TILES:
+            if tile % GPSIMD_EVERY == 0:
                 nc.gpsimd.tensor_tensor(inverse[:], root[:], root[:], ALU.mult)
             else:
                 nc.scalar.activation(inverse[:], root[:], ACT.Square)
@@ -280,13 +284,15 @@ def tile_list_memory_decoder_evidence_kernel(
             last_pass(g, v_w1[g])
             bias_planes(g)
         nc.gpsimd.tensor_scalar(
-            h_bf[0][:].rearrange("p (j t) -> p j t", t=PACK), h_planes[0][:].rearrange("p t j -> p j t"),
+            h_bf[0][:, 0 : STRIP * PACK].rearrange("p (j t) -> p j t", t=PACK),
+            h_planes[0][:, :, 0:STRIP].rearrange("p t j -> p j t"),
             1.0, 0.0, ALU.mult, ALU.add,
         )
         interleave(nc.scalar.copy, h_bf[1][:], h_planes[1][:])
         gather(v_w1_rest, tab_w[1], SCALAR_GROUPS * GROUP, S - SCALAR_GROUPS * GROUP)
         for g in range(SCALAR_GROUPS, GROUPS):
             last_pass(g, v_w1_rest[:, (g - SCALAR_GROUPS) * GROUP : (g - SCALAR_GROUPS + 1) * GROUP])
+        interleave(nc.vector.tensor_copy, h_bf[0][:, STRIP * PACK :], h_planes[0][:, :, STRIP:])
         nc.vector.tensor_copy(
             v2_w[:].bitcast(U32).rearrange("p (t m) -> p m t", t=PACK), tab2_w[:].bitcast(U32).indirect(idx2[:])
         )

@@ -283,23 +283,22 @@ def tile_list_memory_decoder_evidence_kernel(
             gather(v_w1[g], tab_w[1], g * GROUP, GROUP)
             last_pass(g, v_w1[g])
             bias_planes(g)
-        nc.gpsimd.tensor_scalar(
-            h_bf[0][:, 0 : STRIP * PACK].rearrange("p (j t) -> p j t", t=PACK),
-            h_planes[0][:, :, 0:STRIP].rearrange("p t j -> p j t"),
-            1.0, 0.0, ALU.mult, ALU.add,
-        )
-        interleave(nc.scalar.copy, h_bf[1][:], h_planes[1][:])
+            nc.gpsimd.tensor_scalar(
+                h_bf[g][:, 0 : STRIP * PACK].rearrange("p (j t) -> p j t", t=PACK),
+                h_planes[g][:, :, 0:STRIP].rearrange("p t j -> p j t"),
+                1.0, 0.0, ALU.mult, ALU.add,
+            )
+            interleave(nc.scalar.copy, h_bf[g][:, STRIP * PACK :], h_planes[g][:, :, STRIP:])
         gather(v_w1_rest, tab_w[1], SCALAR_GROUPS * GROUP, S - SCALAR_GROUPS * GROUP)
         for g in range(SCALAR_GROUPS, GROUPS):
             last_pass(g, v_w1_rest[:, (g - SCALAR_GROUPS) * GROUP : (g - SCALAR_GROUPS + 1) * GROUP])
-        interleave(nc.vector.tensor_copy, h_bf[0][:, STRIP * PACK :], h_planes[0][:, :, STRIP:])
         nc.vector.tensor_copy(
             v2_w[:].bitcast(U32).rearrange("p (t m) -> p m t", t=PACK), tab2_w[:].bitcast(U32).indirect(idx2[:])
         )
         scores(0)
         bias_strip(2, 0)
-        scores(1)
         bias_strip(2, 1)
+        scores(1)
         bias_strip(3, 0)
         scores(2)
         bias_strip(3, 1)

@@ -38,7 +38,7 @@ EARLY = T // 4
 SCALAR_GROUPS = 2
 H_BANKS = ((0, 1, 6, 7), (2, 3), (4, 5), (6, 7))
 E_BANKS = ((0, 1, 2, 3), (0, 1), (4, 5), (6, 7))
-DEN_BANKS = (6, 7, 4, 5)
+DEN_BANKS = (7, 6, 4, 5)
 GPSIMD_EVERY = 2
 
 
@@ -158,7 +158,8 @@ def tile_list_memory_decoder_evidence_kernel(
         def h_pass(g, a, words):
             banks = H_BANKS[g]
             steps = PACK // len(banks) if g < SCALAR_GROUPS else PACK
-            for u, b in enumerate(banks):
+            order = list(enumerate(banks))
+            for u, b in reversed(order) if 0 < g < SCALAR_GROUPS else order:
                 if a == 0:
                     h_acc[g, u] = bank(b, [P, steps, GROUP if g < SCALAR_GROUPS else STRIP])
                 for step in range(steps):
@@ -223,12 +224,14 @@ def tile_list_memory_decoder_evidence_kernel(
         def scores(g):
             nc.vector.quantize_mx(out=h_w[g][:].bitcast(FP8X4), scales=h_sc[g][:], in_=h_bf[g][:])
             planes = PACK // len(E_BANKS[g])
-            for u, b in enumerate(E_BANKS[g]):
-                e_acc = bank(b, [P, planes, GROUP])
+            e_acc = {}
+            order = list(enumerate(E_BANKS[g]))
+            for u, b in reversed(order) if g >= SCALAR_GROUPS else order:
+                e_acc[u] = bank(b, [P, planes, GROUP])
                 for s in range(planes):
                     t = planes * u + s
                     nc.tensor.matmul_mx(
-                        out=e_acc[:, s, :],
+                        out=e_acc[u][:, s, :],
                         lhsT=v2_w[:, t * P : (t + 1) * P].bitcast(FP8X4),
                         lhsT_scale=v2_sc[:, t * P : (t + 1) * P],
                         rhs=h_w[g][:].bitcast(FP8X4),
@@ -236,9 +239,10 @@ def tile_list_memory_decoder_evidence_kernel(
                         start=True,
                         stop=True,
                     )
-                for s in range(planes):
-                    t = planes * u + s
-                    nc.scalar.activation(act_planes[g][:, t, :], e_acc[:, s, :], ACT.Exp, bias=ln_seg[:, t : t + 1])
+            for t in range(PACK):
+                nc.scalar.activation(
+                    act_planes[g][:, t, :], e_acc[t // planes][:, t % planes, :], ACT.Exp, bias=ln_seg[:, t : t + 1]
+                )
 
         def interleave_act(g, j0=0, j1=GROUP):
             half, u = divmod(g, 2)
@@ -262,10 +266,16 @@ def tile_list_memory_decoder_evidence_kernel(
                 stop=True,
             )
 
+        dens = {}
+
+        def exposure(tile):
+            half, nt = divmod(tile, N_TILES)
+            dens[tile] = bank(DEN_BANKS[nt], [P, HALF])
+            mix(dens[tile], ex_w, ex_sc, nt, half)
+
         def divide(tile):
             half, nt = divmod(tile, N_TILES)
-            den = bank(DEN_BANKS[nt], [P, HALF])
-            mix(den, ex_w, ex_sc, nt, half)
+            den = dens[tile]
             root = ring.tile([P, HALF], F32, name="root")
             nc.scalar.activation(root[:], den[:], ACT.Abs_reciprocal_sqrt)
             inverse = ring.tile([P, HALF], F32, name="inverse")
@@ -314,5 +324,8 @@ def tile_list_memory_decoder_evidence_kernel(
         nc.vector.quantize_mx(out=ev_w[:].bitcast(FP8X4), scales=ev_sc[:], in_=ev_bf[:])
         interleave_act(3)
         quantize_act(1)
-        for tile in range(HALVES * N_TILES):
-            divide(tile)
+        for run in (range(0, N_TILES), range(N_TILES, 2 * N_TILES - 1), range(2 * N_TILES - 1, 2 * N_TILES)):
+            for tile in reversed(run):
+                exposure(tile)
+            for tile in run:
+                divide(tile)

@@ -77,35 +77,38 @@ def tile_list_memory_decoder_evidence_kernel(
         idx = keep.tile([P, S // LIST_ROWS], U16, name="idx")
         idx2 = keep.tile([P, S2 // LIST_ROWS], U16, name="idx2")
 
-        two_pass_row0 = P - PASSES * BLOCKS
+        tab_row0 = P - PASSES * BLOCKS
         one_pass_row0 = P - BLOCKS
         tab_sc = sb("tab_sc", [P, T], U8)
-        wq_sc_raw = sb("wq_sc_raw", [P, H], U8)
         tab2_sc = sb("tab2_sc", [P, T2], U8)
-        first_rows = sb("first_rows", [P, S + H], U8)
-        first_sc = [sb("first_sc%d" % a, [P, S + H], U8) for a in range(PASSES)]
+        v_sc = sb("v_sc", [P, PASSES, S], U8)
+        wq_sc_rows = sb("wq_sc_rows", [ROWS, PASSES * QUADS * H], U8)
+        wq_sc_raw = sb("wq_sc_raw", [P, PASSES * H], U8)
+        wq_sc = sb("wq_sc", [P, PASSES * H], U8)
         later_wide = sb_at("later_wide", [P, 8 * KIB], U8, 0)
         later_rows = later_wide[:, 0 : S2 + N]
         later_sc = sb("later_sc", [P, S2 + N], U8)
-        nc.vector.memset(tab_sc[0:two_pass_row0, :].bitcast(I32), 0)
-        nc.vector.memset(wq_sc_raw[0:two_pass_row0, :].bitcast(I32), 0)
-        nc.vector.memset(first_sc[0][:].bitcast(I32), 0)
-        nc.gpsimd.memset(first_sc[1][:].bitcast(I32), 0)
+        nc.vector.memset(tab_sc[0:tab_row0, :].bitcast(I32), 0)
+        nc.vector.memset(wq_sc_raw[:].bitcast(I32), 0)
+        nc.gpsimd.memset(v_sc[:].rearrange("p a s -> p (a s)").bitcast(I32), 0)
         nc.gpsimd.memset(tab2_sc[0:one_pass_row0, :].bitcast(I32), 0)
         nc.gpsimd.memset(later_sc[:].bitcast(I32), 0)
 
         wq_at = 16 * KIB
-        gathered_sc_at = wq_at + 2 * PASSES * H
+        seg_at = wq_at + 2 * PASSES * H
         wq_raw = sb_at("wq_raw", [P, PASSES, H // 2], I32, wq_at)
         tab_w = [sb("tab_w%d" % a, [P, T], I32) for a in range(PASSES)]
-        seg_sb = sb("seg_sb", [P, PACK], F32)
+        seg_sb = sb_at("seg_sb", [P, PACK], F32, seg_at)
         bq_sb = sb("bq_sb", [P, PACK], F32)
 
-        nc.scalar.dma_start(tab_sc[two_pass_row0:P, :].bitcast(I32), tab_scales.rearrange("a q t -> (a q) t").bitcast(I32))
+        nc.scalar.dma_start(tab_sc[tab_row0:P, :].bitcast(I32), tab_scales.rearrange("a q t -> q a t").bitcast(I32))
         nc.scalar.dma_start(wq_raw[:], wq_words.rearrange("a p c -> p a c").bitcast(I32))
         nc.scalar.dma_start(bq_sb[:], bq.rearrange("(p t) -> p t", t=PACK))
         nc.sync.dma_start(idx[:], offs)
-        nc.sync.dma_start(wq_sc_raw[two_pass_row0:P, :].bitcast(I32), wq_scales.rearrange("a q c -> (a q) c").bitcast(I32))
+        nc.sync.dma_start(
+            wq_sc_rows[:].bitcast(I32).rearrange("i (b c) -> i b c", b=PASSES * QUADS),
+            wq_scales.rearrange("a (q i) c -> i (a q) c", i=ROWS).bitcast(I32),
+        )
         nc.sync.dma_start(idx2[:], offs2)
         nc.sync.dma_start(tab2_sc[one_pass_row0:P, :].bitcast(I32), tab2_scales[0].bitcast(I32))
         nc.sync.dma_start(tab_w[1][:, 0:EARLY], words_of(tab_words[1])[:, 0:EARLY])
@@ -113,15 +116,25 @@ def tile_list_memory_decoder_evidence_kernel(
         nc.sync.dma_start(seg_sb[:], seg.rearrange("(p t) -> p t", t=PACK))
         nc.sync.dma_start(later_rows[one_pass_row0:P, S2:].bitcast(I32), ex_scales[0].bitcast(I32))
 
-        v_sc_g = sb_at("v_sc_g", [P, S], U8, gathered_sc_at)
+        v_sc_g = sb("v_sc_g", [P, S], U8)
         nc.vector.tensor_copy(v_sc_g[:], tab_sc[:].indirect(idx[:]))
-        reorder(first_rows[:, S:], wq_sc_raw[:])
-        nc.vector.tensor_copy(first_rows[:, 0:S].bitcast(I32), v_sc_g[:].bitcast(I32))
-        move_scale_rows(first_sc[0], first_rows, two_pass_row0)
+        for q in (0, 2, 1, 3):
+            row0 = tab_row0 + q * PASSES * ROWS
+            nc.sync.dma_start(
+                v_sc[q * QUAD : q * QUAD + ROWS].bitcast(I32), v_sc_g[row0 : row0 + PASSES * ROWS, :].bitcast(I32)
+            )
         nc.sync.dma_start(tab_w[1][:, EARLY:], words_of(tab_words[1])[:, EARLY:])
-        move_scale_rows(first_sc[1], first_rows, two_pass_row0 + BLOCKS)
 
-        v2_sc_g = sb_at("v2_sc_g", [P, S2], U8, gathered_sc_at)
+        blocks = wq_sc_rows[:].bitcast(I32).rearrange("i (a q c) -> i a q c", a=PASSES, q=QUADS)
+        for q in range(QUADS):
+            nc.vector.tensor_copy(
+                wq_sc_raw[q * QUAD : q * QUAD + ROWS, :].bitcast(I32).rearrange("i (a c) -> i a c", a=PASSES),
+                blocks[:, :, q, :],
+            )
+        for a in range(PASSES):
+            reorder(wq_sc[:, a * H : (a + 1) * H], wq_sc_raw[:, a * H : (a + 1) * H])
+
+        v2_sc_g = sb("v2_sc_g", [P, S2], U8)
         nc.vector.tensor_copy(v2_sc_g[:], tab2_sc[:].indirect(idx2[:]))
         reorder(later_rows[:, 0:S2], v2_sc_g[:])
         v2_sc = later_sc[:, 0:S2]
@@ -136,8 +149,10 @@ def tile_list_memory_decoder_evidence_kernel(
 
         ln_seg = sb("ln_seg", [P, PACK], F32)
         nc.scalar.activation(ln_seg[:], seg_sb[:], ACT.Ln)
-        warm = sb("warm", [P, 1], F32)
-        nc.scalar.activation(warm[:], ln_seg[:, 0:1], ACT.Exp)
+        warm_in = sb("warm_in", [P, 1], F32)
+        nc.gpsimd.memset(warm_in[:], 0.0)
+        warm = sb_at("warm", [P, 1], F32, seg_at)
+        nc.scalar.activation(warm[:], warm_in[:], ACT.Exp)
 
         def gather(words, window, j0, width):
             nc.vector.tensor_copy(
@@ -168,9 +183,9 @@ def tile_list_memory_decoder_evidence_kernel(
                     nc.tensor.matmul_mx(
                         out=h_acc[g, u][:, step, :],
                         lhsT=wq_w[:].bitcast(U8)[:, 2 * col : 2 * (col + P)].bitcast(FP4X4),
-                        lhsT_scale=first_sc[a][:, S + t * P : S + (t + 1) * P],
+                        lhsT_scale=wq_sc[:, col : col + P],
                         rhs=words[:, j0 : j0 + width].bitcast(FP8X4),
-                        rhs_scale=first_sc[a][:, g * GROUP + j0 : g * GROUP + j0 + width],
+                        rhs_scale=v_sc[:, a, g * GROUP + j0 : g * GROUP + j0 + width],
                         start=(a == 0 and step == 0),
                         stop=(a == PASSES - 1 and step == steps - 1),
                     )

@@ -25,6 +25,7 @@ BLOCKS = QUADS * ROWS
 PASSES = K // (P * PACK)
 LIST_ROWS = 16
 RUN = 4
+PAIR = 2
 
 STRIP = 128
 GROUP = 256
@@ -34,7 +35,8 @@ N_TILES = N // P
 
 KIB = 1024
 
-EARLY = T // 4
+EARLY = T // 8
+
 SCALAR_GROUPS = 2
 H_BANKS = ((0, 1, 6, 7), (2, 3), (4, 5), (6, 7))
 E_BANKS = ((0, 1, 2, 3), (0, 1), (4, 5), (6, 7))
@@ -103,7 +105,6 @@ def tile_list_memory_decoder_evidence_kernel(
 
         nc.scalar.dma_start(tab_sc[tab_row0:P, :].bitcast(I32), tab_scales.rearrange("a q t -> q a t").bitcast(I32))
         nc.scalar.dma_start(wq_raw[:], wq_words.rearrange("a p c -> p a c").bitcast(I32))
-        nc.scalar.dma_start(bq_sb[:], bq.rearrange("(p t) -> p t", t=PACK))
         nc.sync.dma_start(idx[:], offs)
         nc.sync.dma_start(
             wq_sc_rows[:].bitcast(I32).rearrange("i (b c) -> i b c", b=PASSES * QUADS),
@@ -114,7 +115,7 @@ def tile_list_memory_decoder_evidence_kernel(
         nc.sync.dma_start(tab_w[1][:, 0:EARLY], words_of(tab_words[1])[:, 0:EARLY])
         nc.sync.dma_start(tab_w[0][:], words_of(tab_words[0]))
         nc.sync.dma_start(seg_sb[:], seg.rearrange("(p t) -> p t", t=PACK))
-        nc.sync.dma_start(later_rows[one_pass_row0:P, S2:].bitcast(I32), ex_scales[0].bitcast(I32))
+        nc.sync.dma_start(bq_sb[:], bq.rearrange("(p t) -> p t", t=PACK))
 
         v_sc_g = sb("v_sc_g", [P, S], U8)
         nc.vector.tensor_copy(v_sc_g[:], tab_sc[:].indirect(idx[:]))
@@ -124,6 +125,7 @@ def tile_list_memory_decoder_evidence_kernel(
                 v_sc[q * QUAD : q * QUAD + ROWS].bitcast(I32), v_sc_g[row0 : row0 + PASSES * ROWS, :].bitcast(I32)
             )
         nc.sync.dma_start(tab_w[1][:, EARLY:], words_of(tab_words[1])[:, EARLY:])
+        nc.sync.dma_start(later_rows[one_pass_row0:P, S2:].bitcast(I32), ex_scales[0].bitcast(I32))
 
         blocks = wq_sc_rows[:].bitcast(I32).rearrange("i (a q c) -> i a q c", a=PASSES, q=QUADS)
         for q in range(QUADS):
@@ -228,11 +230,13 @@ def tile_list_memory_decoder_evidence_kernel(
                     h_planes[g][:, t, :], h_acc[g, t // planes][:, t % planes, :], ACT.Identity, bias=bq_sb[:, t : t + 1]
                 )
 
-        def bias_strip(g, u):
+        def bias_strip(g, u, j0=0, j1=STRIP):
             nc.vector.tensor_tensor(
-                h_bf[g][:, u * STRIP * PACK : (u + 1) * STRIP * PACK].rearrange("p (j t) -> p j t", t=PACK),
-                h_acc[g, u][:].rearrange("p t j -> p j t"),
-                bq_sb[:].unsqueeze(1).to_broadcast([P, STRIP, PACK]),
+                h_bf[g][:, (u * STRIP + j0) * PACK : (u * STRIP + j1) * PACK].rearrange(
+                    "p (c i t) -> p c t i", i=PAIR, t=PACK
+                ),
+                h_acc[g, u][:, :, j0:j1].rearrange("p t (c i) -> p c t i", i=PAIR),
+                bq_sb[:].unsqueeze(1).unsqueeze(3).to_broadcast([P, (j1 - j0) // PAIR, PACK, PAIR]),
                 ALU.add,
             )
 
@@ -322,8 +326,9 @@ def tile_list_memory_decoder_evidence_kernel(
         )
         scores(0)
         bias_strip(2, 0)
-        bias_strip(2, 1)
+        bias_strip(2, 1, 0, STRIP // 2)
         scores(1)
+        bias_strip(2, 1, STRIP // 2, STRIP)
         bias_strip(3, 0)
         scores(2)
         bias_strip(3, 1)
@@ -338,7 +343,8 @@ def tile_list_memory_decoder_evidence_kernel(
         interleave_act(2)
         nc.vector.quantize_mx(out=ev_w[:].bitcast(FP8X4), scales=ev_sc[:], in_=ev_bf[:])
         interleave_act(3)
-        quantize_act(1)
+        quantize_act(1, 0, GROUP)
+        quantize_act(1, GROUP, HALF)
         for run in (range(0, N_TILES), range(N_TILES, 2 * N_TILES - 1), range(2 * N_TILES - 1, 2 * N_TILES)):
             for tile in reversed(run):
                 exposure(tile)

@@ -43,6 +43,8 @@ E_BANKS = ((0, 1, 2, 3), (0, 1), (4, 5), (6, 7))
 DEN_BANKS = (7, 6, 4, 5)
 GPSIMD_EVERY = 2
 
+VECTOR_TILE = 1
+
 
 def tile_list_memory_decoder_evidence_kernel(
     tc, tab_words, tab_scales, tab2_words, tab2_scales, wq_words, wq_scales,
@@ -300,6 +302,9 @@ def tile_list_memory_decoder_evidence_kernel(
             inverse = ring.tile([P, HALF], F32, name="inverse")
             if tile % GPSIMD_EVERY == 0:
                 nc.gpsimd.tensor_tensor(inverse[:], root[:], root[:], ALU.mult)
+            elif tile == VECTOR_TILE:
+                twice = root[:].unsqueeze(2).to_broadcast([P, HALF, 2])
+                nc.vector.tensor_reduce(inverse[:], twice, mybir.AxisListType.X, ALU.mult)
             else:
                 nc.scalar.activation(inverse[:], root[:], ACT.Square)
             num = bank(nt, [P, HALF])

@@ -43,7 +43,7 @@ E_BANKS = ((0, 1, 2, 3), (0, 1), (4, 5), (6, 7))
 DEN_BANKS = (7, 6, 4, 5)
 GPSIMD_EVERY = 2
 
-VECTOR_TILE = 1
+VECTOR_TILE, VECTOR_SHARE = 1, HALF // 2
 
 
 def tile_list_memory_decoder_evidence_kernel(
@@ -303,8 +303,9 @@ def tile_list_memory_decoder_evidence_kernel(
             if tile % GPSIMD_EVERY == 0:
                 nc.gpsimd.tensor_tensor(inverse[:], root[:], root[:], ALU.mult)
             elif tile == VECTOR_TILE:
-                twice = root[:].unsqueeze(2).to_broadcast([P, HALF, 2])
-                nc.vector.tensor_reduce(inverse[:], twice, mybir.AxisListType.X, ALU.mult)
+                twice = root[:, 0:VECTOR_SHARE].unsqueeze(2).to_broadcast([P, VECTOR_SHARE, 2])
+                nc.vector.tensor_reduce(inverse[:, 0:VECTOR_SHARE], twice, mybir.AxisListType.X, ALU.mult)
+                nc.scalar.activation(inverse[:, VECTOR_SHARE:], root[:, VECTOR_SHARE:], ACT.Square)
             else:
                 nc.scalar.activation(inverse[:], root[:], ACT.Square)
             num = bank(nt, [P, HALF])

@@ -44,6 +44,8 @@ DEN_BANKS = (7, 6, 4, 5)
 GPSIMD_EVERY = 2
 
 VECTOR_TILE, VECTOR_SHARE = 1, HALF // 2
+LAST = HALVES * N_TILES - 1
+GPSIMD_LAST_SHARE = 5 * HALF // 8
 
 
 def tile_list_memory_decoder_evidence_kernel(
@@ -294,25 +296,34 @@ def tile_list_memory_decoder_evidence_kernel(
             dens[tile] = bank(DEN_BANKS[nt], [P, HALF])
             mix(dens[tile], ex_w, ex_sc, nt, half)
 
-        def divide(tile):
-            half, nt = divmod(tile, N_TILES)
-            den = dens[tile]
-            root = ring.tile([P, HALF], F32, name="root")
-            nc.scalar.activation(root[:], den[:], ACT.Abs_reciprocal_sqrt)
-            inverse = ring.tile([P, HALF], F32, name="inverse")
-            if tile % GPSIMD_EVERY == 0:
-                nc.gpsimd.tensor_tensor(inverse[:], root[:], root[:], ALU.mult)
-            elif tile == VECTOR_TILE:
-                twice = root[:, 0:VECTOR_SHARE].unsqueeze(2).to_broadcast([P, VECTOR_SHARE, 2])
-                nc.vector.tensor_reduce(inverse[:, 0:VECTOR_SHARE], twice, mybir.AxisListType.X, ALU.mult)
-                nc.scalar.activation(inverse[:, VECTOR_SHARE:], root[:, VECTOR_SHARE:], ACT.Square)
+        roots, inverses = {}, {}
+
+        def root_of(tile, pieces):
+            roots[tile] = ring.tile([P, HALF], F32, name="root")
+            inverses[tile] = ring.tile([P, HALF], F32, name="inverse")
+            for j0 in range(0, HALF, HALF // pieces):
+                j1 = j0 + HALF // pieces
+                nc.scalar.activation(roots[tile][:, j0:j1], dens[tile][:, j0:j1], ACT.Abs_reciprocal_sqrt)
+
+        def square(engine, tile, j0, j1):
+            root, inverse = roots[tile][:, j0:j1], inverses[tile][:, j0:j1]
+            if engine == "gpsimd":
+                nc.gpsimd.tensor_tensor(inverse, root, root, ALU.mult)
+            elif engine == "scalar":
+                nc.scalar.activation(inverse, root, ACT.Square)
             else:
-                nc.scalar.activation(inverse[:], root[:], ACT.Square)
+                twice = root.unsqueeze(2).to_broadcast([P, j1 - j0, 2])
+                nc.vector.tensor_reduce(inverse, twice, mybir.AxisListType.X, ALU.mult)
+
+        def divide(tile, pieces):
+            half, nt = divmod(tile, N_TILES)
             num = bank(nt, [P, HALF])
             mix(num, ev_w, ev_sc, nt, half)
             res = ring.tile([P, HALF], F32, name="res")
-            nc.vector.tensor_tensor(res[:], num[:], inverse[:], ALU.mult)
-            nc.sync.dma_start(out[nt * P : (nt + 1) * P, half * HALF : (half + 1) * HALF], res[:])
+            for j0 in range(0, HALF, HALF // pieces):
+                j1 = j0 + HALF // pieces
+                nc.vector.tensor_tensor(res[:, j0:j1], num[:, j0:j1], inverses[tile][:, j0:j1], ALU.mult)
+                nc.sync.dma_start(out[nt * P : (nt + 1) * P, half * HALF + j0 : half * HALF + j1], res[:, j0:j1])
 
         for g in range(SCALAR_GROUPS):
             gather(v_w1[g], tab_w[1], g * GROUP, GROUP)
@@ -355,4 +366,21 @@ def tile_list_memory_decoder_evidence_kernel(
             for tile in reversed(run):
                 exposure(tile)
             for tile in run:
-                divide(tile)
+                root_of(tile, 2 if tile == LAST else 1)
+                if tile == LAST:
+                    square("scalar", LAST, 0, HALF // 2)
+                    square("scalar", LAST, HALF // 2, HALF)
+                    divide(LAST, 2)
+                elif tile == LAST - 1:
+                    square("gpsimd", tile, 0, GPSIMD_LAST_SHARE)
+                    square("scalar", tile, GPSIMD_LAST_SHARE, HALF)
+                    divide(tile, 1)
+                else:
+                    if tile % GPSIMD_EVERY == 0:
+                        square("gpsimd", tile, 0, HALF)
+                    elif tile == VECTOR_TILE:
+                        square("vector", tile, 0, VECTOR_SHARE)
+                        square("scalar", tile, VECTOR_SHARE, HALF)
+                    else:
+                        square("scalar", tile, 0, HALF)
+                    divide(tile, 1)

@@ -24,7 +24,6 @@ ROWS = 4
 BLOCKS = QUADS * ROWS
 PASSES = K // (P * PACK)
 LIST_ROWS = 16
-RUN = 4
 PAIR = 2
 
 STRIP = 128
@@ -219,7 +218,7 @@ def tile_list_memory_decoder_evidence_kernel(
 
         def interleave(engine_copy, dst, src):
             engine_copy(
-                dst.rearrange("p (c i t) -> p c t i", i=RUN, t=PACK), src.rearrange("p t (c i) -> p c t i", i=RUN)
+                dst.rearrange("p (c i t) -> p c t i", i=PAIR, t=PACK), src.rearrange("p t (c i) -> p c t i", i=PAIR)
             )
 
         def last_pass(g, words):
@@ -323,7 +322,7 @@ def tile_list_memory_decoder_evidence_kernel(
             for j0 in range(0, HALF, HALF // pieces):
                 j1 = j0 + HALF // pieces
                 nc.vector.tensor_tensor(res[:, j0:j1], num[:, j0:j1], inverses[tile][:, j0:j1], ALU.mult)
-                nc.sync.dma_start(out[nt * P : (nt + 1) * P, half * HALF + j0 : half * HALF + j1], res[:, j0:j1])
+            nc.sync.dma_start(out[nt * P : (nt + 1) * P, half * HALF : (half + 1) * HALF], res[:])
 
         for g in range(SCALAR_GROUPS):
             gather(v_w1[g], tab_w[1], g * GROUP, GROUP)

@@ -37,6 +37,7 @@ KIB = 1024
 EARLY = T // 8
 
 SCALAR_GROUPS = 2
+GPSIMD_COLUMNS = (176, 144)
 H_BANKS = ((0, 1, 6, 7), (2, 3), (4, 5), (6, 7))
 E_BANKS = ((0, 1, 2, 3), (0, 1), (4, 5), (6, 7))
 DEN_BANKS = (7, 6, 4, 5)
@@ -328,12 +329,13 @@ def tile_list_memory_decoder_evidence_kernel(
             gather(v_w1[g], tab_w[1], g * GROUP, GROUP)
             last_pass(g, v_w1[g])
             bias_planes(g)
+            share = GPSIMD_COLUMNS[g]
             nc.gpsimd.tensor_scalar(
-                h_bf[g][:, 0 : STRIP * PACK].rearrange("p (j t) -> p j t", t=PACK),
-                h_planes[g][:, :, 0:STRIP].rearrange("p t j -> p j t"),
+                h_bf[g][:, 0 : share * PACK].rearrange("p (j t) -> p j t", t=PACK),
+                h_planes[g][:, :, 0:share].rearrange("p t j -> p j t"),
                 1.0, 0.0, ALU.mult, ALU.add,
             )
-            interleave(nc.scalar.copy, h_bf[g][:, STRIP * PACK :], h_planes[g][:, :, STRIP:])
+            interleave(nc.scalar.copy, h_bf[g][:, share * PACK :], h_planes[g][:, :, share:])
         gather(v_w1_rest, tab_w[1], SCALAR_GROUPS * GROUP, S - SCALAR_GROUPS * GROUP)
         for g in range(SCALAR_GROUPS, GROUPS):
             last_pass(g, v_w1_rest[:, (g - SCALAR_GROUPS) * GROUP : (g - SCALAR_GROUPS + 1) * GROUP])

@@ -236,11 +236,9 @@ def tile_list_memory_decoder_evidence_kernel(
 
         def bias_strip(g, u, j0=0, j1=STRIP):
             nc.vector.tensor_tensor(
-                h_bf[g][:, (u * STRIP + j0) * PACK : (u * STRIP + j1) * PACK].rearrange(
-                    "p (c i t) -> p c t i", i=PAIR, t=PACK
-                ),
-                h_acc[g, u][:, :, j0:j1].rearrange("p t (c i) -> p c t i", i=PAIR),
-                bq_sb[:].unsqueeze(1).unsqueeze(3).to_broadcast([P, (j1 - j0) // PAIR, PACK, PAIR]),
+                h_bf[g][:, (u * STRIP + j0) * PACK : (u * STRIP + j1) * PACK].rearrange("p (j t) -> p j t", t=PACK),
+                h_acc[g, u][:, :, j0:j1].rearrange("p t j -> p j t"),
+                bq_sb[:].unsqueeze(1).to_broadcast([P, j1 - j0, PACK]),
                 ALU.add,
             )
 

from contextlib import ExitStack

import concourse.mybir as mybir

K, T, S, H, T2, S2, N = 1024, 4096, 1024, 512, 2048, 512, 512
FLOPS = 2 * (K * H * S + H * S2 * S + 2 * S2 * N * S)

F32 = mybir.dt.float32
BF16 = mybir.dt.bfloat16
I32 = mybir.dt.int32
U32 = mybir.dt.uint32
U16 = mybir.dt.uint16
U8 = mybir.dt.uint8
FP8X4 = mybir.dt.float8_e4m3fn_x4
FP4X4 = mybir.dt.float4_e2m1fn_x4
ACT = mybir.ActivationFunctionType
ALU = mybir.AluOpType

P = 128
PACK = 4
QUADS = 4
QUAD = P // QUADS
ROWS = 4
BLOCKS = QUADS * ROWS
PASSES = K // (P * PACK)
LIST_ROWS = 16
PAIR = 2

STRIP = 128
GROUP = 256
HALF = 512
GROUPS, HALVES = S // GROUP, S // HALF
N_TILES = N // P

KIB = 1024

EARLY = T // 8

SCALAR_GROUPS = 2
GPSIMD_COLUMNS = (176, 144)
H_BANKS = ((0, 1, 6, 7), (2, 3), (4, 5), (6, 7))
E_BANKS = ((0, 1, 2, 3), (0, 1), (4, 5), (6, 7))
DEN_BANKS = (7, 6, 4, 5)
GPSIMD_EVERY = 2

VECTOR_TILE, VECTOR_SHARE = 1, HALF // 2
LAST = HALVES * N_TILES - 1
GPSIMD_LAST_SHARE = 5 * HALF // 8


def tile_list_memory_decoder_evidence_kernel(
    tc, tab_words, tab_scales, tab2_words, tab2_scales, wq_words, wq_scales,
    ex_words, ex_scales, bq, seg, ev, offs, offs2, out,
):
    nc = tc.nc
    with ExitStack() as ctx:
        keep = ctx.enter_context(tc.tile_pool(name="keep", bufs=1))
        shared = ctx.enter_context(tc.tile_pool(name="shared", bufs=1))
        ring = ctx.enter_context(tc.tile_pool(name="ring", bufs=HALVES * N_TILES))
        psum = ctx.enter_context(tc.psum_pool(name="psum", bufs=1))

        def sb(name, shape, dtype):
            return keep.tile(shape, dtype, name=name, align_bytes=64)

        def sb_at(name, shape, dtype, offset):
            return shared.tile(shape, dtype, name=name, offset=offset, align_bytes=64)

        def bank(b, shape):
            return psum.tile(shape, F32, name="bank%d" % b)

        def reorder(dst, src):
            nc.vector.tensor_copy(
                dst.rearrange("p (t m) -> p m t", t=PACK), src.rearrange("p (m t) -> p m t", t=PACK)
            )

        def move_scale_rows(dst, src, row0):
            for i in range(ROWS):
                nc.sync.dma_start(dst[i:P:QUAD].bitcast(I32), src[row0 + i : row0 + BLOCKS : ROWS, :].bitcast(I32))

        def words_of(dram):
            return dram.rearrange("p t i -> p (t i)").bitcast(I32)

        idx = keep.tile([P, S // LIST_ROWS], U16, name="idx")
        idx2 = keep.tile([P, S2 // LIST_ROWS], U16, name="idx2")

        tab_row0 = P - PASSES * BLOCKS
        one_pass_row0 = P - BLOCKS
        tab_sc = sb("tab_sc", [P, T], U8)
        tab2_sc = sb("tab2_sc", [P, T2], U8)
        v_sc = sb("v_sc", [P, PASSES, S], U8)
        wq_sc_rows = sb("wq_sc_rows", [ROWS, PASSES * QUADS * H], U8)
        wq_sc_raw = sb("wq_sc_raw", [P, PASSES * H], U8)
        wq_sc = sb("wq_sc", [P, PASSES * H], U8)
        later_wide = sb_at("later_wide", [P, 8 * KIB], U8, 0)
        later_rows = later_wide[:, 0 : S2 + N]
        later_sc = sb("later_sc", [P, S2 + N], U8)
        nc.vector.memset(tab_sc[0:tab_row0, :].bitcast(I32), 0)
        nc.vector.memset(wq_sc_raw[:].bitcast(I32), 0)
        nc.gpsimd.memset(v_sc[:].rearrange("p a s -> p (a s)").bitcast(I32), 0)
        nc.gpsimd.memset(tab2_sc[0:one_pass_row0, :].bitcast(I32), 0)
        nc.gpsimd.memset(later_sc[:].bitcast(I32), 0)

        wq_at = 16 * KIB
        seg_at = wq_at + 2 * PASSES * H
        wq_raw = sb_at("wq_raw", [P, PASSES, H // 2], I32, wq_at)
        tab_w = [sb("tab_w%d" % a, [P, T], I32) for a in range(PASSES)]
        seg_sb = sb_at("seg_sb", [P, PACK], F32, seg_at)
        bq_sb = sb("bq_sb", [P, PACK], F32)

        nc.scalar.dma_start(tab_sc[tab_row0:P, :].bitcast(I32), tab_scales.rearrange("a q t -> q a t").bitcast(I32))
        nc.scalar.dma_start(wq_raw[:], wq_words.rearrange("a p c -> p a c").bitcast(I32))
        nc.sync.dma_start(idx[:], offs)
        nc.sync.dma_start(
            wq_sc_rows[:].bitcast(I32).rearrange("i (b c) -> i b c", b=PASSES * QUADS),
            wq_scales.rearrange("a (q i) c -> i (a q) c", i=ROWS).bitcast(I32),
        )
        nc.sync.dma_start(idx2[:], offs2)
        nc.sync.dma_start(tab2_sc[one_pass_row0:P, :].bitcast(I32), tab2_scales[0].bitcast(I32))
        nc.sync.dma_start(tab_w[1][:, 0:EARLY], words_of(tab_words[1])[:, 0:EARLY])
        nc.sync.dma_start(tab_w[0][:], words_of(tab_words[0]))
        nc.sync.dma_start(seg_sb[:], seg.rearrange("(p t) -> p t", t=PACK))
        nc.sync.dma_start(bq_sb[:], bq.rearrange("(p t) -> p t", t=PACK))

        v_sc_g = sb("v_sc_g", [P, S], U8)
        nc.vector.tensor_copy(v_sc_g[:], tab_sc[:].indirect(idx[:]))
        for q in (0, 2, 1, 3):
            row0 = tab_row0 + q * PASSES * ROWS
            nc.sync.dma_start(
                v_sc[q * QUAD : q * QUAD + ROWS].bitcast(I32), v_sc_g[row0 : row0 + PASSES * ROWS, :].bitcast(I32)
            )
        nc.sync.dma_start(tab_w[1][:, EARLY:], words_of(tab_words[1])[:, EARLY:])
        nc.sync.dma_start(later_rows[one_pass_row0:P, S2:].bitcast(I32), ex_scales[0].bitcast(I32))

        blocks = wq_sc_rows[:].bitcast(I32).rearrange("i (a q c) -> i a q c", a=PASSES, q=QUADS)
        for q in range(QUADS):
            nc.vector.tensor_copy(
                wq_sc_raw[q * QUAD : q * QUAD + ROWS, :].bitcast(I32).rearrange("i (a c) -> i a c", a=PASSES),
                blocks[:, :, q, :],
            )
        for a in range(PASSES):
            reorder(wq_sc[:, a * H : (a + 1) * H], wq_sc_raw[:, a * H : (a + 1) * H])

        v2_sc_g = sb("v2_sc_g", [P, S2], U8)
        nc.vector.tensor_copy(v2_sc_g[:], tab2_sc[:].indirect(idx2[:]))
        reorder(later_rows[:, 0:S2], v2_sc_g[:])
        v2_sc = later_sc[:, 0:S2]
        ex_sc = later_sc[:, S2:]
        tab2_w = sb("tab2_w", [P, T2], I32)
        ev_sb = sb("ev_sb", [P, PACK, N], F32)
        ex_w = sb("ex_w", [P, N], I32)
        nc.sync.dma_start(tab2_w[:], words_of(tab2_words[0]))
        move_scale_rows(later_sc, later_rows, one_pass_row0)
        nc.sync.dma_start(ev_sb[:], ev.rearrange("(p t) n -> p t n", t=PACK))
        nc.sync.dma_start(ex_w[:], words_of(ex_words[0]))

        ln_seg = sb("ln_seg", [P, PACK], F32)
        nc.scalar.activation(ln_seg[:], seg_sb[:], ACT.Ln)
        warm_in = sb("warm_in", [P, 1], F32)
        nc.gpsimd.memset(warm_in[:], 0.0)
        warm = sb_at("warm", [P, 1], F32, seg_at)
        nc.scalar.activation(warm[:], warm_in[:], ACT.Exp)

        def gather(words, window, j0, width):
            nc.vector.tensor_copy(
                words[:].bitcast(U32),
                window[:].bitcast(U32).indirect(idx[:, j0 // LIST_ROWS : (j0 + width) // LIST_ROWS]),
            )

        v_w0 = [sb_at("v_w0_0", [P, GROUP], I32, wq_at)]
        v_w0 = v_w0 + [sb("v_w0_%d" % g, [P, GROUP], I32) for g in range(1, GROUPS)]
        wq_w = sb("wq_w", [P, PASSES * H // 2], I32)
        nc.vector.tensor_copy(
            wq_w[:].bitcast(U16).rearrange("p (a t m) -> p a m t", a=PASSES, t=PACK),
            wq_raw[:].bitcast(U16).rearrange("p a (m t) -> p a m t", t=PACK),
        )

        h_acc = {}

        def h_pass(g, a, words):
            banks = H_BANKS[g]
            steps = PACK // len(banks) if g < SCALAR_GROUPS else PACK
            order = list(enumerate(banks))
            for u, b in reversed(order) if 0 < g < SCALAR_GROUPS else order:
                if a == 0:
                    h_acc[g, u] = bank(b, [P, steps, GROUP if g < SCALAR_GROUPS else STRIP])
                for step in range(steps):
                    t, j0, width = (steps * u + step, 0, GROUP) if g < SCALAR_GROUPS else (step, u * STRIP, STRIP)
                    col = a * H + t * P
                    nc.tensor.matmul_mx(
                        out=h_acc[g, u][:, step, :],
                        lhsT=wq_w[:].bitcast(U8)[:, 2 * col : 2 * (col + P)].bitcast(FP4X4),
                        lhsT_scale=wq_sc[:, col : col + P],
                        rhs=words[:, j0 : j0 + width].bitcast(FP8X4),
                        rhs_scale=v_sc[:, a, g * GROUP + j0 : g * GROUP + j0 + width],
                        start=(a == 0 and step == 0),
                        stop=(a == PASSES - 1 and step == steps - 1),
                    )

        for g in range(GROUPS):
            gather(v_w0[g], tab_w[0], g * GROUP, GROUP)
            if g < GROUPS - 1:
                h_pass(g, 0, v_w0[g])

        v_w1 = [sb("v_w1_%d" % g, [P, GROUP], I32) for g in range(SCALAR_GROUPS)]
        v_w1_rest = sb("v_w1_rest", [P, S - SCALAR_GROUPS * GROUP], I32)
        h_bf = [sb("h_bf%d" % g, [P, GROUP * PACK], BF16) for g in range(SCALAR_GROUPS)]
        h_bf = h_bf + [sb_at("h_bf%d" % g, [P, GROUP * PACK], BF16, 2 * g * KIB) for g in range(SCALAR_GROUPS, GROUPS)]
        h_w = [sb_at("h_w%d" % g, [P, GROUP], I32, g * KIB) for g in range(GROUPS)]
        h_sc = [sb("h_sc%d" % g, [P, GROUP], U8) for g in range(GROUPS)]
        h_planes = [sb("h_planes%d" % g, [P, PACK, GROUP], BF16) for g in range(SCALAR_GROUPS)]
        act_planes = [sb("act_planes%d" % g, [P, PACK, GROUP], BF16) for g in range(GROUPS)]
        act_bf = [sb("act_bf%d" % half, [P, HALF * PACK], BF16) for half in range(HALVES)]
        act_w = sb("act_w", [P, S], I32)
        act_sc = sb("act_sc", [P, S], U8)
        v2_w = sb("v2_w", [P, S2], I32)
        ev_bf = sb_at("ev_bf", [P, N * PACK], BF16, 2 * (GROUPS - 1) * KIB)
        ev_w = sb("ev_w", [P, N], I32)
        ev_sc = sb("ev_sc", [P, N], U8)

        def interleave(engine_copy, dst, src):
            engine_copy(
                dst.rearrange("p (c i t) -> p c t i", i=PAIR, t=PACK), src.rearrange("p t (c i) -> p c t i", i=PAIR)
            )

        def last_pass(g, words):
            if g == GROUPS - 1:
                h_pass(g, 0, v_w0[g])
            h_pass(g, PASSES - 1, words)

        def bias_planes(g):
            planes = PACK // len(H_BANKS[g])
            for t in range(PACK):
                nc.scalar.activation(
                    h_planes[g][:, t, :], h_acc[g, t // planes][:, t % planes, :], ACT.Identity, bias=bq_sb[:, t : t + 1]
                )

        def bias_strip(g, u, j0=0, j1=STRIP):
            nc.vector.tensor_tensor(
                h_bf[g][:, (u * STRIP + j0) * PACK : (u * STRIP + j1) * PACK].rearrange("p (j t) -> p j t", t=PACK),
                h_acc[g, u][:, :, j0:j1].rearrange("p t j -> p j t"),
                bq_sb[:].unsqueeze(1).to_broadcast([P, j1 - j0, PACK]),
                ALU.add,
            )

        def scores(g):
            nc.vector.quantize_mx(out=h_w[g][:].bitcast(FP8X4), scales=h_sc[g][:], in_=h_bf[g][:])
            planes = PACK // len(E_BANKS[g])
            e_acc = {}
            order = list(enumerate(E_BANKS[g]))
            for u, b in reversed(order) if g >= SCALAR_GROUPS else order:
                e_acc[u] = bank(b, [P, planes, GROUP])
                for s in range(planes):
                    t = planes * u + s
                    nc.tensor.matmul_mx(
                        out=e_acc[u][:, s, :],
                        lhsT=v2_w[:, t * P : (t + 1) * P].bitcast(FP8X4),
                        lhsT_scale=v2_sc[:, t * P : (t + 1) * P],
                        rhs=h_w[g][:].bitcast(FP8X4),
                        rhs_scale=h_sc[g][:],
                        start=True,
                        stop=True,
                    )
            for t in range(PACK):
                nc.scalar.activation(
                    act_planes[g][:, t, :], e_acc[t // planes][:, t % planes, :], ACT.Exp, bias=ln_seg[:, t : t + 1]
                )

        def interleave_act(g, j0=0, j1=GROUP):
            half, u = divmod(g, 2)
            dst = act_bf[half][:, (u * GROUP + j0) * PACK : (u * GROUP + j1) * PACK]
            interleave(nc.vector.tensor_copy, dst, act_planes[g][:, :, j0:j1])

        def quantize_act(half, j0=0, j1=HALF):
            cols = slice(half * HALF + j0, half * HALF + j1)
            nc.vector.quantize_mx(
                out=act_w[:, cols].bitcast(FP8X4), scales=act_sc[:, cols], in_=act_bf[half][:, j0 * PACK : j1 * PACK]
            )

        def mix(acc, words, scales, nt, half):
            nc.tensor.matmul_mx(
                out=acc[:],
                lhsT=words[:, nt * P : (nt + 1) * P].bitcast(FP8X4),
                lhsT_scale=scales[:, nt * P : (nt + 1) * P],
                rhs=act_w[:, half * HALF : (half + 1) * HALF].bitcast(FP8X4),
                rhs_scale=act_sc[:, half * HALF : (half + 1) * HALF],
                start=True,
                stop=True,
            )

        dens = {}

        def exposure(tile):
            half, nt = divmod(tile, N_TILES)
            dens[tile] = bank(DEN_BANKS[nt], [P, HALF])
            mix(dens[tile], ex_w, ex_sc, nt, half)

        roots, inverses = {}, {}

        def root_of(tile, pieces):
            roots[tile] = ring.tile([P, HALF], F32, name="root")
            inverses[tile] = ring.tile([P, HALF], F32, name="inverse")
            for j0 in range(0, HALF, HALF // pieces):
                j1 = j0 + HALF // pieces
                nc.scalar.activation(roots[tile][:, j0:j1], dens[tile][:, j0:j1], ACT.Abs_reciprocal_sqrt)

        def square(engine, tile, j0, j1):
            root, inverse = roots[tile][:, j0:j1], inverses[tile][:, j0:j1]
            if engine == "gpsimd":
                nc.gpsimd.tensor_tensor(inverse, root, root, ALU.mult)
            elif engine == "scalar":
                nc.scalar.activation(inverse, root, ACT.Square)
            else:
                twice = root.unsqueeze(2).to_broadcast([P, j1 - j0, 2])
                nc.vector.tensor_reduce(inverse, twice, mybir.AxisListType.X, ALU.mult)

        def divide(tile, pieces):
            half, nt = divmod(tile, N_TILES)
            num = bank(nt, [P, HALF])
            mix(num, ev_w, ev_sc, nt, half)
            res = ring.tile([P, HALF], F32, name="res")
            for j0 in range(0, HALF, HALF // pieces):
                j1 = j0 + HALF // pieces
                nc.vector.tensor_tensor(res[:, j0:j1], num[:, j0:j1], inverses[tile][:, j0:j1], ALU.mult)
            nc.sync.dma_start(out[nt * P : (nt + 1) * P, half * HALF : (half + 1) * HALF], res[:])

        for g in range(SCALAR_GROUPS):
            gather(v_w1[g], tab_w[1], g * GROUP, GROUP)
            last_pass(g, v_w1[g])
            bias_planes(g)
            share = GPSIMD_COLUMNS[g]
            nc.gpsimd.tensor_scalar(
                h_bf[g][:, 0 : share * PACK].rearrange("p (j t) -> p j t", t=PACK),
                h_planes[g][:, :, 0:share].rearrange("p t j -> p j t"),
                1.0, 0.0, ALU.mult, ALU.add,
            )
            interleave(nc.scalar.copy, h_bf[g][:, share * PACK :], h_planes[g][:, :, share:])
        gather(v_w1_rest, tab_w[1], SCALAR_GROUPS * GROUP, S - SCALAR_GROUPS * GROUP)
        for g in range(SCALAR_GROUPS, GROUPS):
            last_pass(g, v_w1_rest[:, (g - SCALAR_GROUPS) * GROUP : (g - SCALAR_GROUPS + 1) * GROUP])
        nc.vector.tensor_copy(
            v2_w[:].bitcast(U32).rearrange("p (t m) -> p m t", t=PACK), tab2_w[:].bitcast(U32).indirect(idx2[:])
        )
        scores(0)
        bias_strip(2, 0)
        bias_strip(2, 1, 0, STRIP // 2)
        scores(1)
        bias_strip(2, 1, STRIP // 2, STRIP)
        bias_strip(3, 0)
        scores(2)
        bias_strip(3, 1)
        interleave_act(0, 0, STRIP)
        scores(3)
        interleave_act(0, STRIP, GROUP)
        interleave_act(1)
        quantize_act(0, 0, GROUP)
        quantize_act(0, GROUP, HALF)
        interleave(nc.vector.tensor_copy, ev_bf[:, 0 : PACK * GROUP], ev_sb[:, :, 0:GROUP])
        interleave(nc.vector.tensor_copy, ev_bf[:, PACK * GROUP :], ev_sb[:, :, GROUP:])
        interleave_act(2)
        nc.vector.quantize_mx(out=ev_w[:].bitcast(FP8X4), scales=ev_sc[:], in_=ev_bf[:])
        interleave_act(3)
        quantize_act(1, 0, GROUP)
        quantize_act(1, GROUP, HALF)
        for run in (range(0, N_TILES), range(N_TILES, 2 * N_TILES - 1), range(2 * N_TILES - 1, 2 * N_TILES)):
            for tile in reversed(run):
                exposure(tile)
            for tile in run:
                root_of(tile, 2 if tile == LAST else 1)
                if tile == LAST:
                    square("scalar", LAST, 0, HALF // 2)
                    square("scalar", LAST, HALF // 2, HALF)
                    divide(LAST, 2)
                elif tile == LAST - 1:
                    square("gpsimd", tile, 0, GPSIMD_LAST_SHARE)
                    square("scalar", tile, GPSIMD_LAST_SHARE, HALF)
                    divide(tile, 1)
                else:
                    if tile % GPSIMD_EVERY == 0:
                        square("gpsimd", tile, 0, HALF)
                    elif tile == VECTOR_TILE:
                        square("vector", tile, 0, VECTOR_SHARE)
                        square("scalar", tile, VECTOR_SHARE, HALF)
                    else:
                        square("scalar", tile, 0, HALF)
                    divide(tile, 1)
